import numpy as np
import ml_dtypes


def mxq(x, axis, fmt="e4m3"):
    dtype, down = {"e4m3": (ml_dtypes.float8_e4m3fn, 7), "e5m2": (ml_dtypes.float8_e5m2, 14)}[fmt]
    v = np.moveaxis(np.asarray(x, np.float32).astype(ml_dtypes.bfloat16).astype(np.float64), axis, -1)
    blocks = v.reshape(v.shape[:-1] + (-1, 32))
    amax = np.abs(blocks).max(-1, keepdims=True)
    byte = np.maximum(np.where(amax > 0, np.frexp(amax)[1] - 1 + 127, 0) - down, 1)
    scale = np.exp2(byte - 127.0)
    codes = (blocks / scale).astype(np.float32).astype(dtype).astype(np.float64)
    return np.moveaxis((codes * scale).reshape(v.shape), -1, axis)


WIDE = False


def mx_kscale(k):
    if not WIDE:
        return np.ones(k)
    levels = np.array([18, -18])
    if k % 512:
        return np.exp2(np.random.permutation(np.resize(levels, k // 32))).repeat(32)
    a = np.empty((k // 512, 16))
    for p in range(k // 512):
        a[p, :8] = np.random.permutation(np.resize(levels, 8))
        for g in range(8):
            far = levels[np.abs(levels - a[p, g]) >= 10]
            a[p, g + 8] = far[np.random.randint(len(far))]
    return np.exp2(a.ravel()).repeat(32)


def f64(x):
    return np.asarray(x).astype(np.float64)


def striped(idx):
    return np.tile(np.asarray(idx).reshape(-1, 16).T, (8, 1)).astype(np.uint16)


def unstriped(offs):
    return offs[:16].T.reshape(-1).astype(np.int64)


N, T, D, V = 512, 2048, 512, 512


def setup_inputs():
    n = np.random.standard_normal
    idx = np.random.permutation(T)[:N]
    s = mx_kscale(D)[:, None]
    z = mx_kscale(V)[:, None]
    w = n((D, V)) / np.sqrt(D)
    return {
        "xT": (n((D, T)) / s).astype(np.float32),
        "wd": (w * s).astype(np.float32),
        "wv": (w.T / z).astype(np.float32),
        "y": n((V, N)).astype(np.float32),
        "cw": (np.random.uniform(0.5, 1.5, (V, 1)) / np.sqrt(V) * z).astype(np.float32),
        "rw": np.tile(np.random.uniform(0.5, 1.5, N), (128, 1)).astype(np.float32),
        "offs": striped(idx),
    }


def reference(xT, wd, wv, y, cw, rw, offs):
    idx = unstriped(offs)
    a = mxq(f64(wd), 0, "e4m3").T @ mxq(f64(xT)[:, idx], 0, "e4m3")
    q = a - f64(y)
    g = f64(cw) * f64(rw)[:1] * q / (1.0 + q * q)
    dx = mxq(f64(wv), 0, "e4m3").T @ mxq(g, 0, "e5m2")
    gx = np.zeros((D, T))
    gx[:, idx] = dx
    return gx

@@ -1,0 +1,197 @@
+from contextlib import ExitStack
+
+import concourse.mybir as mybir
+
+N, T, D, V = 512, 2048, 512, 512
+FLOPS = 2 * 2 * N * D * V
+
+F32 = mybir.dt.float32
+BF16 = mybir.dt.bfloat16
+U32 = mybir.dt.uint32
+U16 = mybir.dt.uint16
+U8 = mybir.dt.uint8
+E4M3 = mybir.dt.float8_e4m3fn_x4
+E5M2 = mybir.dt.float8_e5m2_x4
+ALU = mybir.AluOpType
+ACT = mybir.ActivationFunctionType
+
+P = 128
+PACK = 4
+HALF = N // 2
+CHUNK = 128
+CHUNKS = N // CHUNK
+BLOCKS = D // P
+
+
+def tile_attend_gml_cau_kernel(tc, xT, wd, wv, y, cw, rw, offs, out):
+    nc = tc.nc
+    with ExitStack() as ctx:
+        sb = ctx.enter_context(tc.tile_pool(name="sb", bufs=1))
+        ps = ctx.enter_context(tc.psum_pool(name="ps", bufs=1))
+
+        def tiles(name, count, shape, dtype):
+            return [sb.tile(shape, dtype, name="%s%d" % (name, i), align_bytes=64) for i in range(count)]
+
+        def banks(name, count, shape):
+            return [ps.tile(shape, F32, name="%s%d" % (name, i)) for i in range(count)]
+
+        offsets = sb.tile([P, N // 16], U16, name="offsets")
+        cw_sb = sb.tile([P, PACK], F32, name="cw_sb")
+        rw_sb = sb.tile([P, N], F32, name="rw_sb")
+        wd_raw = sb.tile([P, PACK, V], F32, name="wd_raw")
+        wv_raw = sb.tile([P, PACK, D], F32, name="wv_raw")
+        x_plane = tiles("x_plane", PACK, [P, T], F32)
+        y_half = tiles("y_half", 2, [P, PACK, HALF], F32)
+
+        nc.sync.dma_start(offsets[:], offs)
+        nc.sync.dma_start(cw_sb[:], cw.rearrange("(p t) o -> p (t o)", t=PACK))
+        nc.sync.dma_start(rw_sb[:], rw)
+        nc.sync.dma_start(wd_raw[:], wd.rearrange("(p j) v -> p j v", j=PACK))
+        x_rows = xT.rearrange("(p j) c -> p j c", j=PACK)
+        for j in range(PACK):
+            nc.sync.dma_start(x_plane[j][:], x_rows[:, j, :])
+        y_rows = y.rearrange("(p t) i -> p t i", t=PACK)
+        for h in range(2):
+            nc.sync.dma_start(y_half[h][:], y_rows[:, :, h * HALF : (h + 1) * HALF])
+        nc.sync.dma_start(wv_raw[:], wv.rearrange("(p j) d -> p j d", j=PACK))
+
+        warm = sb.tile([P, 1], F32, name="warm")
+        warm_out = sb.tile([P, 1], F32, name="warm_out")
+        nc.vector.memset(warm[:], 0.0)
+        nc.scalar.activation(warm_out[:], warm[:], ACT.Abs_reciprocal_sqrt, bias=1.0)
+
+        window = tiles("window", BLOCKS, [P, T], F32)
+        for b in range(BLOCKS):
+            nc.vector.memset(window[b][:].bitcast(mybir.dt.int32), 0)
+
+        weight = tiles("weight", CHUNKS, [P, CHUNK, PACK], F32)
+        for c in range(CHUNKS):
+            nc.vector.tensor_tensor(
+                weight[c][:],
+                rw_sb[:, c * CHUNK : (c + 1) * CHUNK].unsqueeze(2).to_broadcast([P, CHUNK, PACK]),
+                cw_sb[:].unsqueeze(1).to_broadcast([P, CHUNK, PACK]),
+                ALU.mult,
+            )
+
+        wd_bf = sb.tile([P, PACK, P, PACK], BF16, name="wd_bf", align_bytes=64)
+        nc.scalar.copy(wd_bf[:].rearrange("p t m j -> p m t j"), wd_raw[:].rearrange("p j (m t) -> p m t j", t=PACK))
+        wd_codes = sb.tile([P, V], U32, name="wd_codes", align_bytes=64)
+        wd_scales = sb.tile([P, V], U8, name="wd_scales", align_bytes=64)
+
+        x_bf = tiles("x_bf", 2, [P, HALF, PACK], BF16)
+        x_codes = tiles("x_codes", 2, [P, HALF], U32)
+        x_scales = tiles("x_scales", 2, [P, HALF], U8)
+
+        def gather(j, h):
+            cols = HALF // 16
+            nc.vector.tensor_copy(x_bf[h][:, :, j], x_plane[j][:].indirect(offsets[:, h * cols : (h + 1) * cols]))
+
+        def quantize_x(h):
+            nc.vector.quantize_mx(
+                out=x_codes[h][:].bitcast(E4M3), scales=x_scales[h][:], in_=x_bf[h][:].rearrange("p i j -> p (i j)")
+            )
+
+        for j in range(PACK - 1):
+            gather(j, 0)
+            gather(j, 1)
+            if j == 0:
+                nc.vector.quantize_mx(
+                    out=wd_codes[:].bitcast(E4M3), scales=wd_scales[:], in_=wd_bf[:].rearrange("p t m j -> p (t m j)")
+                )
+
+        a_bank = banks("a_bank", CHUNKS, [P, PACK, CHUNK])
+        q = tiles("q", CHUNKS, [P, CHUNK, PACK], F32)
+        u = tiles("u", CHUNKS, [P, CHUNK, PACK], F32)
+        r = tiles("r", CHUNKS, [P, CHUNK, PACK], F32)
+        inv = tiles("inv", CHUNKS, [P, CHUNK, PACK], F32)
+        num = tiles("num", CHUNKS, [P, CHUNK, PACK], F32)
+        g_bf = tiles("g_bf", CHUNKS, [P, CHUNK, PACK], BF16)
+        g_codes = sb.tile([P, N], U32, name="g_codes", align_bytes=64)
+        g_scales = sb.tile([P, N], U8, name="g_scales", align_bytes=64)
+
+        def first_product(c):
+            h, cols = c // 2, slice((c % 2) * CHUNK, (c % 2 + 1) * CHUNK)
+            for t in range(PACK):
+                m = slice(t * P, (t + 1) * P)
+                nc.tensor.matmul_mx(
+                    out=a_bank[c][:, t, :],
+                    lhsT=wd_codes[:, m].bitcast(E4M3),
+                    lhsT_scale=wd_scales[:, m],
+                    rhs=x_codes[h][:, cols].bitcast(E4M3),
+                    rhs_scale=x_scales[h][:, cols],
+                    start=True,
+                    stop=True,
+                )
+
+        def residual(c):
+            h, cols = c // 2, slice((c % 2) * CHUNK, (c % 2 + 1) * CHUNK)
+            nc.vector.tensor_tensor(
+                q[c][:],
+                a_bank[c][:].rearrange("p t i -> p i t"),
+                y_half[h][:, :, cols].rearrange("p t i -> p i t"),
+                ALU.subtract,
+            )
+            nc.scalar.activation(u[c][:], q[c][:], ACT.Square)
+            nc.scalar.activation(r[c][:], u[c][:], ACT.Abs_reciprocal_sqrt, bias=1.0)
+            nc.scalar.activation(inv[c][:], r[c][:], ACT.Square)
+
+        def numerator(c):
+            nc.vector.tensor_tensor(num[c][:], q[c][:], weight[c][:], ALU.mult)
+
+        def gradient(c):
+            nc.vector.tensor_tensor(g_bf[c][:], num[c][:], inv[c][:], ALU.mult)
+
+        def quantize_g(c):
+            cols = slice(c * CHUNK, (c + 1) * CHUNK)
+            nc.vector.quantize_mx(
+                out=g_codes[:, cols].bitcast(E5M2), scales=g_scales[:, cols], in_=g_bf[c][:].rearrange("p i t -> p (i t)")
+            )
+
+        gather(PACK - 1, 0)
+        quantize_x(0)
+        gather(PACK - 1, 1)
+        first_product(0)
+        first_product(1)
+        residual(0)
+        quantize_x(1)
+        first_product(2)
+        first_product(3)
+        residual(1)
+        numerator(0)
+        residual(2)
+        numerator(1)
+        gradient(0)
+        residual(3)
+        quantize_g(0)
+        numerator(2)
+        gradient(1)
+        numerator(3)
+        quantize_g(1)
+        gradient(2)
+        quantize_g(2)
+        gradient(3)
+        quantize_g(3)
+
+        wv_bf = tiles("wv_bf", BLOCKS, [P, P, PACK], BF16)
+        wv_codes = tiles("wv_codes", BLOCKS, [P, P], U32)
+        wv_scales = tiles("wv_scales", BLOCKS, [P, P], U8)
+        dx_bank = banks("dx_bank", BLOCKS, [P, N])
+        dx = tiles("dx", BLOCKS, [P, N], F32)
+        for b in range(BLOCKS):
+            nc.scalar.copy(wv_bf[b][:], wv_raw[:, :, b * P : (b + 1) * P].rearrange("p j d -> p d j"))
+            nc.vector.quantize_mx(
+                out=wv_codes[b][:].bitcast(E4M3), scales=wv_scales[b][:], in_=wv_bf[b][:].rearrange("p d j -> p (d j)")
+            )
+        for b in range(BLOCKS):
+            nc.tensor.matmul_mx(
+                out=dx_bank[b][:],
+                lhsT=wv_codes[b][:].bitcast(E4M3),
+                lhsT_scale=wv_scales[b][:],
+                rhs=g_codes[:].bitcast(E5M2),
+                rhs_scale=g_scales[:],
+                start=True,
+                stop=True,
+            )
+            nc.scalar.copy(dx[b][:], dx_bank[b][:])
+            nc.vector.tensor_copy(window[b][:].indirect(offsets[:]), dx[b][:])
+            nc.sync.dma_start(out[b * P : (b + 1) * P, :], window[b][:])

@@ -32,9 +32,6 @@ def tile_attend_gml_cau_kernel(tc, xT, wd, wv, y, cw, rw, offs, out):
         def tiles(name, count, shape, dtype):
             return [sb.tile(shape, dtype, name="%s%d" % (name, i), align_bytes=64) for i in range(count)]
 
-        def banks(name, count, shape):
-            return [ps.tile(shape, F32, name="%s%d" % (name, i)) for i in range(count)]
-
         offsets = sb.tile([P, N // 16], U16, name="offsets")
         cw_sb = sb.tile([P, PACK], F32, name="cw_sb")
         rw_sb = sb.tile([P, N], F32, name="rw_sb")
@@ -61,8 +58,9 @@ def tile_attend_gml_cau_kernel(tc, xT, wd, wv, y, cw, rw, offs, out):
         nc.scalar.activation(warm_out[:], warm[:], ACT.Abs_reciprocal_sqrt, bias=1.0)
 
         window = tiles("window", BLOCKS, [P, T], F32)
-        for b in range(BLOCKS):
-            nc.vector.memset(window[b][:].bitcast(mybir.dt.int32), 0)
+        for b in range(BLOCKS - 1):
+            nc.vector.memset(window[b][:], 0.0)
+        nc.gpsimd.memset(window[BLOCKS - 1][:], 0.0)
 
         weight = tiles("weight", CHUNKS, [P, CHUNK, PACK], F32)
         for c in range(CHUNKS):
@@ -99,15 +97,20 @@ def tile_attend_gml_cau_kernel(tc, xT, wd, wv, y, cw, rw, offs, out):
                     out=wd_codes[:].bitcast(E4M3), scales=wd_scales[:], in_=wd_bf[:].rearrange("p t m j -> p (t m j)")
                 )
 
-        a_bank = banks("a_bank", CHUNKS, [P, PACK, CHUNK])
+        a_bank = [ps.tile([P, PACK, CHUNK], F32, name="a_bank%d" % c, tag="bank%d" % c) for c in range(CHUNKS)]
         q = tiles("q", CHUNKS, [P, CHUNK, PACK], F32)
         u = tiles("u", CHUNKS, [P, CHUNK, PACK], F32)
         r = tiles("r", CHUNKS, [P, CHUNK, PACK], F32)
         inv = tiles("inv", CHUNKS, [P, CHUNK, PACK], F32)
         num = tiles("num", CHUNKS, [P, CHUNK, PACK], F32)
-        g_bf = tiles("g_bf", CHUNKS, [P, CHUNK, PACK], BF16)
-        g_codes = sb.tile([P, N], U32, name="g_codes", align_bytes=64)
-        g_scales = sb.tile([P, N], U8, name="g_scales", align_bytes=64)
+        g_bf = tiles("g_bf", 2, [P, HALF, PACK], BF16)
+        g_codes = sb.tile([P, HALF + N], U32, name="g_codes", align_bytes=64)
+        g_scales = sb.tile([P, HALF + N], U8, name="g_scales", align_bytes=64)
+        nc.gpsimd.memset(g_codes[:, :HALF], 0)
+        nc.gpsimd.memset(g_scales[:, :HALF], 0)
+        wv_bf = tiles("wv_bf", 2, [P, 2 * P, PACK], BF16)
+        wv_codes = tiles("wv_codes", 2, [P, 2 * P], U32)
+        wv_scales = tiles("wv_scales", 2, [P, 2 * P], U8)
 
         def first_product(c):
             h, cols = c // 2, slice((c % 2) * CHUNK, (c % 2 + 1) * CHUNK)
@@ -131,6 +134,8 @@ def tile_attend_gml_cau_kernel(tc, xT, wd, wv, y, cw, rw, offs, out):
                 y_half[h][:, :, cols].rearrange("p t i -> p i t"),
                 ALU.subtract,
             )
+
+        def inverse(c):
             nc.scalar.activation(u[c][:], q[c][:], ACT.Square)
             nc.scalar.activation(r[c][:], u[c][:], ACT.Abs_reciprocal_sqrt, bias=1.0)
             nc.scalar.activation(inv[c][:], r[c][:], ACT.Square)
@@ -139,13 +144,47 @@ def tile_attend_gml_cau_kernel(tc, xT, wd, wv, y, cw, rw, offs, out):
             nc.vector.tensor_tensor(num[c][:], q[c][:], weight[c][:], ALU.mult)
 
         def gradient(c):
-            nc.vector.tensor_tensor(g_bf[c][:], num[c][:], inv[c][:], ALU.mult)
+            cols = slice((c % 2) * CHUNK, (c % 2 + 1) * CHUNK)
+            nc.vector.tensor_tensor(g_bf[c // 2][:, cols, :], num[c][:], inv[c][:], ALU.mult)
 
-        def quantize_g(c):
-            cols = slice(c * CHUNK, (c + 1) * CHUNK)
+        def quantize_g(h):
+            cols = slice((h + 1) * HALF, (h + 2) * HALF)
             nc.vector.quantize_mx(
-                out=g_codes[:, cols].bitcast(E5M2), scales=g_scales[:, cols], in_=g_bf[c][:].rearrange("p i t -> p (i t)")
+                out=g_codes[:, cols].bitcast(E5M2), scales=g_scales[:, cols], in_=g_bf[h][:].rearrange("p i t -> p (i t)")
             )
+
+        def interleave_wv(b):
+            cols = slice((b % 2) * P, (b % 2 + 1) * P)
+            nc.scalar.copy(wv_bf[b // 2][:, cols, :], wv_raw[:, :, b * P : (b + 1) * P].rearrange("p j d -> p d j"))
+
+        def quantize_wv(k):
+            nc.vector.quantize_mx(
+                out=wv_codes[k][:].bitcast(E4M3), scales=wv_scales[k][:], in_=wv_bf[k][:].rearrange("p d j -> p (d j)")
+            )
+
+        def second_product(b, first_col, keep, tag):
+            bank = ps.tile([P, N], F32, name="dx_" + tag, tag=tag)
+            m = slice((b % 2) * P, (b % 2 + 1) * P)
+            cols = slice(first_col, first_col + N)
+            nc.tensor.matmul_mx(
+                out=bank[:],
+                lhsT=wv_codes[b // 2][:, m].bitcast(E4M3),
+                lhsT_scale=wv_scales[b // 2][:, m],
+                rhs=g_codes[:, cols].bitcast(E5M2),
+                rhs_scale=g_scales[:, cols],
+                start=True,
+                stop=True,
+            )
+            dx = sb.tile([P, keep], F32, name="dx_sb_" + tag)
+            nc.scalar.copy(dx[:], bank[:, N - keep :])
+            return dx
+
+        def scatter(b, first, dx):
+            count = dx.shape[1]
+            nc.vector.tensor_copy(window[b][:].indirect(offsets[:, first // 16 : (first + count) // 16]), dx[:])
+
+        def store(b):
+            nc.sync.dma_start(out[b * P : (b + 1) * P, :], window[b][:])
 
         gather(PACK - 1, 0)
         quantize_x(0)
@@ -153,45 +192,40 @@ def tile_attend_gml_cau_kernel(tc, xT, wd, wv, y, cw, rw, offs, out):
         first_product(0)
         first_product(1)
         residual(0)
+        inverse(0)
         quantize_x(1)
         first_product(2)
         first_product(3)
         residual(1)
+        inverse(1)
         numerator(0)
         residual(2)
         numerator(1)
-        gradient(0)
         residual(3)
-        quantize_g(0)
-        numerator(2)
+        interleave_wv(0)
+        interleave_wv(1)
+        gradient(0)
         gradient(1)
+        numerator(2)
+        quantize_g(0)
+        quantize_wv(0)
+        inverse(2)
         numerator(3)
-        quantize_g(1)
+        early = [second_product(b, 0, HALF, "bank%d" % b) for b in range(2)]
+        inverse(3)
         gradient(2)
-        quantize_g(2)
+        scatter(0, 0, early[0])
         gradient(3)
-        quantize_g(3)
-
-        wv_bf = tiles("wv_bf", BLOCKS, [P, P, PACK], BF16)
-        wv_codes = tiles("wv_codes", BLOCKS, [P, P], U32)
-        wv_scales = tiles("wv_scales", BLOCKS, [P, P], U8)
-        dx_bank = banks("dx_bank", BLOCKS, [P, N])
-        dx = tiles("dx", BLOCKS, [P, N], F32)
-        for b in range(BLOCKS):
-            nc.scalar.copy(wv_bf[b][:], wv_raw[:, :, b * P : (b + 1) * P].rearrange("p j d -> p d j"))
-            nc.vector.quantize_mx(
-                out=wv_codes[b][:].bitcast(E4M3), scales=wv_scales[b][:], in_=wv_bf[b][:].rearrange("p d j -> p (d j)")
-            )
-        for b in range(BLOCKS):
-            nc.tensor.matmul_mx(
-                out=dx_bank[b][:],
-                lhsT=wv_codes[b][:].bitcast(E4M3),
-                lhsT_scale=wv_scales[b][:],
-                rhs=g_codes[:].bitcast(E5M2),
-                rhs_scale=g_scales[:],
-                start=True,
-                stop=True,
-            )
-            nc.scalar.copy(dx[b][:], dx_bank[b][:])
-            nc.vector.tensor_copy(window[b][:].indirect(offsets[:]), dx[b][:])
-            nc.sync.dma_start(out[b * P : (b + 1) * P, :], window[b][:])
+        quantize_g(1)
+        scatter(1, 0, early[1])
+        late = [second_product(b, HALF, HALF, "bank%d" % (4 + b)) for b in range(2)]
+        interleave_wv(2)
+        interleave_wv(3)
+        scatter(0, HALF, late[0])
+        store(0)
+        quantize_wv(1)
+        scatter(1, HALF, late[1])
+        store(1)
+        for b in range(2, BLOCKS):
+            scatter(b, 0, second_product(b, HALF, N, "bank%d" % (4 + b)))
+            store(b)

@@ -36,7 +36,7 @@ def tile_attend_gml_cau_kernel(tc, xT, wd, wv, y, cw, rw, offs, out):
         cw_sb = sb.tile([P, PACK], F32, name="cw_sb")
         rw_sb = sb.tile([P, N], F32, name="rw_sb")
         wd_raw = sb.tile([P, PACK, V], F32, name="wd_raw")
-        wv_raw = sb.tile([P, PACK, D], F32, name="wv_raw")
+        wv_raw = tiles("wv_raw", 2, [P, PACK, D // 2], F32)
         x_plane = tiles("x_plane", PACK, [P, T], F32)
         y_half = tiles("y_half", 2, [P, PACK, HALF], F32)
 
@@ -47,20 +47,25 @@ def tile_attend_gml_cau_kernel(tc, xT, wd, wv, y, cw, rw, offs, out):
         x_rows = xT.rearrange("(p j) c -> p j c", j=PACK)
         for j in range(PACK):
             nc.sync.dma_start(x_plane[j][:], x_rows[:, j, :])
+        wv_rows = wv.rearrange("(p j) d -> p j d", j=PACK)
         y_rows = y.rearrange("(p t) i -> p t i", t=PACK)
         for h in range(2):
             nc.sync.dma_start(y_half[h][:], y_rows[:, :, h * HALF : (h + 1) * HALF])
-        nc.sync.dma_start(wv_raw[:], wv.rearrange("(p j) d -> p j d", j=PACK))
+            nc.sync.dma_start(wv_raw[h][:], wv_rows[:, :, h * (D // 2) : (h + 1) * (D // 2)])
 
         warm = sb.tile([P, 1], F32, name="warm")
         warm_out = sb.tile([P, 1], F32, name="warm_out")
         nc.vector.memset(warm[:], 0.0)
         nc.scalar.activation(warm_out[:], warm[:], ACT.Abs_reciprocal_sqrt, bias=1.0)
 
-        window = tiles("window", BLOCKS, [P, T], F32)
-        for b in range(BLOCKS - 1):
-            nc.vector.memset(window[b][:], 0.0)
-        nc.gpsimd.memset(window[BLOCKS - 1][:], 0.0)
+        zeroed = tiles("window", BLOCKS - 1, [P, T], F32)
+        for tile in zeroed:
+            nc.vector.memset(tile[:], 0.0)
+        window = zeroed + zeroed[:1]
+        g_codes = sb.tile([P, HALF + N], U32, name="g_codes", align_bytes=64)
+        g_scales = sb.tile([P, HALF + N], U8, name="g_scales", align_bytes=64)
+        nc.vector.memset(g_codes[:, :HALF], 0)
+        nc.vector.memset(g_scales[:, :HALF].bitcast(U32), 0)
 
         weight = tiles("weight", CHUNKS, [P, CHUNK, PACK], F32)
         for c in range(CHUNKS):
@@ -99,18 +104,14 @@ def tile_attend_gml_cau_kernel(tc, xT, wd, wv, y, cw, rw, offs, out):
 
         a_bank = [ps.tile([P, PACK, CHUNK], F32, name="a_bank%d" % c, tag="bank%d" % c) for c in range(CHUNKS)]
         q = tiles("q", CHUNKS, [P, CHUNK, PACK], F32)
-        u = tiles("u", CHUNKS, [P, CHUNK, PACK], F32)
+        u = [sb.tile([P, CHUNK, PACK], F32, name="u%d" % c, tag="shared%d" % c, align_bytes=64) for c in range(CHUNKS)]
         r = tiles("r", CHUNKS, [P, CHUNK, PACK], F32)
         inv = tiles("inv", CHUNKS, [P, CHUNK, PACK], F32)
         num = tiles("num", CHUNKS, [P, CHUNK, PACK], F32)
         g_bf = tiles("g_bf", 2, [P, HALF, PACK], BF16)
-        g_codes = sb.tile([P, HALF + N], U32, name="g_codes", align_bytes=64)
-        g_scales = sb.tile([P, HALF + N], U8, name="g_scales", align_bytes=64)
-        nc.gpsimd.memset(g_codes[:, :HALF], 0)
-        nc.gpsimd.memset(g_scales[:, :HALF], 0)
-        wv_bf = tiles("wv_bf", 2, [P, 2 * P, PACK], BF16)
-        wv_codes = tiles("wv_codes", 2, [P, 2 * P], U32)
-        wv_scales = tiles("wv_scales", 2, [P, 2 * P], U8)
+        wv_bf = {}
+        wv_codes = tiles("wv_codes", BLOCKS, [P, P], U32)
+        wv_scales = tiles("wv_scales", BLOCKS, [P, P], U8)
 
         def first_product(c):
             h, cols = c // 2, slice((c % 2) * CHUNK, (c % 2 + 1) * CHUNK)
@@ -129,15 +130,19 @@ def tile_attend_gml_cau_kernel(tc, xT, wd, wv, y, cw, rw, offs, out):
         def residual(c):
             h, cols = c // 2, slice((c % 2) * CHUNK, (c % 2 + 1) * CHUNK)
             nc.vector.tensor_tensor(
-                q[c][:],
-                a_bank[c][:].rearrange("p t i -> p i t"),
-                y_half[h][:, :, cols].rearrange("p t i -> p i t"),
+                q[c][:].rearrange("p (n e) t -> p n t e", e=2),
+                a_bank[c][:].rearrange("p t (n e) -> p n t e", e=2),
+                y_half[h][:, :, cols].rearrange("p t (n e) -> p n t e", e=2),
                 ALU.subtract,
             )
 
-        def inverse(c):
+        def square(c):
             nc.scalar.activation(u[c][:], q[c][:], ACT.Square)
+
+        def root(c):
             nc.scalar.activation(r[c][:], u[c][:], ACT.Abs_reciprocal_sqrt, bias=1.0)
+
+        def inverse(c):
             nc.scalar.activation(inv[c][:], r[c][:], ACT.Square)
 
         def numerator(c):
@@ -153,9 +158,12 @@ def tile_attend_gml_cau_kernel(tc, xT, wd, wv, y, cw, rw, offs, out):
                 out=g_codes[:, cols].bitcast(E5M2), scales=g_scales[:, cols], in_=g_bf[h][:].rearrange("p i t -> p (i t)")
             )
 
-        def interleave_wv(b):
-            cols = slice((b % 2) * P, (b % 2 + 1) * P)
-            nc.scalar.copy(wv_bf[b // 2][:, cols, :], wv_raw[:, :, b * P : (b + 1) * P].rearrange("p j d -> p d j"))
+        def interleave_wv(b, tag):
+            wv_bf[b] = sb.tile([P, P, PACK], BF16, name="wv_bf%d" % b, tag=tag, align_bytes=64)
+            nc.scalar.copy(
+                wv_bf[b][:].rearrange("p (n e) j -> p n j e", e=4),
+                wv_raw[b // 2][:, :, (b % 2) * P : (b % 2 + 1) * P].rearrange("p j (n e) -> p n j e", e=4),
+            )
 
         def quantize_wv(k):
             nc.vector.quantize_mx(
@@ -164,12 +172,11 @@ def tile_attend_gml_cau_kernel(tc, xT, wd, wv, y, cw, rw, offs, out):
 
         def second_product(b, first_col, keep, tag):
             bank = ps.tile([P, N], F32, name="dx_" + tag, tag=tag)
-            m = slice((b % 2) * P, (b % 2 + 1) * P)
             cols = slice(first_col, first_col + N)
             nc.tensor.matmul_mx(
                 out=bank[:],
-                lhsT=wv_codes[b // 2][:, m].bitcast(E4M3),
-                lhsT_scale=wv_scales[b // 2][:, m],
+                lhsT=wv_codes[b][:].bitcast(E4M3),
+                lhsT_scale=wv_scales[b][:],
                 rhs=g_codes[:, cols].bitcast(E5M2),
                 rhs_scale=g_scales[:, cols],
                 start=True,
@@ -186,46 +193,54 @@ def tile_attend_gml_cau_kernel(tc, xT, wd, wv, y, cw, rw, offs, out):
         def store(b):
             nc.sync.dma_start(out[b * P : (b + 1) * P, :], window[b][:])
 
+        interleave_wv(0, "wv_first")
         gather(PACK - 1, 0)
         quantize_x(0)
         gather(PACK - 1, 1)
         first_product(0)
         first_product(1)
         residual(0)
-        inverse(0)
+        residual(1)
         quantize_x(1)
         first_product(2)
         first_product(3)
-        residual(1)
-        inverse(1)
+        for stage in (square, root, inverse):
+            stage(0)
+            stage(1)
         numerator(0)
-        residual(2)
         numerator(1)
+        residual(2)
         residual(3)
-        interleave_wv(0)
-        interleave_wv(1)
+        square(2)
+        square(3)
+        interleave_wv(1, "shared1")
+        root(2)
         gradient(0)
         gradient(1)
-        numerator(2)
-        quantize_g(0)
         quantize_wv(0)
+        quantize_g(0)
+        early0 = second_product(0, 0, HALF, "bank0")
+        root(3)
         inverse(2)
-        numerator(3)
-        early = [second_product(b, 0, HALF, "bank%d" % b) for b in range(2)]
         inverse(3)
-        gradient(2)
-        scatter(0, 0, early[0])
-        gradient(3)
-        quantize_g(1)
-        scatter(1, 0, early[1])
-        late = [second_product(b, HALF, HALF, "bank%d" % (4 + b)) for b in range(2)]
-        interleave_wv(2)
-        interleave_wv(3)
-        scatter(0, HALF, late[0])
-        store(0)
+        numerator(2)
         quantize_wv(1)
-        scatter(1, HALF, late[1])
-        store(1)
+        numerator(3)
+        scatter(0, 0, early0)
+        interleave_wv(2, "shared2")
+        interleave_wv(3, "shared3")
+        early1 = second_product(1, 0, HALF, "bank1")
+        gradient(2)
+        gradient(3)
+        quantize_wv(2)
+        quantize_wv(3)
+        quantize_g(1)
+        scatter(1, 0, early1)
+        late = [second_product(b, HALF, HALF, "bank%d" % (4 + b)) for b in range(2)]
+        full = [second_product(b, HALF, N, "bank%d" % (4 + b)) for b in range(2, BLOCKS)]
+        for b in range(2):
+            scatter(b, HALF, late[b])
+            store(b)
         for b in range(2, BLOCKS):
-            scatter(b, 0, second_product(b, HALF, N, "bank%d" % (4 + b)))
+            scatter(b, 0, full[b - 2])
             store(b)

@@ -35,20 +35,23 @@ def tile_attend_gml_cau_kernel(tc, xT, wd, wv, y, cw, rw, offs, out):
         offsets = sb.tile([P, N // 16], U16, name="offsets")
         cw_sb = sb.tile([P, PACK], F32, name="cw_sb")
         rw_sb = sb.tile([P, N], F32, name="rw_sb")
-        wd_raw = sb.tile([P, PACK, V], F32, name="wd_raw")
+        wd_raw = [sb.tile([P, PACK, V // 2], F32, name="wd_raw%d" % h, tag="wd_raw%d" % h, align_bytes=64) for h in range(2)]
         wv_raw = tiles("wv_raw", 2, [P, PACK, D // 2], F32)
         x_plane = tiles("x_plane", PACK, [P, T], F32)
         y_half = tiles("y_half", 2, [P, PACK, HALF], F32)
 
+        x_rows = xT.rearrange("(p j) c -> p j c", j=PACK)
+        wd_rows = wd.rearrange("(p j) v -> p j v", j=PACK)
+        wv_rows = wv.rearrange("(p j) d -> p j d", j=PACK)
+        y_rows = y.rearrange("(p t) i -> p t i", t=PACK)
+        nc.sync.dma_start(x_plane[0][:], x_rows[:, 0, :])
         nc.sync.dma_start(offsets[:], offs)
         nc.sync.dma_start(cw_sb[:], cw.rearrange("(p t) o -> p (t o)", t=PACK))
         nc.sync.dma_start(rw_sb[:], rw)
-        nc.sync.dma_start(wd_raw[:], wd.rearrange("(p j) v -> p j v", j=PACK))
-        x_rows = xT.rearrange("(p j) c -> p j c", j=PACK)
-        for j in range(PACK):
+        for j in range(1, PACK):
             nc.sync.dma_start(x_plane[j][:], x_rows[:, j, :])
-        wv_rows = wv.rearrange("(p j) d -> p j d", j=PACK)
-        y_rows = y.rearrange("(p t) i -> p t i", t=PACK)
+        for h in range(2):
+            nc.sync.dma_start(wd_raw[h][:], wd_rows[:, :, h * (V // 2) : (h + 1) * (V // 2)])
         for h in range(2):
             nc.sync.dma_start(y_half[h][:], y_rows[:, :, h * HALF : (h + 1) * HALF])
             nc.sync.dma_start(wv_raw[h][:], wv_rows[:, :, h * (D // 2) : (h + 1) * (D // 2)])
@@ -67,90 +70,101 @@ def tile_attend_gml_cau_kernel(tc, xT, wd, wv, y, cw, rw, offs, out):
         nc.vector.memset(g_codes[:, :HALF], 0)
         nc.vector.memset(g_scales[:, :HALF].bitcast(U32), 0)
 
-        weight = tiles("weight", CHUNKS, [P, CHUNK, PACK], F32)
-        for c in range(CHUNKS):
-            nc.vector.tensor_tensor(
-                weight[c][:],
-                rw_sb[:, c * CHUNK : (c + 1) * CHUNK].unsqueeze(2).to_broadcast([P, CHUNK, PACK]),
-                cw_sb[:].unsqueeze(1).to_broadcast([P, CHUNK, PACK]),
-                ALU.mult,
+        weight_rows = sb.tile([P, PACK, N], F32, name="weight_rows")
+        for t in range(PACK):
+            nc.scalar.activation(weight_rows[:, t, :], rw_sb[:], ACT.Copy, scale=cw_sb[:, t : t + 1])
+        weight = tiles("weight", 2, [P, HALF, PACK], F32)
+        for h in range(2):
+            nc.scalar.copy(
+                weight[h][:].rearrange("p (n e) t -> p n t e", e=2),
+                weight_rows[:, :, h * HALF : (h + 1) * HALF].rearrange("p t (n e) -> p n t e", e=2),
             )
 
-        wd_bf = sb.tile([P, PACK, P, PACK], BF16, name="wd_bf", align_bytes=64)
-        nc.scalar.copy(wd_bf[:].rearrange("p t m j -> p m t j"), wd_raw[:].rearrange("p j (m t) -> p m t j", t=PACK))
-        wd_codes = sb.tile([P, V], U32, name="wd_codes", align_bytes=64)
-        wd_scales = sb.tile([P, V], U8, name="wd_scales", align_bytes=64)
-
         x_bf = tiles("x_bf", 2, [P, HALF, PACK], BF16)
-        x_codes = tiles("x_codes", 2, [P, HALF], U32)
+        x_codes = {}
         x_scales = tiles("x_scales", 2, [P, HALF], U8)
+        for j in range(PACK):
+            for h in range(2):
+                cols = HALF // 16
+                nc.vector.tensor_copy(x_bf[h][:, :, j], x_plane[j][:].indirect(offsets[:, h * cols : (h + 1) * cols]))
 
-        def gather(j, h):
-            cols = HALF // 16
-            nc.vector.tensor_copy(x_bf[h][:, :, j], x_plane[j][:].indirect(offsets[:, h * cols : (h + 1) * cols]))
-
-        def quantize_x(h):
+        def quantize_x(h, tag):
+            x_codes[h] = sb.tile([P, HALF], U32, name="x_codes%d" % h, tag=tag, align_bytes=64)
             nc.vector.quantize_mx(
                 out=x_codes[h][:].bitcast(E4M3), scales=x_scales[h][:], in_=x_bf[h][:].rearrange("p i j -> p (i j)")
             )
 
-        for j in range(PACK - 1):
-            gather(j, 0)
-            gather(j, 1)
-            if j == 0:
-                nc.vector.quantize_mx(
-                    out=wd_codes[:].bitcast(E4M3), scales=wd_scales[:], in_=wd_bf[:].rearrange("p t m j -> p (t m j)")
-                )
+        quantize_x(0, "x_first")
+
+        wd_bf = tiles("wd_bf", 2, [P, 2, P, PACK], BF16)
+        wd_codes = tiles("wd_codes", 2, [P, 2 * P], U32)
+        wd_scales = tiles("wd_scales", 2, [P, 2 * P], U8)
+
+        def interleave_wd(copy, h, k):
+            copy(
+                wd_bf[k][:, :, h * (P // 2) : (h + 1) * (P // 2), :].rearrange("p t m j -> p m j t"),
+                wd_raw[h][:].rearrange("p j (m t) -> p m j t", t=PACK)[:, :, :, 2 * k : 2 * k + 2],
+            )
+
+        interleave_wd(nc.scalar.copy, 0, 0)
+        interleave_wd(nc.scalar.copy, 0, 1)
+        interleave_wd(nc.vector.tensor_copy, 1, 0)
+        interleave_wd(nc.scalar.copy, 1, 1)
+        for k in range(2):
+            nc.vector.quantize_mx(
+                out=wd_codes[k][:].bitcast(E4M3), scales=wd_scales[k][:], in_=wd_bf[k][:].rearrange("p t m j -> p (t m j)")
+            )
+        quantize_x(1, "wd_raw1")
 
         a_bank = [ps.tile([P, PACK, CHUNK], F32, name="a_bank%d" % c, tag="bank%d" % c) for c in range(CHUNKS)]
-        q = tiles("q", CHUNKS, [P, CHUNK, PACK], F32)
+        q = tiles("q", 2, [P, HALF, PACK], F32)
         u = [sb.tile([P, CHUNK, PACK], F32, name="u%d" % c, tag="shared%d" % c, align_bytes=64) for c in range(CHUNKS)]
         r = tiles("r", CHUNKS, [P, CHUNK, PACK], F32)
-        inv = tiles("inv", CHUNKS, [P, CHUNK, PACK], F32)
-        num = tiles("num", CHUNKS, [P, CHUNK, PACK], F32)
+        inv = tiles("inv", 2, [P, HALF, PACK], F32)
+        num = tiles("num", 2, [P, HALF, PACK], F32)
         g_bf = tiles("g_bf", 2, [P, HALF, PACK], BF16)
         wv_bf = {}
         wv_codes = tiles("wv_codes", BLOCKS, [P, P], U32)
         wv_scales = tiles("wv_scales", BLOCKS, [P, P], U8)
 
+        def part(c):
+            return slice((c % 2) * CHUNK, (c % 2 + 1) * CHUNK)
+
         def first_product(c):
-            h, cols = c // 2, slice((c % 2) * CHUNK, (c % 2 + 1) * CHUNK)
             for t in range(PACK):
-                m = slice(t * P, (t + 1) * P)
+                m = slice((t % 2) * P, (t % 2 + 1) * P)
                 nc.tensor.matmul_mx(
                     out=a_bank[c][:, t, :],
-                    lhsT=wd_codes[:, m].bitcast(E4M3),
-                    lhsT_scale=wd_scales[:, m],
-                    rhs=x_codes[h][:, cols].bitcast(E4M3),
-                    rhs_scale=x_scales[h][:, cols],
+                    lhsT=wd_codes[t // 2][:, m].bitcast(E4M3),
+                    lhsT_scale=wd_scales[t // 2][:, m],
+                    rhs=x_codes[c // 2][:, part(c)].bitcast(E4M3),
+                    rhs_scale=x_scales[c // 2][:, part(c)],
                     start=True,
                     stop=True,
                 )
 
         def residual(c):
-            h, cols = c // 2, slice((c % 2) * CHUNK, (c % 2 + 1) * CHUNK)
             nc.vector.tensor_tensor(
-                q[c][:].rearrange("p (n e) t -> p n t e", e=2),
+                q[c // 2][:, part(c), :].rearrange("p (n e) t -> p n t e", e=2),
                 a_bank[c][:].rearrange("p t (n e) -> p n t e", e=2),
-                y_half[h][:, :, cols].rearrange("p t (n e) -> p n t e", e=2),
+                y_half[c // 2][:, :, part(c)].rearrange("p t (n e) -> p n t e", e=2),
                 ALU.subtract,
             )
 
         def square(c):
-            nc.scalar.activation(u[c][:], q[c][:], ACT.Square)
+            nc.scalar.activation(u[c][:], q[c // 2][:, part(c), :], ACT.Square)
 
         def root(c):
             nc.scalar.activation(r[c][:], u[c][:], ACT.Abs_reciprocal_sqrt, bias=1.0)
 
         def inverse(c):
-            nc.scalar.activation(inv[c][:], r[c][:], ACT.Square)
+            nc.scalar.activation(inv[c // 2][:, part(c), :], r[c][:], ACT.Square)
 
-        def numerator(c):
-            nc.vector.tensor_tensor(num[c][:], q[c][:], weight[c][:], ALU.mult)
+        def numerator(h):
+            nc.vector.tensor_tensor(num[h][:], q[h][:], weight[h][:], ALU.mult)
 
-        def gradient(c):
-            cols = slice((c % 2) * CHUNK, (c % 2 + 1) * CHUNK)
-            nc.vector.tensor_tensor(g_bf[c // 2][:, cols, :], num[c][:], inv[c][:], ALU.mult)
+        def gradient(h, cols):
+            nc.vector.tensor_tensor(g_bf[h][:, cols, :], num[h][:, cols, :], inv[h][:, cols, :], ALU.mult)
 
         def quantize_g(h):
             cols = slice((h + 1) * HALF, (h + 2) * HALF)
@@ -165,9 +179,9 @@ def tile_attend_gml_cau_kernel(tc, xT, wd, wv, y, cw, rw, offs, out):
                 wv_raw[b // 2][:, :, (b % 2) * P : (b % 2 + 1) * P].rearrange("p j (n e) -> p n j e", e=4),
             )
 
-        def quantize_wv(k):
+        def quantize_wv(b):
             nc.vector.quantize_mx(
-                out=wv_codes[k][:].bitcast(E4M3), scales=wv_scales[k][:], in_=wv_bf[k][:].rearrange("p d j -> p (d j)")
+                out=wv_codes[b][:].bitcast(E4M3), scales=wv_scales[b][:], in_=wv_bf[b][:].rearrange("p d j -> p (d j)")
             )
 
         def second_product(b, first_col, keep, tag):
@@ -191,47 +205,39 @@ def tile_attend_gml_cau_kernel(tc, xT, wd, wv, y, cw, rw, offs, out):
             nc.vector.tensor_copy(window[b][:].indirect(offsets[:, first // 16 : (first + count) // 16]), dx[:])
 
         def store(b):
-            nc.sync.dma_start(out[b * P : (b + 1) * P, :], window[b][:])
+            for cols in (slice(0, T // 2), slice(T // 2, T)):
+                nc.sync.dma_start(out[b * P : (b + 1) * P, cols], window[b][:, cols])
 
+        for c in range(CHUNKS):
+            first_product(c)
         interleave_wv(0, "wv_first")
-        gather(PACK - 1, 0)
-        quantize_x(0)
-        gather(PACK - 1, 1)
-        first_product(0)
-        first_product(1)
         residual(0)
         residual(1)
-        quantize_x(1)
-        first_product(2)
-        first_product(3)
         for stage in (square, root, inverse):
             stage(0)
             stage(1)
         numerator(0)
-        numerator(1)
         residual(2)
         residual(3)
         square(2)
         square(3)
         interleave_wv(1, "shared1")
         root(2)
-        gradient(0)
-        gradient(1)
+        gradient(0, part(0))
+        gradient(0, part(1))
         quantize_wv(0)
         quantize_g(0)
         early0 = second_product(0, 0, HALF, "bank0")
         root(3)
         inverse(2)
         inverse(3)
-        numerator(2)
+        numerator(1)
         quantize_wv(1)
-        numerator(3)
         scatter(0, 0, early0)
         interleave_wv(2, "shared2")
         interleave_wv(3, "shared3")
         early1 = second_product(1, 0, HALF, "bank1")
-        gradient(2)
-        gradient(3)
+        gradient(1, slice(0, HALF))
         quantize_wv(2)
         quantize_wv(3)
         quantize_g(1)

@@ -36,7 +36,7 @@ def tile_attend_gml_cau_kernel(tc, xT, wd, wv, y, cw, rw, offs, out):
         cw_sb = sb.tile([P, PACK], F32, name="cw_sb")
         rw_sb = sb.tile([P, N], F32, name="rw_sb")
         wd_raw = [sb.tile([P, PACK, V // 2], F32, name="wd_raw%d" % h, tag="wd_raw%d" % h, align_bytes=64) for h in range(2)]
-        wv_raw = tiles("wv_raw", 2, [P, PACK, D // 2], F32)
+        wv_raw = sb.tile([P, PACK, D], F32, name="wv_raw")
         x_plane = tiles("x_plane", PACK, [P, T], F32)
         y_half = tiles("y_half", 2, [P, PACK, HALF], F32)
 
@@ -54,7 +54,7 @@ def tile_attend_gml_cau_kernel(tc, xT, wd, wv, y, cw, rw, offs, out):
             nc.sync.dma_start(wd_raw[h][:], wd_rows[:, :, h * (V // 2) : (h + 1) * (V // 2)])
         for h in range(2):
             nc.sync.dma_start(y_half[h][:], y_rows[:, :, h * HALF : (h + 1) * HALF])
-            nc.sync.dma_start(wv_raw[h][:], wv_rows[:, :, h * (D // 2) : (h + 1) * (D // 2)])
+        nc.sync.dma_start(wv_raw[:], wv_rows)
 
         warm = sb.tile([P, 1], F32, name="warm")
         warm_out = sb.tile([P, 1], F32, name="warm_out")
@@ -118,10 +118,10 @@ def tile_attend_gml_cau_kernel(tc, xT, wd, wv, y, cw, rw, offs, out):
 
         a_bank = [ps.tile([P, PACK, CHUNK], F32, name="a_bank%d" % c, tag="bank%d" % c) for c in range(CHUNKS)]
         q = tiles("q", 2, [P, HALF, PACK], F32)
-        u = [sb.tile([P, CHUNK, PACK], F32, name="u%d" % c, tag="shared%d" % c, align_bytes=64) for c in range(CHUNKS)]
-        r = tiles("r", CHUNKS, [P, CHUNK, PACK], F32)
-        inv = tiles("inv", 2, [P, HALF, PACK], F32)
-        num = tiles("num", 2, [P, HALF, PACK], F32)
+        u = tiles("u", CHUNKS, [P, CHUNK, PACK], F32)
+        r = [sb.tile([P, CHUNK, PACK], F32, name="r%d" % c, tag="shared%d" % c, align_bytes=64) for c in range(CHUNKS)]
+        inv = [sb.tile([P, HALF, PACK], F32, name="inv%d" % h, tag="inv%d" % h, align_bytes=64) for h in range(2)]
+        num = {}
         g_bf = tiles("g_bf", 2, [P, HALF, PACK], BF16)
         wv_bf = {}
         wv_codes = tiles("wv_codes", BLOCKS, [P, P], U32)
@@ -161,6 +161,7 @@ def tile_attend_gml_cau_kernel(tc, xT, wd, wv, y, cw, rw, offs, out):
             nc.scalar.activation(inv[c // 2][:, part(c), :], r[c][:], ACT.Square)
 
         def numerator(h):
+            num[h] = sb.tile([P, HALF, PACK], F32, name="num%d" % h, tag="num", align_bytes=64)
             nc.vector.tensor_tensor(num[h][:], q[h][:], weight[h][:], ALU.mult)
 
         def gradient(h, cols):
@@ -172,11 +173,11 @@ def tile_attend_gml_cau_kernel(tc, xT, wd, wv, y, cw, rw, offs, out):
                 out=g_codes[:, cols].bitcast(E5M2), scales=g_scales[:, cols], in_=g_bf[h][:].rearrange("p i t -> p (i t)")
             )
 
-        def interleave_wv(b, tag):
-            wv_bf[b] = sb.tile([P, P, PACK], BF16, name="wv_bf%d" % b, tag=tag, align_bytes=64)
+        def interleave_wv(b):
+            wv_bf[b] = sb.tile([P, P, PACK], BF16, name="wv_bf%d" % b, tag="shared%d" % b, align_bytes=64)
             nc.scalar.copy(
                 wv_bf[b][:].rearrange("p (n e) j -> p n j e", e=4),
-                wv_raw[b // 2][:, :, (b % 2) * P : (b % 2 + 1) * P].rearrange("p j (n e) -> p n j e", e=4),
+                wv_raw[:, :, b * P : (b + 1) * P].rearrange("p j (n e) -> p n j e", e=4),
             )
 
         def quantize_wv(b):
@@ -184,7 +185,7 @@ def tile_attend_gml_cau_kernel(tc, xT, wd, wv, y, cw, rw, offs, out):
                 out=wv_codes[b][:].bitcast(E4M3), scales=wv_scales[b][:], in_=wv_bf[b][:].rearrange("p d j -> p (d j)")
             )
 
-        def second_product(b, first_col, keep, tag):
+        def second_product(b, first_col, keep, tag, slot=None):
             bank = ps.tile([P, N], F32, name="dx_" + tag, tag=tag)
             cols = slice(first_col, first_col + N)
             nc.tensor.matmul_mx(
@@ -196,7 +197,7 @@ def tile_attend_gml_cau_kernel(tc, xT, wd, wv, y, cw, rw, offs, out):
                 start=True,
                 stop=True,
             )
-            dx = sb.tile([P, keep], F32, name="dx_sb_" + tag)
+            dx = sb.tile([P, keep], F32, name="dx_sb_" + tag, tag=slot or "dx_" + tag, align_bytes=64)
             nc.scalar.copy(dx[:], bank[:, N - keep :])
             return dx
 
@@ -210,38 +211,38 @@ def tile_attend_gml_cau_kernel(tc, xT, wd, wv, y, cw, rw, offs, out):
 
         for c in range(CHUNKS):
             first_product(c)
-        interleave_wv(0, "wv_first")
         residual(0)
         residual(1)
         for stage in (square, root, inverse):
             stage(0)
             stage(1)
+        interleave_wv(0)
+        interleave_wv(1)
         numerator(0)
         residual(2)
         residual(3)
         square(2)
         square(3)
-        interleave_wv(1, "shared1")
-        root(2)
         gradient(0, part(0))
         gradient(0, part(1))
         quantize_wv(0)
         quantize_g(0)
         early0 = second_product(0, 0, HALF, "bank0")
-        root(3)
-        inverse(2)
-        inverse(3)
+        for stage in (root, inverse):
+            stage(2)
+            stage(3)
         numerator(1)
         quantize_wv(1)
         scatter(0, 0, early0)
-        interleave_wv(2, "shared2")
-        interleave_wv(3, "shared3")
-        early1 = second_product(1, 0, HALF, "bank1")
-        gradient(1, slice(0, HALF))
+        interleave_wv(2)
+        interleave_wv(3)
+        gradient(1, part(0))
+        gradient(1, part(1))
+        early1 = second_product(1, 0, HALF, "bank1", "inv1")
         quantize_wv(2)
-        quantize_wv(3)
         quantize_g(1)
         scatter(1, 0, early1)
+        quantize_wv(3)
         late = [second_product(b, HALF, HALF, "bank%d" % (4 + b)) for b in range(2)]
         full = [second_product(b, HALF, N, "bank%d" % (4 + b)) for b in range(2, BLOCKS)]
         for b in range(2):

@@ -1,6 +1,7 @@
 from contextlib import ExitStack
 
 import concourse.mybir as mybir
+from concourse.masks import make_identity
 
 N, T, D, V = 512, 2048, 512, 512
 FLOPS = 2 * 2 * N * D * V
@@ -34,7 +35,7 @@ def tile_attend_gml_cau_kernel(tc, xT, wd, wv, y, cw, rw, offs, out):
 
         offsets = sb.tile([P, N // 16], U16, name="offsets")
         cw_sb = sb.tile([P, PACK], F32, name="cw_sb")
-        rw_sb = sb.tile([P, N], F32, name="rw_sb")
+        rw_sb = sb.tile([P, PACK], F32, name="rw_sb")
         wd_raw = [sb.tile([P, PACK, V // 2], F32, name="wd_raw%d" % h, tag="wd_raw%d" % h, align_bytes=64) for h in range(2)]
         wv_raw = sb.tile([P, PACK, D], F32, name="wv_raw")
         x_plane = tiles("x_plane", PACK, [P, T], F32)
@@ -46,8 +47,8 @@ def tile_attend_gml_cau_kernel(tc, xT, wd, wv, y, cw, rw, offs, out):
         y_rows = y.rearrange("(p t) i -> p t i", t=PACK)
         nc.sync.dma_start(x_plane[0][:], x_rows[:, 0, :])
         nc.sync.dma_start(offsets[:], offs)
-        nc.sync.dma_start(cw_sb[:], cw.rearrange("(p t) o -> p (t o)", t=PACK))
-        nc.sync.dma_start(rw_sb[:], rw)
+        nc.scalar.dma_start(cw_sb[:], cw.rearrange("(p t) o -> p (t o)", t=PACK))
+        nc.scalar.dma_start(rw_sb[:], rw[0:1, :].rearrange("o (k j) -> k (o j)", j=PACK))
         for j in range(1, PACK):
             nc.sync.dma_start(x_plane[j][:], x_rows[:, j, :])
         for h in range(2):
@@ -70,9 +71,19 @@ def tile_attend_gml_cau_kernel(tc, xT, wd, wv, y, cw, rw, offs, out):
         nc.vector.memset(g_codes[:, :HALF], 0)
         nc.vector.memset(g_scales[:, :HALF].bitcast(U32), 0)
 
+        identity = sb.tile([P, P], F32, name="identity")
+        make_identity(nc, identity[:])
+        rw_bank = ps.tile([P, PACK, P], F32, name="rw_bank", tag="bank7")
+        for j in range(PACK):
+            nc.tensor.transpose(rw_bank[:, j, :], rw_sb[:, j : j + 1].to_broadcast([P, P]), identity[:])
         weight_rows = sb.tile([P, PACK, N], F32, name="weight_rows")
         for t in range(PACK):
-            nc.scalar.activation(weight_rows[:, t, :], rw_sb[:], ACT.Copy, scale=cw_sb[:, t : t + 1])
+            nc.scalar.activation(
+                weight_rows[:, t, :].rearrange("p (k j) -> p k j", j=PACK),
+                rw_bank[:].rearrange("p j k -> p k j"),
+                ACT.Copy,
+                scale=cw_sb[:, t : t + 1],
+            )
         weight = tiles("weight", 2, [P, HALF, PACK], F32)
         for h in range(2):
             nc.scalar.copy(

@@ -84,12 +84,6 @@ def tile_attend_gml_cau_kernel(tc, xT, wd, wv, y, cw, rw, offs, out):
                 ACT.Copy,
                 scale=cw_sb[:, t : t + 1],
             )
-        weight = tiles("weight", 2, [P, HALF, PACK], F32)
-        for h in range(2):
-            nc.scalar.copy(
-                weight[h][:].rearrange("p (n e) t -> p n t e", e=2),
-                weight_rows[:, :, h * HALF : (h + 1) * HALF].rearrange("p t (n e) -> p n t e", e=2),
-            )
 
         x_bf = tiles("x_bf", 2, [P, HALF, PACK], BF16)
         x_codes = {}
@@ -117,21 +111,29 @@ def tile_attend_gml_cau_kernel(tc, xT, wd, wv, y, cw, rw, offs, out):
                 wd_raw[h][:].rearrange("p j (m t) -> p m j t", t=PACK)[:, :, :, 2 * k : 2 * k + 2],
             )
 
+        def quantize_wd(h, t):
+            cols = slice((t % 2) * P + h * (P // 2), (t % 2) * P + (h + 1) * (P // 2))
+            nc.vector.quantize_mx(
+                out=wd_codes[t // 2][:, cols].bitcast(E4M3),
+                scales=wd_scales[t // 2][:, cols],
+                in_=wd_bf[t // 2][:, t % 2, h * (P // 2) : (h + 1) * (P // 2), :].rearrange("p m j -> p (m j)"),
+            )
+
         interleave_wd(nc.scalar.copy, 0, 0)
         interleave_wd(nc.scalar.copy, 0, 1)
+        for t in range(PACK):
+            quantize_wd(0, t)
         interleave_wd(nc.vector.tensor_copy, 1, 0)
         interleave_wd(nc.scalar.copy, 1, 1)
-        for k in range(2):
-            nc.vector.quantize_mx(
-                out=wd_codes[k][:].bitcast(E4M3), scales=wd_scales[k][:], in_=wd_bf[k][:].rearrange("p t m j -> p (t m j)")
-            )
+        for t in range(PACK):
+            quantize_wd(1, t)
         quantize_x(1, "wd_raw1")
 
         a_bank = [ps.tile([P, PACK, CHUNK], F32, name="a_bank%d" % c, tag="bank%d" % c) for c in range(CHUNKS)]
-        q = tiles("q", 2, [P, HALF, PACK], F32)
-        u = tiles("u", CHUNKS, [P, CHUNK, PACK], F32)
-        r = [sb.tile([P, CHUNK, PACK], F32, name="r%d" % c, tag="shared%d" % c, align_bytes=64) for c in range(CHUNKS)]
-        inv = [sb.tile([P, HALF, PACK], F32, name="inv%d" % h, tag="inv%d" % h, align_bytes=64) for h in range(2)]
+        q = tiles("q", 2, [P, PACK, HALF], F32)
+        u = [sb.tile([P, PACK, CHUNK], F32, name="u%d" % c, tag="u%d" % c, align_bytes=64) for c in range(CHUNKS)]
+        r = [sb.tile([P, PACK, CHUNK], F32, name="r%d" % c, tag="shared%d" % c, align_bytes=64) for c in range(CHUNKS)]
+        inv = [sb.tile([P, PACK, CHUNK], F32, name="inv%d" % c, tag="inv%d" % c, align_bytes=64) for c in range(CHUNKS)]
         num = {}
         g_bf = tiles("g_bf", 2, [P, HALF, PACK], BF16)
         wv_bf = {}
@@ -155,38 +157,41 @@ def tile_attend_gml_cau_kernel(tc, xT, wd, wv, y, cw, rw, offs, out):
                 )
 
         def residual(c):
-            nc.vector.tensor_tensor(
-                q[c // 2][:, part(c), :].rearrange("p (n e) t -> p n t e", e=2),
-                a_bank[c][:].rearrange("p t (n e) -> p n t e", e=2),
-                y_half[c // 2][:, :, part(c)].rearrange("p t (n e) -> p n t e", e=2),
-                ALU.subtract,
-            )
+            nc.vector.tensor_tensor(q[c // 2][:, :, part(c)], a_bank[c][:], y_half[c // 2][:, :, part(c)], ALU.subtract)
 
         def square(c):
-            nc.scalar.activation(u[c][:], q[c // 2][:, part(c), :], ACT.Square)
+            nc.scalar.activation(u[c][:], q[c // 2][:, :, part(c)], ACT.Square)
 
         def root(c):
             nc.scalar.activation(r[c][:], u[c][:], ACT.Abs_reciprocal_sqrt, bias=1.0)
 
         def inverse(c):
-            nc.scalar.activation(inv[c // 2][:, part(c), :], r[c][:], ACT.Square)
+            nc.scalar.activation(inv[c][:], r[c][:], ACT.Square)
 
         def numerator(h):
-            num[h] = sb.tile([P, HALF, PACK], F32, name="num%d" % h, tag="num", align_bytes=64)
-            nc.vector.tensor_tensor(num[h][:], q[h][:], weight[h][:], ALU.mult)
+            num[h] = sb.tile([P, PACK, HALF], F32, name="num%d" % h, tag="num", align_bytes=64)
+            nc.vector.tensor_tensor(num[h][:], q[h][:], weight_rows[:, :, h * HALF : (h + 1) * HALF], ALU.mult)
 
-        def gradient(h, cols):
-            nc.vector.tensor_tensor(g_bf[h][:, cols, :], num[h][:, cols, :], inv[h][:, cols, :], ALU.mult)
-
-        def quantize_g(h):
-            cols = slice((h + 1) * HALF, (h + 2) * HALF)
-            nc.vector.quantize_mx(
-                out=g_codes[:, cols].bitcast(E5M2), scales=g_scales[:, cols], in_=g_bf[h][:].rearrange("p i t -> p (i t)")
+        def gradient(c):
+            h, cols = c // 2, part(c)
+            nc.vector.tensor_tensor(
+                g_bf[h][:, cols, :].rearrange("p (n e) t -> p n t e", e=2),
+                num[h][:, :, cols].rearrange("p t (n e) -> p n t e", e=2),
+                inv[c][:].rearrange("p t (n e) -> p n t e", e=2),
+                ALU.mult,
             )
 
-        def interleave_wv(b):
-            wv_bf[b] = sb.tile([P, P, PACK], BF16, name="wv_bf%d" % b, tag="shared%d" % b, align_bytes=64)
-            nc.scalar.copy(
+        def quantize_g(h, first=0, count=HALF):
+            cols = slice((h + 1) * HALF + first, (h + 1) * HALF + first + count)
+            nc.vector.quantize_mx(
+                out=g_codes[:, cols].bitcast(E5M2),
+                scales=g_scales[:, cols],
+                in_=g_bf[h][:, first : first + count, :].rearrange("p i t -> p (i t)"),
+            )
+
+        def interleave_wv(b, copy=nc.scalar.copy, tag=None):
+            wv_bf[b] = sb.tile([P, P, PACK], BF16, name="wv_bf%d" % b, tag=tag or "shared%d" % b, align_bytes=64)
+            copy(
                 wv_bf[b][:].rearrange("p (n e) j -> p n j e", e=4),
                 wv_raw[:, :, b * P : (b + 1) * P].rearrange("p j (n e) -> p n j e", e=4),
             )
@@ -196,7 +201,7 @@ def tile_attend_gml_cau_kernel(tc, xT, wd, wv, y, cw, rw, offs, out):
                 out=wv_codes[b][:].bitcast(E4M3), scales=wv_scales[b][:], in_=wv_bf[b][:].rearrange("p d j -> p (d j)")
             )
 
-        def second_product(b, first_col, keep, tag, slot=None):
+        def second_product(b, first_col, keep, tag, slot=None, copy=nc.scalar.copy):
             bank = ps.tile([P, N], F32, name="dx_" + tag, tag=tag)
             cols = slice(first_col, first_col + N)
             nc.tensor.matmul_mx(
@@ -209,7 +214,7 @@ def tile_attend_gml_cau_kernel(tc, xT, wd, wv, y, cw, rw, offs, out):
                 stop=True,
             )
             dx = sb.tile([P, keep], F32, name="dx_sb_" + tag, tag=slot or "dx_" + tag, align_bytes=64)
-            nc.scalar.copy(dx[:], bank[:, N - keep :])
+            copy(dx[:], bank[:, N - keep :])
             return dx
 
         def scatter(b, first, dx):
@@ -227,29 +232,30 @@ def tile_attend_gml_cau_kernel(tc, xT, wd, wv, y, cw, rw, offs, out):
         for stage in (square, root, inverse):
             stage(0)
             stage(1)
-        interleave_wv(0)
         interleave_wv(1)
         numerator(0)
         residual(2)
         residual(3)
         square(2)
         square(3)
-        gradient(0, part(0))
-        gradient(0, part(1))
+        gradient(0)
+        gradient(1)
+        interleave_wv(0, nc.vector.tensor_copy, "u0")
+        quantize_g(0, 0, CHUNK)
         quantize_wv(0)
-        quantize_g(0)
-        early0 = second_product(0, 0, HALF, "bank0")
+        quantize_g(0, CHUNK, CHUNK)
         for stage in (root, inverse):
             stage(2)
             stage(3)
         numerator(1)
+        early0 = second_product(0, 0, HALF, "bank0", copy=nc.vector.tensor_copy)
         quantize_wv(1)
         scatter(0, 0, early0)
         interleave_wv(2)
         interleave_wv(3)
-        gradient(1, part(0))
-        gradient(1, part(1))
-        early1 = second_product(1, 0, HALF, "bank1", "inv1")
+        gradient(2)
+        gradient(3)
+        early1 = second_product(1, 0, HALF, "bank1", "inv3")
         quantize_wv(2)
         quantize_g(1)
         scatter(1, 0, early1)

@@ -63,16 +63,17 @@ def tile_attend_gml_cau_kernel(tc, xT, wd, wv, y, cw, rw, offs, out):
         nc.scalar.activation(warm_out[:], warm[:], ACT.Abs_reciprocal_sqrt, bias=1.0)
 
         zeroed = tiles("window", BLOCKS - 1, [P, T], F32)
-        for tile in zeroed:
-            nc.vector.memset(tile[:], 0.0)
+        identity = sb.tile([P, P], F32, name="identity")
+        make_identity(nc, identity[:])
+        nc.vector.memset(zeroed[0][:], 0.0)
+        for tile in zeroed[1:]:
+            nc.gpsimd.memset(tile[:], 0.0)
         window = zeroed + zeroed[:1]
         g_codes = sb.tile([P, HALF + N], U32, name="g_codes", align_bytes=64)
         g_scales = sb.tile([P, HALF + N], U8, name="g_scales", align_bytes=64)
         nc.vector.memset(g_codes[:, :HALF], 0)
         nc.vector.memset(g_scales[:, :HALF].bitcast(U32), 0)
 
-        identity = sb.tile([P, P], F32, name="identity")
-        make_identity(nc, identity[:])
         rw_bank = ps.tile([P, PACK, P], F32, name="rw_bank", tag="bank7")
         for j in range(PACK):
             nc.tensor.transpose(rw_bank[:, j, :], rw_sb[:, j : j + 1].to_broadcast([P, P]), identity[:])

@@ -22,6 +22,7 @@ HALF = N // 2
 CHUNK = 128
 CHUNKS = N // CHUNK
 BLOCKS = D // P
+WHOLE, LOW, HIGH = slice(0, CHUNK), slice(0, CHUNK // 2), slice(CHUNK // 2, CHUNK)
 
 
 def tile_attend_gml_cau_kernel(tc, xT, wd, wv, y, cw, rw, offs, out):
@@ -62,13 +63,11 @@ def tile_attend_gml_cau_kernel(tc, xT, wd, wv, y, cw, rw, offs, out):
         nc.vector.memset(warm[:], 0.0)
         nc.scalar.activation(warm_out[:], warm[:], ACT.Abs_reciprocal_sqrt, bias=1.0)
 
-        zeroed = tiles("window", BLOCKS - 1, [P, T], F32)
+        window = tiles("window", BLOCKS, [P, T], F32)
         identity = sb.tile([P, P], F32, name="identity")
         make_identity(nc, identity[:])
-        nc.vector.memset(zeroed[0][:], 0.0)
-        for tile in zeroed[1:]:
-            nc.gpsimd.memset(tile[:], 0.0)
-        window = zeroed + zeroed[:1]
+        for b in range(BLOCKS):
+            (nc.vector if b < 2 else nc.gpsimd).memset(window[b][:], 0.0)
         g_codes = sb.tile([P, HALF + N], U32, name="g_codes", align_bytes=64)
         g_scales = sb.tile([P, HALF + N], U8, name="g_scales", align_bytes=64)
         nc.vector.memset(g_codes[:, :HALF], 0)
@@ -122,27 +121,32 @@ def tile_attend_gml_cau_kernel(tc, xT, wd, wv, y, cw, rw, offs, out):
 
         interleave_wd(nc.scalar.copy, 0, 0)
         interleave_wd(nc.scalar.copy, 0, 1)
-        for t in range(PACK):
-            quantize_wd(0, t)
+        quantize_wd(0, 0)
+        quantize_wd(0, 1)
         interleave_wd(nc.vector.tensor_copy, 1, 0)
         interleave_wd(nc.scalar.copy, 1, 1)
-        for t in range(PACK):
+        quantize_wd(1, 0)
+        quantize_wd(1, 1)
+        for t in (2, 3):
+            quantize_wd(0, t)
             quantize_wd(1, t)
         quantize_x(1, "wd_raw1")
 
         a_bank = [ps.tile([P, PACK, CHUNK], F32, name="a_bank%d" % c, tag="bank%d" % c) for c in range(CHUNKS)]
         q = tiles("q", 2, [P, PACK, HALF], F32)
-        u = [sb.tile([P, PACK, CHUNK], F32, name="u%d" % c, tag="u%d" % c, align_bytes=64) for c in range(CHUNKS)]
-        r = [sb.tile([P, PACK, CHUNK], F32, name="r%d" % c, tag="shared%d" % c, align_bytes=64) for c in range(CHUNKS)]
-        inv = [sb.tile([P, PACK, CHUNK], F32, name="inv%d" % c, tag="inv%d" % c, align_bytes=64) for c in range(CHUNKS)]
+        u, r, inv = {}, {}, {}
         num = {}
         g_bf = tiles("g_bf", 2, [P, HALF, PACK], BF16)
         wv_bf = {}
         wv_codes = tiles("wv_codes", BLOCKS, [P, P], U32)
         wv_scales = tiles("wv_scales", BLOCKS, [P, P], U8)
+        for c in range(CHUNKS):
+            inv[c] = sb.tile([P, PACK, CHUNK], F32, name="inv%d" % c, tag="inv%d" % c, align_bytes=64)
+        for c in range(2):
+            u[c] = sb.tile([P, PACK, CHUNK], F32, name="u%d" % c, tag="u%d" % c, align_bytes=64)
 
-        def part(c):
-            return slice((c % 2) * CHUNK, (c % 2 + 1) * CHUNK)
+        def part(c, piece=WHOLE):
+            return slice((c % 2) * CHUNK + piece.start, (c % 2) * CHUNK + piece.stop)
 
         def first_product(c):
             for t in range(PACK):
@@ -157,28 +161,31 @@ def tile_attend_gml_cau_kernel(tc, xT, wd, wv, y, cw, rw, offs, out):
                     stop=True,
                 )
 
-        def residual(c):
-            nc.vector.tensor_tensor(q[c // 2][:, :, part(c)], a_bank[c][:], y_half[c // 2][:, :, part(c)], ALU.subtract)
+        def residual(c, piece=WHOLE):
+            cols = part(c, piece)
+            nc.vector.tensor_tensor(q[c // 2][:, :, cols], a_bank[c][:, :, piece], y_half[c // 2][:, :, cols], ALU.subtract)
 
-        def square(c):
-            nc.scalar.activation(u[c][:], q[c // 2][:, :, part(c)], ACT.Square)
+        def square(c, piece=WHOLE):
+            nc.scalar.activation(u[c][:, :, piece], q[c // 2][:, :, part(c, piece)], ACT.Square)
 
-        def root(c):
-            nc.scalar.activation(r[c][:], u[c][:], ACT.Abs_reciprocal_sqrt, bias=1.0)
+        def root(c, piece=WHOLE):
+            tag = "r%d_%d" % (c, piece.start)
+            r[c, piece.start] = sb.tile([P, PACK, piece.stop - piece.start], F32, name=tag, tag=tag, align_bytes=64)
+            nc.scalar.activation(r[c, piece.start][:], u[c][:, :, piece], ACT.Abs_reciprocal_sqrt, bias=1.0)
 
-        def inverse(c):
-            nc.scalar.activation(inv[c][:], r[c][:], ACT.Square)
+        def inverse(c, piece=WHOLE):
+            nc.scalar.activation(inv[c][:, :, piece], r[c, piece.start][:], ACT.Square)
 
         def numerator(h):
             num[h] = sb.tile([P, PACK, HALF], F32, name="num%d" % h, tag="num", align_bytes=64)
             nc.vector.tensor_tensor(num[h][:], q[h][:], weight_rows[:, :, h * HALF : (h + 1) * HALF], ALU.mult)
 
-        def gradient(c):
-            h, cols = c // 2, part(c)
+        def gradient(c, piece=WHOLE):
+            h, cols = c // 2, part(c, piece)
             nc.vector.tensor_tensor(
                 g_bf[h][:, cols, :].rearrange("p (n e) t -> p n t e", e=2),
                 num[h][:, :, cols].rearrange("p t (n e) -> p n t e", e=2),
-                inv[c][:].rearrange("p t (n e) -> p n t e", e=2),
+                inv[c][:, :, piece].rearrange("p t (n e) -> p n t e", e=2),
                 ALU.mult,
             )
 
@@ -190,9 +197,9 @@ def tile_attend_gml_cau_kernel(tc, xT, wd, wv, y, cw, rw, offs, out):
                 in_=g_bf[h][:, first : first + count, :].rearrange("p i t -> p (i t)"),
             )
 
-        def interleave_wv(b, copy=nc.scalar.copy, tag=None):
-            wv_bf[b] = sb.tile([P, P, PACK], BF16, name="wv_bf%d" % b, tag=tag or "shared%d" % b, align_bytes=64)
-            copy(
+        def interleave_wv(b, tag):
+            wv_bf[b] = sb.tile([P, P, PACK], BF16, name="wv_bf%d" % b, tag=tag, align_bytes=64)
+            nc.scalar.copy(
                 wv_bf[b][:].rearrange("p (n e) j -> p n j e", e=4),
                 wv_raw[:, :, b * P : (b + 1) * P].rearrange("p j (n e) -> p n j e", e=4),
             )
@@ -228,23 +235,36 @@ def tile_attend_gml_cau_kernel(tc, xT, wd, wv, y, cw, rw, offs, out):
 
         for c in range(CHUNKS):
             first_product(c)
-        residual(0)
+        residual(0, LOW)
+        residual(0, HIGH)
         residual(1)
-        for stage in (square, root, inverse):
-            stage(0)
-            stage(1)
-        interleave_wv(1)
+        square(0, LOW)
+        square(0, HIGH)
+        root(0, LOW)
+        square(1)
+        root(0, HIGH)
+        inverse(0, LOW)
+        inverse(0, HIGH)
+        root(1, LOW)
+        root(1, HIGH)
+        inverse(1, LOW)
+        inverse(1, HIGH)
+        interleave_wv(0, "u1")
+        interleave_wv(1, "r1_0")
         numerator(0)
         residual(2)
         residual(3)
+        u_late = sb.tile([P, PACK, HALF], F32, name="u_late", tag="r1_64", align_bytes=64)
+        u[2], u[3] = u_late[:, :, :CHUNK], u_late[:, :, CHUNK:]
         square(2)
         square(3)
         gradient(0)
-        gradient(1)
-        interleave_wv(0, nc.vector.tensor_copy, "u0")
+        gradient(1, LOW)
+        gradient(1, HIGH)
         quantize_g(0, 0, CHUNK)
+        quantize_g(0, CHUNK, CHUNK // 2)
+        quantize_g(0, CHUNK + CHUNK // 2, CHUNK // 2)
         quantize_wv(0)
-        quantize_g(0, CHUNK, CHUNK)
         for stage in (root, inverse):
             stage(2)
             stage(3)
@@ -252,11 +272,11 @@ def tile_attend_gml_cau_kernel(tc, xT, wd, wv, y, cw, rw, offs, out):
         early0 = second_product(0, 0, HALF, "bank0", copy=nc.vector.tensor_copy)
         quantize_wv(1)
         scatter(0, 0, early0)
-        interleave_wv(2)
-        interleave_wv(3)
+        interleave_wv(2, "r2_0")
+        interleave_wv(3, "r3_0")
         gradient(2)
         gradient(3)
-        early1 = second_product(1, 0, HALF, "bank1", "inv3")
+        early1 = second_product(1, 0, HALF, "bank1", "inv2")
         quantize_wv(2)
         quantize_g(1)
         scatter(1, 0, early1)

@@ -277,8 +277,9 @@ def tile_attend_gml_cau_kernel(tc, xT, wd, wv, y, cw, rw, offs, out):
         gradient(2)
         gradient(3)
         early1 = second_product(1, 0, HALF, "bank1", "inv2")
+        quantize_g(1, 0, CHUNK)
+        quantize_g(1, CHUNK, CHUNK)
         quantize_wv(2)
-        quantize_g(1)
         scatter(1, 0, early1)
         quantize_wv(3)
         late = [second_product(b, HALF, HALF, "bank%d" % (4 + b)) for b in range(2)]

@@ -132,7 +132,14 @@ def tile_attend_gml_cau_kernel(tc, xT, wd, wv, y, cw, rw, offs, out):
             quantize_wd(1, t)
         quantize_x(1, "wd_raw1")
 
-        a_bank = [ps.tile([P, PACK, CHUNK], F32, name="a_bank%d" % c, tag="bank%d" % c) for c in range(CHUNKS)]
+        a_pair = {
+            (c, k): ps.tile([P, 2, CHUNK], F32, name="a_pair%d%d" % (c, k), tag="bank%d" % (2 * c + k))
+            for c in range(2)
+            for k in range(2)
+        }
+        a_bank = {c: ps.tile([P, PACK, CHUNK], F32, name="a_bank%d" % c, tag="bank%d" % (c + 2)) for c in (2, 3)}
+        for c in (2, 3):
+            a_pair[c, 0], a_pair[c, 1] = a_bank[c][:, :2, :], a_bank[c][:, 2:, :]
         q = tiles("q", 2, [P, PACK, HALF], F32)
         u, r, inv = {}, {}, {}
         num = {}
@@ -148,11 +155,11 @@ def tile_attend_gml_cau_kernel(tc, xT, wd, wv, y, cw, rw, offs, out):
         def part(c, piece=WHOLE):
             return slice((c % 2) * CHUNK + piece.start, (c % 2) * CHUNK + piece.stop)
 
-        def first_product(c):
-            for t in range(PACK):
+        def first_product(c, k):
+            for t in (2 * k, 2 * k + 1):
                 m = slice((t % 2) * P, (t % 2 + 1) * P)
                 nc.tensor.matmul_mx(
-                    out=a_bank[c][:, t, :],
+                    out=a_pair[c, k][:, t % 2, :],
                     lhsT=wd_codes[t // 2][:, m].bitcast(E4M3),
                     lhsT_scale=wd_scales[t // 2][:, m],
                     rhs=x_codes[c // 2][:, part(c)].bitcast(E4M3),
@@ -164,6 +171,21 @@ def tile_attend_gml_cau_kernel(tc, xT, wd, wv, y, cw, rw, offs, out):
         def residual(c, piece=WHOLE):
             cols = part(c, piece)
             nc.vector.tensor_tensor(q[c // 2][:, :, cols], a_bank[c][:, :, piece], y_half[c // 2][:, :, cols], ALU.subtract)
+
+        def residual_pair(c, k):
+            slots = slice(2 * k, 2 * k + 2)
+            nc.vector.tensor_tensor(q[0][:, slots, part(c)], a_pair[c, k][:], y_half[0][:, slots, part(c)], ALU.subtract)
+
+        def square_pair(c, k):
+            slots = slice(2 * k, 2 * k + 2)
+            nc.scalar.activation(u[c][:, slots, :], q[0][:, slots, part(c)], ACT.Square)
+
+        def root_pair(k):
+            r[0, k] = sb.tile([P, 2, CHUNK], F32, name="r0_%d" % k, tag="r0_%d" % k, align_bytes=64)
+            nc.scalar.activation(r[0, k][:], u[0][:, 2 * k : 2 * k + 2, :], ACT.Abs_reciprocal_sqrt, bias=1.0)
+
+        def inverse_pair(k):
+            nc.scalar.activation(inv[0][:, 2 * k : 2 * k + 2, :], r[0, k][:], ACT.Square)
 
         def square(c, piece=WHOLE):
             nc.scalar.activation(u[c][:, :, piece], q[c // 2][:, :, part(c, piece)], ACT.Square)
@@ -233,19 +255,20 @@ def tile_attend_gml_cau_kernel(tc, xT, wd, wv, y, cw, rw, offs, out):
             for cols in (slice(0, T // 2), slice(T // 2, T)):
                 nc.sync.dma_start(out[b * P : (b + 1) * P, cols], window[b][:, cols])
 
-        for c in range(CHUNKS):
-            first_product(c)
-        residual(0, LOW)
-        residual(0, HIGH)
-        residual(1)
-        square(0, LOW)
-        square(0, HIGH)
-        root(0, LOW)
-        square(1)
-        root(0, HIGH)
-        inverse(0, LOW)
-        inverse(0, HIGH)
+        for c, k in ((0, 0), (1, 0), (0, 1), (1, 1), (2, 0), (2, 1), (3, 0), (3, 1)):
+            first_product(c, k)
+        for k in range(2):
+            for c in range(2):
+                residual_pair(c, k)
+        square_pair(0, 0)
+        square_pair(1, 0)
+        root_pair(0)
+        square_pair(0, 1)
+        inverse_pair(0)
+        square_pair(1, 1)
+        root_pair(1)
         root(1, LOW)
+        inverse_pair(1)
         root(1, HIGH)
         inverse(1, LOW)
         inverse(1, HIGH)
@@ -282,7 +305,7 @@ def tile_attend_gml_cau_kernel(tc, xT, wd, wv, y, cw, rw, offs, out):
         quantize_wv(2)
         scatter(1, 0, early1)
         quantize_wv(3)
-        late = [second_product(b, HALF, HALF, "bank%d" % (4 + b)) for b in range(2)]
+        late = [second_product(b, HALF, HALF, "bank%d" % (2 + b)) for b in range(2)]
         full = [second_product(b, HALF, N, "bank%d" % (4 + b)) for b in range(2, BLOCKS)]
         for b in range(2):
             scatter(b, HALF, late[b])

@@ -40,7 +40,8 @@ def tile_attend_gml_cau_kernel(tc, xT, wd, wv, y, cw, rw, offs, out):
         wd_raw = [sb.tile([P, PACK, V // 2], F32, name="wd_raw%d" % h, tag="wd_raw%d" % h, align_bytes=64) for h in range(2)]
         wv_raw = sb.tile([P, PACK, D], F32, name="wv_raw")
         x_plane = tiles("x_plane", PACK, [P, T], F32)
-        y_half = tiles("y_half", 2, [P, PACK, HALF], F32)
+        y_pair = tiles("y_pair", 2, [P, 2, HALF], F32)
+        y_half = {1: sb.tile([P, PACK, HALF], F32, name="y_late", align_bytes=64)}
 
         x_rows = xT.rearrange("(p j) c -> p j c", j=PACK)
         wd_rows = wd.rearrange("(p j) v -> p j v", j=PACK)
@@ -54,8 +55,9 @@ def tile_attend_gml_cau_kernel(tc, xT, wd, wv, y, cw, rw, offs, out):
             nc.sync.dma_start(x_plane[j][:], x_rows[:, j, :])
         for h in range(2):
             nc.sync.dma_start(wd_raw[h][:], wd_rows[:, :, h * (V // 2) : (h + 1) * (V // 2)])
-        for h in range(2):
-            nc.sync.dma_start(y_half[h][:], y_rows[:, :, h * HALF : (h + 1) * HALF])
+        for k in range(2):
+            nc.sync.dma_start(y_pair[k][:], y_rows[:, 2 * k : 2 * k + 2, :HALF])
+        nc.sync.dma_start(y_half[1][:], y_rows[:, :, HALF:])
         nc.sync.dma_start(wv_raw[:], wv_rows)
 
         warm = sb.tile([P, 1], F32, name="warm")
@@ -174,7 +176,7 @@ def tile_attend_gml_cau_kernel(tc, xT, wd, wv, y, cw, rw, offs, out):
 
         def residual_pair(c, k):
             slots = slice(2 * k, 2 * k + 2)
-            nc.vector.tensor_tensor(q[0][:, slots, part(c)], a_pair[c, k][:], y_half[0][:, slots, part(c)], ALU.subtract)
+            nc.vector.tensor_tensor(q[0][:, slots, part(c)], a_pair[c, k][:], y_pair[k][:, :, part(c)], ALU.subtract)
 
         def square_pair(c, k):
             slots = slice(2 * k, 2 * k + 2)

@@ -35,8 +35,8 @@ def tile_attend_gml_cau_kernel(tc, xT, wd, wv, y, cw, rw, offs, out):
             return [sb.tile(shape, dtype, name="%s%d" % (name, i), align_bytes=64) for i in range(count)]
 
         offsets = sb.tile([P, N // 16], U16, name="offsets")
-        cw_sb = sb.tile([P, PACK], F32, name="cw_sb")
-        rw_sb = sb.tile([P, PACK], F32, name="rw_sb")
+        weights_row = sb.tile([P, N], F32, name="weights_row")
+        nc.gpsimd.memset(weights_row[:], 0.0)
         wd_raw = [sb.tile([P, PACK, V // 2], F32, name="wd_raw%d" % h, tag="wd_raw%d" % h, align_bytes=64) for h in range(2)]
         wv_raw = sb.tile([P, PACK, D], F32, name="wv_raw")
         x_plane = tiles("x_plane", PACK, [P, T], F32)
@@ -49,8 +49,8 @@ def tile_attend_gml_cau_kernel(tc, xT, wd, wv, y, cw, rw, offs, out):
         y_rows = y.rearrange("(p t) i -> p t i", t=PACK)
         nc.sync.dma_start(x_plane[0][:], x_rows[:, 0, :])
         nc.sync.dma_start(offsets[:], offs)
-        nc.scalar.dma_start(cw_sb[:], cw.rearrange("(p t) o -> p (t o)", t=PACK))
-        nc.scalar.dma_start(rw_sb[:], rw[0:1, :].rearrange("o (k j) -> k (o j)", j=PACK))
+        nc.sync.dma_start(weights_row[0:1, :], cw.rearrange("v o -> o v"))
+        nc.sync.dma_start(weights_row[1:2, :], rw[0:1, :])
         for j in range(1, PACK):
             nc.sync.dma_start(x_plane[j][:], x_rows[:, j, :])
         for h in range(2):
@@ -75,16 +75,21 @@ def tile_attend_gml_cau_kernel(tc, xT, wd, wv, y, cw, rw, offs, out):
         nc.vector.memset(g_codes[:, :HALF], 0)
         nc.vector.memset(g_scales[:, :HALF].bitcast(U32), 0)
 
+        turned = ps.tile([P, PACK, P], F32, name="turned", tag="bank6")
+        for j in range(PACK):
+            nc.tensor.transpose(turned[:, j, :], weights_row[:, j::PACK], identity[:])
+        weights_col = sb.tile([P, PACK, 2], F32, name="weights_col")
+        nc.scalar.copy(weights_col[:], turned[:, :, :2])
         rw_bank = ps.tile([P, PACK, P], F32, name="rw_bank", tag="bank7")
         for j in range(PACK):
-            nc.tensor.transpose(rw_bank[:, j, :], rw_sb[:, j : j + 1].to_broadcast([P, P]), identity[:])
+            nc.tensor.transpose(rw_bank[:, j, :], weights_col[:, j, 1:2].to_broadcast([P, P]), identity[:])
         weight_rows = sb.tile([P, PACK, N], F32, name="weight_rows")
         for t in range(PACK):
             nc.scalar.activation(
                 weight_rows[:, t, :].rearrange("p (k j) -> p k j", j=PACK),
                 rw_bank[:].rearrange("p j k -> p k j"),
                 ACT.Copy,
-                scale=cw_sb[:, t : t + 1],
+                scale=weights_col[:, t, 0:1],
             )
 
         x_bf = tiles("x_bf", 2, [P, HALF, PACK], BF16)

@@ -37,11 +37,17 @@ def tile_attend_gml_cau_kernel(tc, xT, wd, wv, y, cw, rw, offs, out):
         offsets = sb.tile([P, N // 16], U16, name="offsets")
         weights_row = sb.tile([P, N], F32, name="weights_row")
         nc.gpsimd.memset(weights_row[:], 0.0)
-        wd_raw = [sb.tile([P, PACK, V // 2], F32, name="wd_raw%d" % h, tag="wd_raw%d" % h, align_bytes=64) for h in range(2)]
-        wv_raw = sb.tile([P, PACK, D], F32, name="wv_raw")
+        reuse = ctx.enter_context(tc.tile_pool(name="reuse", bufs=1))
+        wd_raw = [
+            sb.tile([P, PACK, V // 2], F32, name="wd_raw0", align_bytes=64),
+            reuse.tile([P, PACK, V // 2], F32, name="wd_raw1", align_bytes=64, offset=0),
+        ]
+        wv_first = tiles("wv_first", 2, [P, PACK, P], F32)
+        wv_last = sb.tile([P, PACK, 2 * P], F32, name="wv_last", align_bytes=64)
         x_plane = tiles("x_plane", PACK, [P, T], F32)
-        y_pair = tiles("y_pair", 2, [P, 2, HALF], F32)
-        y_half = {1: sb.tile([P, PACK, HALF], F32, name="y_late", align_bytes=64)}
+        y_first = tiles("y_first", 2, [P, 2, CHUNK], F32)
+        y_second = sb.tile([P, PACK, CHUNK], F32, name="y_second", align_bytes=64)
+        y_late = tiles("y_late", 2, [P, PACK, CHUNK], F32)
 
         x_rows = xT.rearrange("(p j) c -> p j c", j=PACK)
         wd_rows = wd.rearrange("(p j) v -> p j v", j=PACK)
@@ -56,9 +62,13 @@ def tile_attend_gml_cau_kernel(tc, xT, wd, wv, y, cw, rw, offs, out):
         for h in range(2):
             nc.sync.dma_start(wd_raw[h][:], wd_rows[:, :, h * (V // 2) : (h + 1) * (V // 2)])
         for k in range(2):
-            nc.sync.dma_start(y_pair[k][:], y_rows[:, 2 * k : 2 * k + 2, :HALF])
-        nc.sync.dma_start(y_half[1][:], y_rows[:, :, HALF:])
-        nc.sync.dma_start(wv_raw[:], wv_rows)
+            nc.sync.dma_start(wv_first[k][:], wv_rows[:, :, k * P : (k + 1) * P])
+        for k in range(2):
+            nc.sync.dma_start(y_first[k][:], y_rows[:, 2 * k : 2 * k + 2, :CHUNK])
+        nc.sync.dma_start(y_second[:], y_rows[:, :, CHUNK:HALF])
+        for c in range(2):
+            nc.sync.dma_start(y_late[c][:], y_rows[:, :, HALF + c * CHUNK : HALF + (c + 1) * CHUNK])
+        nc.sync.dma_start(wv_last[:], wv_rows[:, :, 2 * P :])
 
         warm = sb.tile([P, 1], F32, name="warm")
         warm_out = sb.tile([P, 1], F32, name="warm_out")
@@ -92,6 +102,9 @@ def tile_attend_gml_cau_kernel(tc, xT, wd, wv, y, cw, rw, offs, out):
                 scale=weights_col[:, t, 0:1],
             )
 
+        weight_late = sb.tile([P, HALF, PACK], F32, name="weight_late", tag="weight_late", align_bytes=64)
+        nc.gpsimd.tensor_copy(weight_late[:], weight_rows[:, :, HALF:].rearrange("p t i -> p i t"))
+
         x_bf = tiles("x_bf", 2, [P, HALF, PACK], BF16)
         x_codes = {}
         x_scales = tiles("x_scales", 2, [P, HALF], U8)
@@ -100,13 +113,13 @@ def tile_attend_gml_cau_kernel(tc, xT, wd, wv, y, cw, rw, offs, out):
                 cols = HALF // 16
                 nc.vector.tensor_copy(x_bf[h][:, :, j], x_plane[j][:].indirect(offsets[:, h * cols : (h + 1) * cols]))
 
-        def quantize_x(h, tag):
-            x_codes[h] = sb.tile([P, HALF], U32, name="x_codes%d" % h, tag=tag, align_bytes=64)
+        def quantize_x(h, codes):
+            x_codes[h] = codes
             nc.vector.quantize_mx(
                 out=x_codes[h][:].bitcast(E4M3), scales=x_scales[h][:], in_=x_bf[h][:].rearrange("p i j -> p (i j)")
             )
 
-        quantize_x(0, "x_first")
+        quantize_x(0, sb.tile([P, HALF], U32, name="x_codes0", align_bytes=64))
 
         wd_bf = tiles("wd_bf", 2, [P, 2, P, PACK], BF16)
         wd_codes = tiles("wd_codes", 2, [P, 2 * P], U32)
@@ -137,7 +150,7 @@ def tile_attend_gml_cau_kernel(tc, xT, wd, wv, y, cw, rw, offs, out):
         for t in (2, 3):
             quantize_wd(0, t)
             quantize_wd(1, t)
-        quantize_x(1, "wd_raw1")
+        quantize_x(1, reuse.tile([P, HALF], U32, name="x_codes1", align_bytes=64, offset=0))
 
         a_pair = {
             (c, k): ps.tile([P, 2, CHUNK], F32, name="a_pair%d%d" % (c, k), tag="bank%d" % (2 * c + k))
@@ -147,16 +160,13 @@ def tile_attend_gml_cau_kernel(tc, xT, wd, wv, y, cw, rw, offs, out):
         a_bank = {c: ps.tile([P, PACK, CHUNK], F32, name="a_bank%d" % c, tag="bank%d" % (c + 2)) for c in (2, 3)}
         for c in (2, 3):
             a_pair[c, 0], a_pair[c, 1] = a_bank[c][:, :2, :], a_bank[c][:, 2:, :]
-        q = tiles("q", 2, [P, PACK, HALF], F32)
+        q = sb.tile([P, PACK, HALF], F32, name="q", align_bytes=64)
+        q_late = sb.tile([P, HALF, PACK], F32, name="q_late", align_bytes=64)
         u, r, inv = {}, {}, {}
-        num = {}
-        g_bf = tiles("g_bf", 2, [P, HALF, PACK], BF16)
-        wv_bf = {}
-        wv_codes = tiles("wv_codes", BLOCKS, [P, P], U32)
-        wv_scales = tiles("wv_scales", BLOCKS, [P, P], U8)
-        for c in range(CHUNKS):
-            inv[c] = sb.tile([P, PACK, CHUNK], F32, name="inv%d" % c, tag="inv%d" % c, align_bytes=64)
+        g_bf = {}
+        wv_bf, wv_codes, wv_scales = {}, {}, {}
         for c in range(2):
+            inv[c] = sb.tile([P, PACK, CHUNK], F32, name="inv%d" % c, tag="inv%d" % c, align_bytes=64)
             u[c] = sb.tile([P, PACK, CHUNK], F32, name="u%d" % c, tag="u%d" % c, align_bytes=64)
 
         def part(c, piece=WHOLE):
@@ -175,65 +185,87 @@ def tile_attend_gml_cau_kernel(tc, xT, wd, wv, y, cw, rw, offs, out):
                     stop=True,
                 )
 
-        def residual(c, piece=WHOLE):
-            cols = part(c, piece)
-            nc.vector.tensor_tensor(q[c // 2][:, :, cols], a_bank[c][:, :, piece], y_half[c // 2][:, :, cols], ALU.subtract)
+        def residual_late(c):
+            nc.vector.tensor_tensor(
+                q_late[:, part(c), :].rearrange("p (n e) t -> p n t e", e=4),
+                a_bank[c][:].rearrange("p t (n e) -> p n t e", e=4),
+                y_late[c - 2][:].rearrange("p t (n e) -> p n t e", e=4),
+                ALU.subtract,
+            )
 
         def residual_pair(c, k):
+            targets = y_second[:, 2 * k : 2 * k + 2, :] if c else y_first[k][:]
             slots = slice(2 * k, 2 * k + 2)
-            nc.vector.tensor_tensor(q[0][:, slots, part(c)], a_pair[c, k][:], y_pair[k][:, :, part(c)], ALU.subtract)
+            nc.vector.tensor_tensor(q[:, slots, part(c)], a_pair[c, k][:], targets, ALU.subtract)
 
         def square_pair(c, k):
             slots = slice(2 * k, 2 * k + 2)
-            nc.scalar.activation(u[c][:, slots, :], q[0][:, slots, part(c)], ACT.Square)
+            nc.scalar.activation(u[c][:, slots, :], q[:, slots, part(c)], ACT.Square)
 
-        def root_pair(k):
-            r[0, k] = sb.tile([P, 2, CHUNK], F32, name="r0_%d" % k, tag="r0_%d" % k, align_bytes=64)
-            nc.scalar.activation(r[0, k][:], u[0][:, 2 * k : 2 * k + 2, :], ACT.Abs_reciprocal_sqrt, bias=1.0)
-
-        def inverse_pair(k):
-            nc.scalar.activation(inv[0][:, 2 * k : 2 * k + 2, :], r[0, k][:], ACT.Square)
-
-        def square(c, piece=WHOLE):
-            nc.scalar.activation(u[c][:, :, piece], q[c // 2][:, :, part(c, piece)], ACT.Square)
-
-        def root(c, piece=WHOLE):
+        def root(c, piece):
             tag = "r%d_%d" % (c, piece.start)
             r[c, piece.start] = sb.tile([P, PACK, piece.stop - piece.start], F32, name=tag, tag=tag, align_bytes=64)
             nc.scalar.activation(r[c, piece.start][:], u[c][:, :, piece], ACT.Abs_reciprocal_sqrt, bias=1.0)
 
-        def inverse(c, piece=WHOLE):
+        def inverse(c, piece):
             nc.scalar.activation(inv[c][:, :, piece], r[c, piece.start][:], ACT.Square)
 
-        def numerator(h):
-            num[h] = sb.tile([P, PACK, HALF], F32, name="num%d" % h, tag="num", align_bytes=64)
-            nc.vector.tensor_tensor(num[h][:], q[h][:], weight_rows[:, :, h * HALF : (h + 1) * HALF], ALU.mult)
+        def square_late(c, piece):
+            nc.scalar.activation(u[c][:, piece, :], q_late[:, part(c, piece), :], ACT.Square)
+
+        def root_late(c, piece):
+            tag = "r%d_%d" % (c, piece.start)
+            r[c, piece.start] = sb.tile([P, piece.stop - piece.start, PACK], F32, name=tag, tag=tag, align_bytes=64)
+            nc.scalar.activation(r[c, piece.start][:], u[c][:, piece, :], ACT.Abs_reciprocal_sqrt, bias=1.0)
+
+        def inverse_late(c, piece):
+            tag = "inv%d_%d" % (c, piece.start)
+            inv[c, piece.start] = sb.tile([P, piece.stop - piece.start, PACK], F32, name=tag, tag=tag, align_bytes=64)
+            nc.scalar.activation(inv[c, piece.start][:], r[c, piece.start][:], ACT.Square)
+
+        def numerator_pair(c, k):
+            slots = slice(2 * k, 2 * k + 2)
+            nc.gpsimd.tensor_tensor(num[c][:, slots, :], q[:, slots, part(c)], weight_rows[:, slots, part(c)], ALU.mult)
+
+        def numerator_late(c, tag):
+            num[c] = sb.tile([P, CHUNK, PACK], F32, name="num%d" % c, tag=tag, align_bytes=64)
+            nc.vector.tensor_tensor(num[c][:], q_late[:, part(c), :], weight_late[:, part(c), :], ALU.mult)
 
         def gradient(c, piece=WHOLE):
-            h, cols = c // 2, part(c, piece)
+            g_bf[c, piece.start] = sb.tile([P, piece.stop - piece.start, PACK], BF16, name="g%d_%d" % (c, piece.start), align_bytes=64)
             nc.vector.tensor_tensor(
-                g_bf[h][:, cols, :].rearrange("p (n e) t -> p n t e", e=2),
-                num[h][:, :, cols].rearrange("p t (n e) -> p n t e", e=2),
+                g_bf[c, piece.start][:].rearrange("p (n e) t -> p n t e", e=2),
+                num[c][:, :, piece].rearrange("p t (n e) -> p n t e", e=2),
                 inv[c][:, :, piece].rearrange("p t (n e) -> p n t e", e=2),
                 ALU.mult,
             )
 
-        def quantize_g(h, first=0, count=HALF):
-            cols = slice((h + 1) * HALF + first, (h + 1) * HALF + first + count)
+        def gradient_late(engine, c, piece, tag=None):
+            name = "g%d_%d" % (c, piece.start)
+            g_bf[c, piece.start] = sb.tile([P, piece.stop - piece.start, PACK], BF16, name=name, tag=tag or name, align_bytes=64)
+            engine.tensor_tensor(g_bf[c, piece.start][:], num[c][:, piece, :], inv[c, piece.start][:], ALU.mult)
+
+        def quantize_g(c, piece=WHOLE):
+            cols = slice(HALF + c * CHUNK + piece.start, HALF + c * CHUNK + piece.stop)
             nc.vector.quantize_mx(
                 out=g_codes[:, cols].bitcast(E5M2),
                 scales=g_scales[:, cols],
-                in_=g_bf[h][:, first : first + count, :].rearrange("p i t -> p (i t)"),
+                in_=g_bf[c, piece.start][:].rearrange("p i t -> p (i t)"),
             )
 
-        def interleave_wv(b, tag):
-            wv_bf[b] = sb.tile([P, P, PACK], BF16, name="wv_bf%d" % b, tag=tag, align_bytes=64)
+        def interleave_wv(b, source, tag=None):
+            if tag:
+                wv_bf[b] = sb.tile([P, P, PACK], BF16, name="wv_bf%d" % b, tag=tag, align_bytes=64)
+            else:
+                wv_bf[b] = reuse.tile([P, P, PACK], BF16, name="wv_bf%d" % b, align_bytes=64, offset=1024 * (b + 1))
             nc.scalar.copy(
                 wv_bf[b][:].rearrange("p (n e) j -> p n j e", e=4),
-                wv_raw[:, :, b * P : (b + 1) * P].rearrange("p j (n e) -> p n j e", e=4),
+                source.rearrange("p j (n e) -> p n j e", e=4),
             )
 
-        def quantize_wv(b):
+        def quantize_wv(b, tag):
+            wv_codes[b] = sb.tile([P, P], U32, name="wv_codes%d" % b, tag=tag, align_bytes=64)
+            wv_scales[b] = sb.tile([P, P], U8, name="wv_scales%d" % b, align_bytes=64)
             nc.vector.quantize_mx(
                 out=wv_codes[b][:].bitcast(E4M3), scales=wv_scales[b][:], in_=wv_bf[b][:].rearrange("p d j -> p (d j)")
             )
@@ -262,56 +294,67 @@ def tile_attend_gml_cau_kernel(tc, xT, wd, wv, y, cw, rw, offs, out):
             for cols in (slice(0, T // 2), slice(T // 2, T)):
                 nc.sync.dma_start(out[b * P : (b + 1) * P, cols], window[b][:, cols])
 
-        for c, k in ((0, 0), (1, 0), (0, 1), (1, 1), (2, 0), (2, 1), (3, 0), (3, 1)):
-            first_product(c, k)
-        for k in range(2):
-            for c in range(2):
+        num = {c: sb.tile([P, PACK, CHUNK], F32, name="num%d" % c, tag="num%d" % c, align_bytes=64) for c in range(2)}
+        interleave_wv(0, wv_first[0][:])
+        interleave_wv(1, wv_first[1][:])
+        for c in range(CHUNKS):
+            for k in range(2):
+                first_product(c, k)
+        for c in range(2):
+            for k in range(2):
                 residual_pair(c, k)
-        square_pair(0, 0)
-        square_pair(1, 0)
-        root_pair(0)
-        square_pair(0, 1)
-        inverse_pair(0)
-        square_pair(1, 1)
-        root_pair(1)
+                numerator_pair(c, k)
+                square_pair(c, k)
+        root(0, LOW)
+        root(0, HIGH)
         root(1, LOW)
-        inverse_pair(1)
+        inverse(0, LOW)
         root(1, HIGH)
+        inverse(0, HIGH)
         inverse(1, LOW)
         inverse(1, HIGH)
-        interleave_wv(0, "u1")
-        interleave_wv(1, "r1_0")
-        numerator(0)
-        residual(2)
-        residual(3)
-        u_late = sb.tile([P, PACK, HALF], F32, name="u_late", tag="r1_64", align_bytes=64)
-        u[2], u[3] = u_late[:, :, :CHUNK], u_late[:, :, CHUNK:]
-        square(2)
-        square(3)
-        gradient(0)
+        residual_late(2)
+        residual_late(3)
+        numerator_late(2, "num2")
+        gradient(0, LOW)
+        quantize_wv(0, "r0_0")
+        quantize_g(0, LOW)
+        gradient(0, HIGH)
         gradient(1, LOW)
         gradient(1, HIGH)
-        quantize_g(0, 0, CHUNK)
-        quantize_g(0, CHUNK, CHUNK // 2)
-        quantize_g(0, CHUNK + CHUNK // 2, CHUNK // 2)
-        quantize_wv(0)
-        for stage in (root, inverse):
-            stage(2)
-            stage(3)
-        numerator(1)
+        quantize_g(0, HIGH)
+        quantize_g(1, LOW)
+        quantize_g(1, HIGH)
+        quantize_wv(1, "inv1")
+        u[2] = sb.tile([P, CHUNK, PACK], F32, name="u2", tag="r1_0", align_bytes=64)
+        u[3] = sb.tile([P, CHUNK, PACK], F32, name="u3", tag="r1_64", align_bytes=64)
+        square_late(2, LOW)
+        square_late(2, HIGH)
+        root_late(2, LOW)
+        root_late(2, HIGH)
+        inverse_late(2, LOW)
+        square_late(3, WHOLE)
+        inverse_late(2, HIGH)
+        root_late(3, LOW)
+        root_late(3, HIGH)
+        inverse_late(3, LOW)
+        inverse_late(3, HIGH)
+        numerator_late(3, "num1")
         early0 = second_product(0, 0, HALF, "bank0", copy=nc.vector.tensor_copy)
-        quantize_wv(1)
         scatter(0, 0, early0)
-        interleave_wv(2, "r2_0")
-        interleave_wv(3, "r3_0")
-        gradient(2)
-        gradient(3)
-        early1 = second_product(1, 0, HALF, "bank1", "inv2")
-        quantize_g(1, 0, CHUNK)
-        quantize_g(1, CHUNK, CHUNK)
-        quantize_wv(2)
+        gradient_late(nc.gpsimd, 2, LOW, "weight_late")
+        gradient_late(nc.gpsimd, 2, HIGH)
+        gradient_late(nc.gpsimd, 3, LOW)
+        gradient_late(nc.vector, 3, HIGH)
+        early1 = second_product(1, 0, HALF, "bank1", "inv3_0")
+        interleave_wv(2, wv_last[:, :, :P], "r3_0")
+        interleave_wv(3, wv_last[:, :, P:], "inv3_64")
+        for c in (2, 3):
+            quantize_g(c, LOW)
+            quantize_g(c, HIGH)
         scatter(1, 0, early1)
-        quantize_wv(3)
+        quantize_wv(2, "wv_codes2")
+        quantize_wv(3, "wv_codes3")
         late = [second_product(b, HALF, HALF, "bank%d" % (2 + b)) for b in range(2)]
         full = [second_product(b, HALF, N, "bank%d" % (4 + b)) for b in range(2, BLOCKS)]
         for b in range(2):

@@ -45,9 +45,8 @@ def tile_attend_gml_cau_kernel(tc, xT, wd, wv, y, cw, rw, offs, out):
         wv_first = tiles("wv_first", 2, [P, PACK, P], F32)
         wv_last = sb.tile([P, PACK, 2 * P], F32, name="wv_last", align_bytes=64)
         x_plane = tiles("x_plane", PACK, [P, T], F32)
-        y_first = tiles("y_first", 2, [P, 2, CHUNK], F32)
-        y_second = sb.tile([P, PACK, CHUNK], F32, name="y_second", align_bytes=64)
-        y_late = tiles("y_late", 2, [P, PACK, CHUNK], F32)
+        y_pair = tiles("y_pair", 2, [P, 2, HALF], F32)
+        y_late = sb.tile([P, PACK, HALF], F32, name="y_late", align_bytes=64)
 
         x_rows = xT.rearrange("(p j) c -> p j c", j=PACK)
         wd_rows = wd.rearrange("(p j) v -> p j v", j=PACK)
@@ -61,13 +60,11 @@ def tile_attend_gml_cau_kernel(tc, xT, wd, wv, y, cw, rw, offs, out):
             nc.sync.dma_start(x_plane[j][:], x_rows[:, j, :])
         for h in range(2):
             nc.sync.dma_start(wd_raw[h][:], wd_rows[:, :, h * (V // 2) : (h + 1) * (V // 2)])
+        nc.sync.dma_start(wv_first[0][:], wv_rows[:, :, :P])
         for k in range(2):
-            nc.sync.dma_start(wv_first[k][:], wv_rows[:, :, k * P : (k + 1) * P])
-        for k in range(2):
-            nc.sync.dma_start(y_first[k][:], y_rows[:, 2 * k : 2 * k + 2, :CHUNK])
-        nc.sync.dma_start(y_second[:], y_rows[:, :, CHUNK:HALF])
-        for c in range(2):
-            nc.sync.dma_start(y_late[c][:], y_rows[:, :, HALF + c * CHUNK : HALF + (c + 1) * CHUNK])
+            nc.sync.dma_start(y_pair[k][:], y_rows[:, 2 * k : 2 * k + 2, :HALF])
+        nc.sync.dma_start(y_late[:], y_rows[:, :, HALF:])
+        nc.sync.dma_start(wv_first[1][:], wv_rows[:, :, P : 2 * P])
         nc.sync.dma_start(wv_last[:], wv_rows[:, :, 2 * P :])
 
         warm = sb.tile([P, 1], F32, name="warm")
@@ -164,6 +161,7 @@ def tile_attend_gml_cau_kernel(tc, xT, wd, wv, y, cw, rw, offs, out):
         q_late = sb.tile([P, HALF, PACK], F32, name="q_late", align_bytes=64)
         u, r, inv = {}, {}, {}
         g_bf = {}
+        g_late = sb.tile([P, HALF, PACK], BF16, name="g_late", align_bytes=64)
         wv_bf, wv_codes, wv_scales = {}, {}, {}
         for c in range(2):
             inv[c] = sb.tile([P, PACK, CHUNK], F32, name="inv%d" % c, tag="inv%d" % c, align_bytes=64)
@@ -189,18 +187,25 @@ def tile_attend_gml_cau_kernel(tc, xT, wd, wv, y, cw, rw, offs, out):
             nc.vector.tensor_tensor(
                 q_late[:, part(c), :].rearrange("p (n e) t -> p n t e", e=4),
                 a_bank[c][:].rearrange("p t (n e) -> p n t e", e=4),
-                y_late[c - 2][:].rearrange("p t (n e) -> p n t e", e=4),
+                y_late[:, :, part(c)].rearrange("p t (n e) -> p n t e", e=4),
                 ALU.subtract,
             )
 
         def residual_pair(c, k):
-            targets = y_second[:, 2 * k : 2 * k + 2, :] if c else y_first[k][:]
+            targets = y_pair[k][:, :, part(c)]
             slots = slice(2 * k, 2 * k + 2)
             nc.vector.tensor_tensor(q[:, slots, part(c)], a_pair[c, k][:], targets, ALU.subtract)
 
         def square_pair(c, k):
             slots = slice(2 * k, 2 * k + 2)
             nc.scalar.activation(u[c][:, slots, :], q[:, slots, part(c)], ACT.Square)
+
+        def root_pair(k):
+            r[0, k] = sb.tile([P, 2, CHUNK], F32, name="r0_%d" % k, tag="r0_%d" % k, align_bytes=64)
+            nc.scalar.activation(r[0, k][:], u[0][:, 2 * k : 2 * k + 2, :], ACT.Abs_reciprocal_sqrt, bias=1.0)
+
+        def inverse_pair(k):
+            nc.scalar.activation(inv[0][:, 2 * k : 2 * k + 2, :], r[0, k][:], ACT.Square)
 
         def root(c, piece):
             tag = "r%d_%d" % (c, piece.start)
@@ -223,27 +228,17 @@ def tile_attend_gml_cau_kernel(tc, xT, wd, wv, y, cw, rw, offs, out):
             inv[c, piece.start] = sb.tile([P, piece.stop - piece.start, PACK], F32, name=tag, tag=tag, align_bytes=64)
             nc.scalar.activation(inv[c, piece.start][:], r[c, piece.start][:], ACT.Square)
 
-        def numerator_pair(c, k):
-            slots = slice(2 * k, 2 * k + 2)
-            nc.gpsimd.tensor_tensor(num[c][:, slots, :], q[:, slots, part(c)], weight_rows[:, slots, part(c)], ALU.mult)
-
-        def numerator_late(c, tag):
-            num[c] = sb.tile([P, CHUNK, PACK], F32, name="num%d" % c, tag=tag, align_bytes=64)
-            nc.vector.tensor_tensor(num[c][:], q_late[:, part(c), :], weight_late[:, part(c), :], ALU.mult)
-
         def gradient(c, piece=WHOLE):
             g_bf[c, piece.start] = sb.tile([P, piece.stop - piece.start, PACK], BF16, name="g%d_%d" % (c, piece.start), align_bytes=64)
             nc.vector.tensor_tensor(
                 g_bf[c, piece.start][:].rearrange("p (n e) t -> p n t e", e=2),
-                num[c][:, :, piece].rearrange("p t (n e) -> p n t e", e=2),
+                num[:, :, part(c, piece)].rearrange("p t (n e) -> p n t e", e=2),
                 inv[c][:, :, piece].rearrange("p t (n e) -> p n t e", e=2),
                 ALU.mult,
             )
 
-        def gradient_late(engine, c, piece, tag=None):
-            name = "g%d_%d" % (c, piece.start)
-            g_bf[c, piece.start] = sb.tile([P, piece.stop - piece.start, PACK], BF16, name=name, tag=tag or name, align_bytes=64)
-            engine.tensor_tensor(g_bf[c, piece.start][:], num[c][:, piece, :], inv[c, piece.start][:], ALU.mult)
+        def gradient_late(engine, c, piece):
+            engine.tensor_tensor(g_late[:, part(c, piece), :], num_late[:, part(c, piece), :], inv[c, piece.start][:], ALU.mult)
 
         def quantize_g(c, piece=WHOLE):
             cols = slice(HALF + c * CHUNK + piece.start, HALF + c * CHUNK + piece.stop)
@@ -251,6 +246,14 @@ def tile_attend_gml_cau_kernel(tc, xT, wd, wv, y, cw, rw, offs, out):
                 out=g_codes[:, cols].bitcast(E5M2),
                 scales=g_scales[:, cols],
                 in_=g_bf[c, piece.start][:].rearrange("p i t -> p (i t)"),
+            )
+
+        def quantize_g_late(c, piece):
+            cols = slice(HALF + c * CHUNK + piece.start, HALF + c * CHUNK + piece.stop)
+            nc.vector.quantize_mx(
+                out=g_codes[:, cols].bitcast(E5M2),
+                scales=g_scales[:, cols],
+                in_=g_late[:, part(c, piece), :].rearrange("p i t -> p (i t)"),
             )
 
         def interleave_wv(b, source, tag=None):
@@ -294,40 +297,38 @@ def tile_attend_gml_cau_kernel(tc, xT, wd, wv, y, cw, rw, offs, out):
             for cols in (slice(0, T // 2), slice(T // 2, T)):
                 nc.sync.dma_start(out[b * P : (b + 1) * P, cols], window[b][:, cols])
 
-        num = {c: sb.tile([P, PACK, CHUNK], F32, name="num%d" % c, tag="num%d" % c, align_bytes=64) for c in range(2)}
+        num = sb.tile([P, PACK, HALF], F32, name="num", tag="num", align_bytes=64)
         interleave_wv(0, wv_first[0][:])
-        interleave_wv(1, wv_first[1][:])
-        for c in range(CHUNKS):
-            for k in range(2):
-                first_product(c, k)
-        for c in range(2):
-            for k in range(2):
+        for c, k in ((0, 0), (1, 0), (0, 1), (1, 1), (2, 0), (2, 1), (3, 0), (3, 1)):
+            first_product(c, k)
+        for k in range(2):
+            for c in range(2):
                 residual_pair(c, k)
-                numerator_pair(c, k)
-                square_pair(c, k)
-        root(0, LOW)
-        root(0, HIGH)
+        square_pair(0, 0)
+        square_pair(1, 0)
+        root_pair(0)
+        square_pair(0, 1)
+        inverse_pair(0)
+        square_pair(1, 1)
+        root_pair(1)
         root(1, LOW)
-        inverse(0, LOW)
+        inverse_pair(1)
         root(1, HIGH)
-        inverse(0, HIGH)
         inverse(1, LOW)
         inverse(1, HIGH)
+        interleave_wv(1, wv_first[1][:], "r1_0")
+        nc.vector.tensor_tensor(num[:], q[:], weight_rows[:, :, :HALF], ALU.mult)
         residual_late(2)
         residual_late(3)
-        numerator_late(2, "num2")
-        gradient(0, LOW)
-        quantize_wv(0, "r0_0")
-        quantize_g(0, LOW)
-        gradient(0, HIGH)
+        gradient(0)
         gradient(1, LOW)
         gradient(1, HIGH)
-        quantize_g(0, HIGH)
+        quantize_wv(0, "r0_1")
+        quantize_g(0)
         quantize_g(1, LOW)
         quantize_g(1, HIGH)
-        quantize_wv(1, "inv1")
-        u[2] = sb.tile([P, CHUNK, PACK], F32, name="u2", tag="r1_0", align_bytes=64)
-        u[3] = sb.tile([P, CHUNK, PACK], F32, name="u3", tag="r1_64", align_bytes=64)
+        u_late = sb.tile([P, HALF, PACK], F32, name="u_late", tag="r1_64", align_bytes=64)
+        u[2], u[3] = u_late[:, :CHUNK, :], u_late[:, CHUNK:, :]
         square_late(2, LOW)
         square_late(2, HIGH)
         root_late(2, LOW)
@@ -339,21 +340,23 @@ def tile_attend_gml_cau_kernel(tc, xT, wd, wv, y, cw, rw, offs, out):
         root_late(3, HIGH)
         inverse_late(3, LOW)
         inverse_late(3, HIGH)
-        numerator_late(3, "num1")
+        num_late = sb.tile([P, HALF, PACK], F32, name="num_late", tag="num", align_bytes=64)
+        nc.vector.tensor_tensor(num_late[:], q_late[:], weight_late[:], ALU.mult)
         early0 = second_product(0, 0, HALF, "bank0", copy=nc.vector.tensor_copy)
+        quantize_wv(1, "wv_codes1")
         scatter(0, 0, early0)
-        gradient_late(nc.gpsimd, 2, LOW, "weight_late")
+        gradient_late(nc.gpsimd, 2, LOW)
         gradient_late(nc.gpsimd, 2, HIGH)
         gradient_late(nc.gpsimd, 3, LOW)
         gradient_late(nc.vector, 3, HIGH)
         early1 = second_product(1, 0, HALF, "bank1", "inv3_0")
         interleave_wv(2, wv_last[:, :, :P], "r3_0")
         interleave_wv(3, wv_last[:, :, P:], "inv3_64")
-        for c in (2, 3):
-            quantize_g(c, LOW)
-            quantize_g(c, HIGH)
-        scatter(1, 0, early1)
+        quantize_g_late(2, WHOLE)
+        quantize_g_late(3, LOW)
+        quantize_g_late(3, HIGH)
         quantize_wv(2, "wv_codes2")
+        scatter(1, 0, early1)
         quantize_wv(3, "wv_codes3")
         late = [second_product(b, HALF, HALF, "bank%d" % (2 + b)) for b in range(2)]
         full = [second_product(b, HALF, N, "bank%d" % (4 + b)) for b in range(2, BLOCKS)]

@@ -99,9 +99,6 @@ def tile_attend_gml_cau_kernel(tc, xT, wd, wv, y, cw, rw, offs, out):
                 scale=weights_col[:, t, 0:1],
             )
 
-        weight_late = sb.tile([P, HALF, PACK], F32, name="weight_late", tag="weight_late", align_bytes=64)
-        nc.gpsimd.tensor_copy(weight_late[:], weight_rows[:, :, HALF:].rearrange("p t i -> p i t"))
-
         x_bf = tiles("x_bf", 2, [P, HALF, PACK], BF16)
         x_codes = {}
         x_scales = tiles("x_scales", 2, [P, HALF], U8)
@@ -158,7 +155,7 @@ def tile_attend_gml_cau_kernel(tc, xT, wd, wv, y, cw, rw, offs, out):
         for c in (2, 3):
             a_pair[c, 0], a_pair[c, 1] = a_bank[c][:, :2, :], a_bank[c][:, 2:, :]
         q = sb.tile([P, PACK, HALF], F32, name="q", align_bytes=64)
-        q_late = sb.tile([P, HALF, PACK], F32, name="q_late", align_bytes=64)
+        q_late = sb.tile([P, PACK, HALF], F32, name="q_late", align_bytes=64)
         u, r, inv = {}, {}, {}
         g_bf = {}
         g_late = sb.tile([P, HALF, PACK], BF16, name="g_late", align_bytes=64)
@@ -184,12 +181,7 @@ def tile_attend_gml_cau_kernel(tc, xT, wd, wv, y, cw, rw, offs, out):
                 )
 
         def residual_late(c):
-            nc.vector.tensor_tensor(
-                q_late[:, part(c), :].rearrange("p (n e) t -> p n t e", e=4),
-                a_bank[c][:].rearrange("p t (n e) -> p n t e", e=4),
-                y_late[:, :, part(c)].rearrange("p t (n e) -> p n t e", e=4),
-                ALU.subtract,
-            )
+            nc.vector.tensor_tensor(q_late[:, :, part(c)], a_bank[c][:], y_late[:, :, part(c)], ALU.subtract)
 
         def residual_pair(c, k):
             targets = y_pair[k][:, :, part(c)]
@@ -216,7 +208,11 @@ def tile_attend_gml_cau_kernel(tc, xT, wd, wv, y, cw, rw, offs, out):
             nc.scalar.activation(inv[c][:, :, piece], r[c, piece.start][:], ACT.Square)
 
         def square_late(c, piece):
-            nc.scalar.activation(u[c][:, piece, :], q_late[:, part(c, piece), :], ACT.Square)
+            nc.scalar.activation(
+                u[c][:, piece, :].rearrange("p (n e) t -> p n t e", e=2),
+                q_late[:, :, part(c, piece)].rearrange("p t (n e) -> p n t e", e=2),
+                ACT.Square,
+            )
 
         def root_late(c, piece):
             tag = "r%d_%d" % (c, piece.start)
@@ -341,7 +337,12 @@ def tile_attend_gml_cau_kernel(tc, xT, wd, wv, y, cw, rw, offs, out):
         inverse_late(3, LOW)
         inverse_late(3, HIGH)
         num_late = sb.tile([P, HALF, PACK], F32, name="num_late", tag="num", align_bytes=64)
-        nc.vector.tensor_tensor(num_late[:], q_late[:], weight_late[:], ALU.mult)
+        nc.vector.tensor_tensor(
+            num_late[:].rearrange("p (n e) t -> p n t e", e=2),
+            q_late[:].rearrange("p t (n e) -> p n t e", e=2),
+            weight_rows[:, :, HALF:].rearrange("p t (n e) -> p n t e", e=2),
+            ALU.mult,
+        )
         early0 = second_product(0, 0, HALF, "bank0", copy=nc.vector.tensor_copy)
         quantize_wv(1, "wv_codes1")
         scatter(0, 0, early0)

@@ -77,10 +77,8 @@ def tile_attend_gml_cau_kernel(tc, xT, wd, wv, y, cw, rw, offs, out):
         make_identity(nc, identity[:])
         for b in range(BLOCKS):
             (nc.vector if b < 2 else nc.gpsimd).memset(window[b][:], 0.0)
-        g_codes = sb.tile([P, HALF + N], U32, name="g_codes", align_bytes=64)
-        g_scales = sb.tile([P, HALF + N], U8, name="g_scales", align_bytes=64)
-        nc.vector.memset(g_codes[:, :HALF], 0)
-        nc.vector.memset(g_scales[:, :HALF].bitcast(U32), 0)
+        g_codes = sb.tile([P, N], U32, name="g_codes", align_bytes=64)
+        g_scales = sb.tile([P, N], U8, name="g_scales", align_bytes=64)
 
         turned = ps.tile([P, PACK, P], F32, name="turned", tag="bank6")
         for j in range(PACK):
@@ -237,7 +235,7 @@ def tile_attend_gml_cau_kernel(tc, xT, wd, wv, y, cw, rw, offs, out):
             engine.tensor_tensor(g_late[:, part(c, piece), :], num_late[:, part(c, piece), :], inv[c, piece.start][:], ALU.mult)
 
         def quantize_g(c, piece=WHOLE):
-            cols = slice(HALF + c * CHUNK + piece.start, HALF + c * CHUNK + piece.stop)
+            cols = slice(c * CHUNK + piece.start, c * CHUNK + piece.stop)
             nc.vector.quantize_mx(
                 out=g_codes[:, cols].bitcast(E5M2),
                 scales=g_scales[:, cols],
@@ -245,7 +243,7 @@ def tile_attend_gml_cau_kernel(tc, xT, wd, wv, y, cw, rw, offs, out):
             )
 
         def quantize_g_late(c, piece):
-            cols = slice(HALF + c * CHUNK + piece.start, HALF + c * CHUNK + piece.stop)
+            cols = slice(c * CHUNK + piece.start, c * CHUNK + piece.stop)
             nc.vector.quantize_mx(
                 out=g_codes[:, cols].bitcast(E5M2),
                 scales=g_scales[:, cols],
@@ -269,9 +267,9 @@ def tile_attend_gml_cau_kernel(tc, xT, wd, wv, y, cw, rw, offs, out):
                 out=wv_codes[b][:].bitcast(E4M3), scales=wv_scales[b][:], in_=wv_bf[b][:].rearrange("p d j -> p (d j)")
             )
 
-        def second_product(b, first_col, keep, tag, slot=None, copy=nc.scalar.copy):
-            bank = ps.tile([P, N], F32, name="dx_" + tag, tag=tag)
-            cols = slice(first_col, first_col + N)
+        def second_product(b, cols, tag, copy, slot=None):
+            count = cols.stop - cols.start
+            bank = ps.tile([P, count], F32, name="dx_" + tag, tag=tag)
             nc.tensor.matmul_mx(
                 out=bank[:],
                 lhsT=wv_codes[b][:].bitcast(E4M3),
@@ -281,17 +279,22 @@ def tile_attend_gml_cau_kernel(tc, xT, wd, wv, y, cw, rw, offs, out):
                 start=True,
                 stop=True,
             )
-            dx = sb.tile([P, keep], F32, name="dx_sb_" + tag, tag=slot or "dx_" + tag, align_bytes=64)
-            copy(dx[:], bank[:, N - keep :])
+            dx = sb.tile([P, count], F32, name="dx_sb_" + tag, tag=slot or "dx_" + tag, align_bytes=64)
+            copy(dx[:], bank[:])
             return dx
 
-        def scatter(b, first, dx):
-            count = dx.shape[1]
-            nc.vector.tensor_copy(window[b][:].indirect(offsets[:, first // 16 : (first + count) // 16]), dx[:])
+        def scatter_on_vector(b, first, values):
+            count = values.shape[1]
+            nc.vector.tensor_copy(window[b][:].indirect(offsets[:, first // 16 : (first + count) // 16]), values)
+
+        def scatter_on_scalar(b, first, values):
+            count = values.shape[1]
+            nc.scalar.activation(window[b][:].indirect(offsets[:, first // 16 : (first + count) // 16]), values, ACT.Copy)
 
         def store(b):
+            queue = nc.scalar if b % 2 else nc.sync
             for cols in (slice(0, T // 2), slice(T // 2, T)):
-                nc.sync.dma_start(out[b * P : (b + 1) * P, cols], window[b][:, cols])
+                queue.dma_start(out[b * P : (b + 1) * P, cols], window[b][:, cols])
 
         num = sb.tile([P, PACK, HALF], F32, name="num", tag="num", align_bytes=64)
         interleave_wv(0, wv_first[0][:])
@@ -343,27 +346,35 @@ def tile_attend_gml_cau_kernel(tc, xT, wd, wv, y, cw, rw, offs, out):
             weight_rows[:, :, HALF:].rearrange("p t (n e) -> p n t e", e=2),
             ALU.mult,
         )
-        early0 = second_product(0, 0, HALF, "bank0", copy=nc.vector.tensor_copy)
+        early = second_product(0, slice(0, HALF), "bank0", nc.vector.tensor_copy)
         quantize_wv(1, "wv_codes1")
-        scatter(0, 0, early0)
+        scatter_on_vector(0, 0, early[:])
         gradient_late(nc.gpsimd, 2, LOW)
         gradient_late(nc.gpsimd, 2, HIGH)
         gradient_late(nc.gpsimd, 3, LOW)
         gradient_late(nc.vector, 3, HIGH)
-        early1 = second_product(1, 0, HALF, "bank1", "inv3_0")
         interleave_wv(2, wv_last[:, :, :P], "r3_0")
-        interleave_wv(3, wv_last[:, :, P:], "inv3_64")
+        first_half = second_product(1, slice(0, HALF), "bank5", nc.scalar.copy, "r3_64")
+        scatter_on_scalar(1, 0, first_half[:])
+        interleave_wv(3, wv_last[:, :, P:], "inv3_0")
         quantize_g_late(2, WHOLE)
         quantize_g_late(3, LOW)
         quantize_g_late(3, HIGH)
         quantize_wv(2, "wv_codes2")
-        scatter(1, 0, early1)
+        late = second_product(0, slice(HALF, N), "bank1", nc.vector.tensor_copy)
+        scatter_on_vector(0, HALF, late[:])
+        store(0)
+        second_half = second_product(1, slice(HALF, N), "bank2", nc.scalar.copy)
+        scatter_on_scalar(1, HALF, second_half[:])
+        store(1)
         quantize_wv(3, "wv_codes3")
-        late = [second_product(b, HALF, HALF, "bank%d" % (2 + b)) for b in range(2)]
-        full = [second_product(b, HALF, N, "bank%d" % (4 + b)) for b in range(2, BLOCKS)]
-        for b in range(2):
-            scatter(b, HALF, late[b])
-            store(b)
-        for b in range(2, BLOCKS):
-            scatter(b, 0, full[b - 2])
-            store(b)
+        dx = second_product(2, slice(0, N), "bank3", nc.vector.tensor_copy)
+        scatter_on_vector(2, 0, dx[:])
+        store(2)
+        halves = [
+            second_product(3, slice(0, HALF), "bank4", nc.scalar.copy, "dx_bank2"),
+            second_product(3, slice(HALF, N), "bank6", nc.scalar.copy, "r3_64"),
+        ]
+        for h in range(2):
+            scatter_on_scalar(3, h * HALF, halves[h][:])
+        store(3)

@@ -77,6 +77,8 @@ def tile_attend_gml_cau_kernel(tc, xT, wd, wv, y, cw, rw, offs, out):
         make_identity(nc, identity[:])
         for b in range(BLOCKS):
             (nc.vector if b < 2 else nc.gpsimd).memset(window[b][:], 0.0)
+        zeros = sb.tile([P, CHUNK], F32, name="zeros", align_bytes=64)
+        nc.vector.memset(zeros[:], 0.0)
         g_codes = sb.tile([P, N], U32, name="g_codes", align_bytes=64)
         g_scales = sb.tile([P, N], U8, name="g_scales", align_bytes=64)
 
@@ -287,14 +289,18 @@ def tile_attend_gml_cau_kernel(tc, xT, wd, wv, y, cw, rw, offs, out):
             count = values.shape[1]
             nc.vector.tensor_copy(window[b][:].indirect(offsets[:, first // 16 : (first + count) // 16]), values)
 
+        def scatter_chunk(b, first, values):
+            nc.vector.tensor_tensor(
+                window[b][:].indirect(offsets[:, first // 16 : (first + CHUNK) // 16]), values, zeros[:], ALU.add
+            )
+
         def scatter_on_scalar(b, first, values):
             count = values.shape[1]
             nc.scalar.activation(window[b][:].indirect(offsets[:, first // 16 : (first + count) // 16]), values, ACT.Copy)
 
         def store(b):
-            queue = nc.scalar if b % 2 else nc.sync
-            for cols in (slice(0, T // 2), slice(T // 2, T)):
-                queue.dma_start(out[b * P : (b + 1) * P, cols], window[b][:, cols])
+            for cols in (slice(0, T // 2), slice(T // 2, T)) if b == BLOCKS - 1 else (slice(0, T),):
+                nc.sync.dma_start(out[b * P : (b + 1) * P, cols], window[b][:, cols])
 
         num = sb.tile([P, PACK, HALF], F32, name="num", tag="num", align_bytes=64)
         interleave_wv(0, wv_first[0][:])
@@ -352,29 +358,28 @@ def tile_attend_gml_cau_kernel(tc, xT, wd, wv, y, cw, rw, offs, out):
         gradient_late(nc.gpsimd, 2, LOW)
         gradient_late(nc.gpsimd, 2, HIGH)
         gradient_late(nc.gpsimd, 3, LOW)
-        gradient_late(nc.vector, 3, HIGH)
-        interleave_wv(2, wv_last[:, :, :P], "r3_0")
-        first_half = second_product(1, slice(0, HALF), "bank5", nc.scalar.copy, "r3_64")
-        scatter_on_scalar(1, 0, first_half[:])
-        interleave_wv(3, wv_last[:, :, P:], "inv3_0")
         quantize_g_late(2, WHOLE)
+        gradient_late(nc.vector, 3, HIGH)
         quantize_g_late(3, LOW)
         quantize_g_late(3, HIGH)
+        first_half = second_product(1, slice(0, HALF), "bank5", nc.scalar.copy, "r3_64")
+        interleave_wv(2, wv_last[:, :, :P], "r3_0")
+        third = second_product(0, slice(2 * CHUNK, 3 * CHUNK), "bank3", nc.scalar.copy)
+        scatter_on_scalar(1, 0, first_half[:])
+        interleave_wv(3, wv_last[:, :, P:], "r3_64")
         quantize_wv(2, "wv_codes2")
-        late = second_product(0, slice(HALF, N), "bank1", nc.vector.tensor_copy)
-        scatter_on_vector(0, HALF, late[:])
+        scatter_chunk(0, 2 * CHUNK, third[:])
+        last = second_product(0, slice(3 * CHUNK, N), "bank1", nc.vector.tensor_copy)
+        scatter_chunk(0, 3 * CHUNK, last[:])
         store(0)
-        second_half = second_product(1, slice(HALF, N), "bank2", nc.scalar.copy)
+        second_half = second_product(1, slice(HALF, N), "bank5", nc.scalar.copy, "dx_w1b")
         scatter_on_scalar(1, HALF, second_half[:])
         store(1)
+        dx = second_product(2, slice(0, N), "bank1", nc.vector.tensor_copy, "dx_w2")
         quantize_wv(3, "wv_codes3")
-        dx = second_product(2, slice(0, N), "bank3", nc.vector.tensor_copy)
         scatter_on_vector(2, 0, dx[:])
         store(2)
-        halves = [
-            second_product(3, slice(0, HALF), "bank4", nc.scalar.copy, "dx_bank2"),
-            second_product(3, slice(HALF, N), "bank6", nc.scalar.copy, "r3_64"),
-        ]
-        for h in range(2):
-            scatter_on_scalar(3, h * HALF, halves[h][:])
+        dx = second_product(3, slice(0, N), "bank5", nc.scalar.copy, "dx_w3")
+        for first in (0, HALF):
+            scatter_on_scalar(3, first, dx[:, first : first + HALF])
         store(3)

@@ -34,6 +34,7 @@ def tile_attend_gml_cau_kernel(tc, xT, wd, wv, y, cw, rw, offs, out):
         def tiles(name, count, shape, dtype):
             return [sb.tile(shape, dtype, name="%s%d" % (name, i), align_bytes=64) for i in range(count)]
 
+        vector_windows = tiles("vector_window", 2, [P, T], F32)
         offsets = sb.tile([P, N // 16], U16, name="offsets")
         weights_row = sb.tile([P, N], F32, name="weights_row")
         nc.gpsimd.memset(weights_row[:], 0.0)
@@ -72,7 +73,9 @@ def tile_attend_gml_cau_kernel(tc, xT, wd, wv, y, cw, rw, offs, out):
         nc.vector.memset(warm[:], 0.0)
         nc.scalar.activation(warm_out[:], warm[:], ACT.Abs_reciprocal_sqrt, bias=1.0)
 
-        window = tiles("window", BLOCKS, [P, T], F32)
+        far = ctx.enter_context(tc.tile_pool(name="far", bufs=1))
+        scalar_windows = [far.tile([P, T], F32, name="scalar_window%d" % i, align_bytes=64) for i in range(2)]
+        window = [vector_windows[0], scalar_windows[0], vector_windows[1], scalar_windows[1]]
         identity = sb.tile([P, P], F32, name="identity")
         make_identity(nc, identity[:])
         for b in range(BLOCKS):

@@ -22,6 +22,7 @@ HALF = N // 2
 CHUNK = 128
 CHUNKS = N // CHUNK
 BLOCKS = D // P
+DMA_ALIGN = 256
 WHOLE, LOW, HIGH = slice(0, CHUNK), slice(0, CHUNK // 2), slice(CHUNK // 2, CHUNK)
 
 
@@ -31,23 +32,23 @@ def tile_attend_gml_cau_kernel(tc, xT, wd, wv, y, cw, rw, offs, out):
         sb = ctx.enter_context(tc.tile_pool(name="sb", bufs=1))
         ps = ctx.enter_context(tc.psum_pool(name="ps", bufs=1))
 
-        def tiles(name, count, shape, dtype):
-            return [sb.tile(shape, dtype, name="%s%d" % (name, i), align_bytes=64) for i in range(count)]
+        def tiles(name, count, shape, dtype, align=64):
+            return [sb.tile(shape, dtype, name="%s%d" % (name, i), align_bytes=align) for i in range(count)]
 
-        vector_windows = tiles("vector_window", 2, [P, T], F32)
+        vector_windows = tiles("vector_window", 2, [P, T], F32, DMA_ALIGN)
         offsets = sb.tile([P, N // 16], U16, name="offsets")
-        weights_row = sb.tile([P, N], F32, name="weights_row")
+        weights_row = sb.tile([P, N], F32, name="weights_row", align_bytes=DMA_ALIGN)
         nc.gpsimd.memset(weights_row[:], 0.0)
         reuse = ctx.enter_context(tc.tile_pool(name="reuse", bufs=1))
         wd_raw = [
-            sb.tile([P, PACK, V // 2], F32, name="wd_raw0", align_bytes=64),
-            reuse.tile([P, PACK, V // 2], F32, name="wd_raw1", align_bytes=64, offset=0),
+            sb.tile([P, PACK, V // 2], F32, name="wd_raw0", align_bytes=DMA_ALIGN),
+            reuse.tile([P, PACK, V // 2], F32, name="wd_raw1", align_bytes=DMA_ALIGN, offset=0),
         ]
-        wv_first = tiles("wv_first", 2, [P, PACK, P], F32)
-        wv_last = sb.tile([P, PACK, 2 * P], F32, name="wv_last", align_bytes=64)
-        x_plane = tiles("x_plane", PACK, [P, T], F32)
-        y_pair = tiles("y_pair", 2, [P, 2, HALF], F32)
-        y_late = sb.tile([P, PACK, HALF], F32, name="y_late", align_bytes=64)
+        wv_first = tiles("wv_first", 2, [P, PACK, P], F32, DMA_ALIGN)
+        wv_last = sb.tile([P, PACK, 2 * P], F32, name="wv_last", align_bytes=DMA_ALIGN)
+        x_plane = tiles("x_plane", PACK, [P, T], F32, DMA_ALIGN)
+        y_pair = tiles("y_pair", 2, [P, 2, HALF], F32, DMA_ALIGN)
+        y_late = sb.tile([P, PACK, HALF], F32, name="y_late", align_bytes=DMA_ALIGN)
 
         x_rows = xT.rearrange("(p j) c -> p j c", j=PACK)
         wd_rows = wd.rearrange("(p j) v -> p j v", j=PACK)
@@ -74,7 +75,7 @@ def tile_attend_gml_cau_kernel(tc, xT, wd, wv, y, cw, rw, offs, out):
         nc.scalar.activation(warm_out[:], warm[:], ACT.Abs_reciprocal_sqrt, bias=1.0)
 
         far = ctx.enter_context(tc.tile_pool(name="far", bufs=1))
-        scalar_windows = [far.tile([P, T], F32, name="scalar_window%d" % i, align_bytes=64) for i in range(2)]
+        scalar_windows = [far.tile([P, T], F32, name="scalar_window%d" % i, align_bytes=DMA_ALIGN) for i in range(2)]
         window = [vector_windows[0], scalar_windows[0], vector_windows[1], scalar_windows[1]]
         identity = sb.tile([P, P], F32, name="identity")
         make_identity(nc, identity[:])

@@ -303,7 +303,7 @@ def tile_attend_gml_cau_kernel(tc, xT, wd, wv, y, cw, rw, offs, out):
             nc.scalar.activation(window[b][:].indirect(offsets[:, first // 16 : (first + count) // 16]), values, ACT.Copy)
 
         def store(b):
-            for cols in (slice(0, T // 2), slice(T // 2, T)) if b == BLOCKS - 1 else (slice(0, T),):
+            for cols in (slice(0, T // 2), slice(T // 2, T)):
                 nc.sync.dma_start(out[b * P : (b + 1) * P, cols], window[b][:, cols])
 
         num = sb.tile([P, PACK, HALF], F32, name="num", tag="num", align_bytes=64)

@@ -39,6 +39,13 @@ def tile_attend_gml_cau_kernel(tc, xT, wd, wv, y, cw, rw, offs, out):
         offsets = sb.tile([P, N // 16], U16, name="offsets")
         weights_row = sb.tile([P, N], F32, name="weights_row", align_bytes=DMA_ALIGN)
         nc.gpsimd.memset(weights_row[:], 0.0)
+        late_tiles = {}
+        for c in (2, 3):
+            for piece in (LOW, HIGH):
+                for kind in ("r", "inv"):
+                    tag = "%s%d_%d" % (kind, c, piece.start)
+                    late_tiles[tag] = sb.tile([P, CHUNK // 2, PACK], F32, name=tag, tag=tag, align_bytes=64)
+        late_tiles["r1_64"] = sb.tile([P, PACK, CHUNK // 2], F32, name="r1_64", tag="r1_64", align_bytes=64)
         reuse = ctx.enter_context(tc.tile_pool(name="reuse", bufs=1))
         wd_raw = [
             sb.tile([P, PACK, V // 2], F32, name="wd_raw0", align_bytes=DMA_ALIGN),
@@ -205,7 +212,9 @@ def tile_attend_gml_cau_kernel(tc, xT, wd, wv, y, cw, rw, offs, out):
 
         def root(c, piece):
             tag = "r%d_%d" % (c, piece.start)
-            r[c, piece.start] = sb.tile([P, PACK, piece.stop - piece.start], F32, name=tag, tag=tag, align_bytes=64)
+            if tag not in late_tiles:
+                late_tiles[tag] = sb.tile([P, PACK, CHUNK // 2], F32, name=tag, tag=tag, align_bytes=64)
+            r[c, piece.start] = late_tiles[tag]
             nc.scalar.activation(r[c, piece.start][:], u[c][:, :, piece], ACT.Abs_reciprocal_sqrt, bias=1.0)
 
         def inverse(c, piece):
@@ -220,12 +229,12 @@ def tile_attend_gml_cau_kernel(tc, xT, wd, wv, y, cw, rw, offs, out):
 
         def root_late(c, piece):
             tag = "r%d_%d" % (c, piece.start)
-            r[c, piece.start] = sb.tile([P, piece.stop - piece.start, PACK], F32, name=tag, tag=tag, align_bytes=64)
+            r[c, piece.start] = late_tiles[tag]
             nc.scalar.activation(r[c, piece.start][:], u[c][:, piece, :], ACT.Abs_reciprocal_sqrt, bias=1.0)
 
         def inverse_late(c, piece):
             tag = "inv%d_%d" % (c, piece.start)
-            inv[c, piece.start] = sb.tile([P, piece.stop - piece.start, PACK], F32, name=tag, tag=tag, align_bytes=64)
+            inv[c, piece.start] = late_tiles[tag]
             nc.scalar.activation(inv[c, piece.start][:], r[c, piece.start][:], ACT.Square)
 
         def gradient(c, piece=WHOLE):
@@ -376,14 +385,14 @@ def tile_attend_gml_cau_kernel(tc, xT, wd, wv, y, cw, rw, offs, out):
         last = second_product(0, slice(3 * CHUNK, N), "bank1", nc.vector.tensor_copy)
         scatter_chunk(0, 3 * CHUNK, last[:])
         store(0)
-        second_half = second_product(1, slice(HALF, N), "bank5", nc.scalar.copy, "dx_w1b")
+        second_half = second_product(1, slice(HALF, N), "bank5", nc.scalar.copy, "r2_0")
         scatter_on_scalar(1, HALF, second_half[:])
         store(1)
         dx = second_product(2, slice(0, N), "bank1", nc.vector.tensor_copy, "dx_w2")
         quantize_wv(3, "wv_codes3")
         scatter_on_vector(2, 0, dx[:])
         store(2)
-        dx = second_product(3, slice(0, N), "bank5", nc.scalar.copy, "dx_w3")
+        dx = second_product(3, slice(0, N), "bank5", nc.scalar.copy, "r1_64")
         for first in (0, HALF):
             scatter_on_scalar(3, first, dx[:, first : first + HALF])
         store(3)

@@ -35,24 +35,29 @@ def tile_attend_gml_cau_kernel(tc, xT, wd, wv, y, cw, rw, offs, out):
         def tiles(name, count, shape, dtype, align=64):
             return [sb.tile(shape, dtype, name="%s%d" % (name, i), align_bytes=align) for i in range(count)]
 
+        def tagged(name, tag, shape, dtype):
+            return sb.tile(shape, dtype, name=name, tag=tag, align_bytes=64)
+
+        def pairs_of_slot_major(ap):
+            return ap.rearrange("p t (n e) -> p n t e", e=2)
+
+        def pairs_of_position_major(ap):
+            return ap.rearrange("p (n e) t -> p n t e", e=2)
+
         vector_windows = tiles("vector_window", 2, [P, T], F32, DMA_ALIGN)
         offsets = sb.tile([P, N // 16], U16, name="offsets")
         weights_row = sb.tile([P, N], F32, name="weights_row", align_bytes=DMA_ALIGN)
         nc.gpsimd.memset(weights_row[:], 0.0)
-        late_tiles = {}
-        for c in (2, 3):
-            for piece in (LOW, HIGH):
-                for kind in ("r", "inv"):
-                    tag = "%s%d_%d" % (kind, c, piece.start)
-                    late_tiles[tag] = sb.tile([P, CHUNK // 2, PACK], F32, name=tag, tag=tag, align_bytes=64)
-        late_tiles["r1_64"] = sb.tile([P, PACK, CHUNK // 2], F32, name="r1_64", tag="r1_64", align_bytes=64)
-        reuse = ctx.enter_context(tc.tile_pool(name="reuse", bufs=1))
-        wd_raw = [
-            sb.tile([P, PACK, V // 2], F32, name="wd_raw0", align_bytes=DMA_ALIGN),
-            reuse.tile([P, PACK, V // 2], F32, name="wd_raw1", align_bytes=DMA_ALIGN, offset=0),
-        ]
-        wv_first = tiles("wv_first", 2, [P, PACK, P], F32, DMA_ALIGN)
-        wv_last = sb.tile([P, PACK, 2 * P], F32, name="wv_last", align_bytes=DMA_ALIGN)
+        u_late = tagged("u_late", "u_late", [P, HALF, PACK], F32)
+        root2 = tagged("root2", "root2", [P, CHUNK, PACK], F32)
+        root3 = tagged("root3", "root3", [P, CHUNK, PACK], F32)
+        inv_late = [tagged("inv%d" % c, "inv%d" % c, [P, CHUNK, PACK], F32) for c in (2, 3)]
+        root_early = tagged("root_early", "root_early", [P, HALF, PACK], F32)
+        inv_early = tagged("inv_early", "inv_early", [P, HALF, PACK], F32)
+        wd_raw = tiles("wd_raw", 2, [P, PACK, V // 2], F32, DMA_ALIGN)
+        wv_first = sb.tile([P, PACK, P], F32, name="wv_first", align_bytes=DMA_ALIGN)
+        wv_middle = sb.tile([P, PACK, 2 * P], F32, name="wv_middle", align_bytes=DMA_ALIGN)
+        wv_last = sb.tile([P, PACK, P], F32, name="wv_last", align_bytes=DMA_ALIGN)
         x_plane = tiles("x_plane", PACK, [P, T], F32, DMA_ALIGN)
         y_pair = tiles("y_pair", 2, [P, 2, HALF], F32, DMA_ALIGN)
         y_late = sb.tile([P, PACK, HALF], F32, name="y_late", align_bytes=DMA_ALIGN)
@@ -69,12 +74,12 @@ def tile_attend_gml_cau_kernel(tc, xT, wd, wv, y, cw, rw, offs, out):
             nc.sync.dma_start(x_plane[j][:], x_rows[:, j, :])
         for h in range(2):
             nc.sync.dma_start(wd_raw[h][:], wd_rows[:, :, h * (V // 2) : (h + 1) * (V // 2)])
-        nc.sync.dma_start(wv_first[0][:], wv_rows[:, :, :P])
-        for k in range(2):
-            nc.sync.dma_start(y_pair[k][:], y_rows[:, 2 * k : 2 * k + 2, :HALF])
+        nc.sync.dma_start(y_pair[0][:], y_rows[:, :2, :HALF])
+        nc.sync.dma_start(y_pair[1][:], y_rows[:, 2:, :HALF])
+        nc.sync.dma_start(wv_first[:], wv_rows[:, :, :P])
+        nc.sync.dma_start(wv_middle[:], wv_rows[:, :, P : 3 * P])
         nc.sync.dma_start(y_late[:], y_rows[:, :, HALF:])
-        nc.sync.dma_start(wv_first[1][:], wv_rows[:, :, P : 2 * P])
-        nc.sync.dma_start(wv_last[:], wv_rows[:, :, 2 * P :])
+        nc.sync.dma_start(wv_last[:], wv_rows[:, :, 3 * P :])
 
         warm = sb.tile([P, 1], F32, name="warm")
         warm_out = sb.tile([P, 1], F32, name="warm_out")
@@ -88,203 +93,155 @@ def tile_attend_gml_cau_kernel(tc, xT, wd, wv, y, cw, rw, offs, out):
         make_identity(nc, identity[:])
         for b in range(BLOCKS):
             (nc.vector if b < 2 else nc.gpsimd).memset(window[b][:], 0.0)
-        zeros = sb.tile([P, CHUNK], F32, name="zeros", align_bytes=64)
-        nc.vector.memset(zeros[:], 0.0)
         g_codes = sb.tile([P, N], U32, name="g_codes", align_bytes=64)
         g_scales = sb.tile([P, N], U8, name="g_scales", align_bytes=64)
 
-        turned = ps.tile([P, PACK, P], F32, name="turned", tag="bank6")
-        for j in range(PACK):
-            nc.tensor.transpose(turned[:, j, :], weights_row[:, j::PACK], identity[:])
-        weights_col = sb.tile([P, PACK, 2], F32, name="weights_col")
-        nc.scalar.copy(weights_col[:], turned[:, :, :2])
-        rw_bank = ps.tile([P, PACK, P], F32, name="rw_bank", tag="bank7")
-        for j in range(PACK):
-            nc.tensor.transpose(rw_bank[:, j, :], weights_col[:, j, 1:2].to_broadcast([P, P]), identity[:])
-        weight_rows = sb.tile([P, PACK, N], F32, name="weight_rows")
+        cw_turned = ps.tile([P, PACK, P], F32, name="cw_turned", tag="bank0")
+        rw_turned = ps.tile([P, CHUNKS, P], F32, name="rw_turned", tag="bank1")
         for t in range(PACK):
-            nc.scalar.activation(
-                weight_rows[:, t, :].rearrange("p (k j) -> p k j", j=PACK),
-                rw_bank[:].rearrange("p j k -> p k j"),
-                ACT.Copy,
-                scale=weights_col[:, t, 0:1],
-            )
+            nc.tensor.transpose(cw_turned[:, t, :], weights_row[:, t::PACK], identity[:])
+        for c in range(CHUNKS):
+            nc.tensor.transpose(rw_turned[:, c, :], weights_row[:, c * CHUNK : (c + 1) * CHUNK], identity[:])
+        cw_col = sb.tile([P, PACK, 1], F32, name="cw_col")
+        rw_col = sb.tile([P, CHUNKS, 1], F32, name="rw_col")
+        nc.scalar.copy(cw_col[:], cw_turned[:, :, 0:1])
+        nc.scalar.copy(rw_col[:], rw_turned[:, :, 1:2])
+        cw_spread = ps.tile([P, PACK, P], F32, name="cw_spread", tag="bank2")
+        for t in range(PACK):
+            nc.tensor.transpose(cw_spread[:, t, :], cw_col[:, t, :].to_broadcast([P, P]), identity[:])
+        table_turned = tiles("table_turned", CHUNKS, [P, PACK, P], F32)
+        table = [ps.tile([P, PACK, CHUNK], F32, name="table%d" % c, tag="bank%d" % (4 + c)) for c in range(CHUNKS)]
+        for c in range(CHUNKS):
+            nc.scalar.activation(table_turned[c][:], cw_spread[:], ACT.Copy, scale=rw_col[:, c, :])
+            for t in range(PACK):
+                nc.tensor.transpose(table[c][:, t, :], table_turned[c][:, t, :], identity[:])
 
-        x_bf = tiles("x_bf", 2, [P, HALF, PACK], BF16)
-        x_codes = {}
+        x_bf = [tagged("x_bf%d" % h, "x_bf%d" % h, [P, HALF, PACK], BF16) for h in range(2)]
+        x_codes = tiles("x_codes", 2, [P, HALF], U32)
         x_scales = tiles("x_scales", 2, [P, HALF], U8)
         for j in range(PACK):
             for h in range(2):
                 cols = HALF // 16
                 nc.vector.tensor_copy(x_bf[h][:, :, j], x_plane[j][:].indirect(offsets[:, h * cols : (h + 1) * cols]))
 
-        def quantize_x(h, codes):
-            x_codes[h] = codes
-            nc.vector.quantize_mx(
-                out=x_codes[h][:].bitcast(E4M3), scales=x_scales[h][:], in_=x_bf[h][:].rearrange("p i j -> p (i j)")
-            )
+        def quantize(codes, scales, values, fmt):
+            nc.vector.quantize_mx(out=codes.bitcast(fmt), scales=scales, in_=values.rearrange("p i j -> p (i j)"))
 
-        quantize_x(0, sb.tile([P, HALF], U32, name="x_codes0", align_bytes=64))
+        for h in range(2):
+            quantize(x_codes[h][:], x_scales[h][:], x_bf[h][:], E4M3)
 
-        wd_bf = tiles("wd_bf", 2, [P, 2, P, PACK], BF16)
+        wd_bf = [tagged("wd_bf%d" % k, "wd_bf%d" % k, [P, 2, P, PACK], BF16) for k in range(2)]
         wd_codes = tiles("wd_codes", 2, [P, 2 * P], U32)
         wd_scales = tiles("wd_scales", 2, [P, 2 * P], U8)
 
-        def interleave_wd(copy, h, k):
+        def interleave_wd(copy, h, slots):
+            k = slots.start // 2
+            own = slice(slots.start - 2 * k, slots.stop - 2 * k)
             copy(
-                wd_bf[k][:, :, h * (P // 2) : (h + 1) * (P // 2), :].rearrange("p t m j -> p m j t"),
-                wd_raw[h][:].rearrange("p j (m t) -> p m j t", t=PACK)[:, :, :, 2 * k : 2 * k + 2],
+                wd_bf[k][:, own, h * (P // 2) : (h + 1) * (P // 2), :].rearrange("p t m j -> p m j t"),
+                wd_raw[h][:].rearrange("p j (m t) -> p m j t", t=PACK)[:, :, :, slots],
             )
 
         def quantize_wd(h, t):
             cols = slice((t % 2) * P + h * (P // 2), (t % 2) * P + (h + 1) * (P // 2))
-            nc.vector.quantize_mx(
-                out=wd_codes[t // 2][:, cols].bitcast(E4M3),
-                scales=wd_scales[t // 2][:, cols],
-                in_=wd_bf[t // 2][:, t % 2, h * (P // 2) : (h + 1) * (P // 2), :].rearrange("p m j -> p (m j)"),
-            )
+            values = wd_bf[t // 2][:, t % 2, h * (P // 2) : (h + 1) * (P // 2), :]
+            quantize(wd_codes[t // 2][:, cols], wd_scales[t // 2][:, cols], values, E4M3)
 
-        interleave_wd(nc.scalar.copy, 0, 0)
-        interleave_wd(nc.scalar.copy, 0, 1)
+        interleave_wd(nc.scalar.copy, 0, slice(0, 2))
+        interleave_wd(nc.scalar.copy, 0, slice(2, 4))
         quantize_wd(0, 0)
         quantize_wd(0, 1)
-        interleave_wd(nc.vector.tensor_copy, 1, 0)
-        interleave_wd(nc.scalar.copy, 1, 1)
+        interleave_wd(nc.vector.tensor_copy, 1, slice(0, 1))
+        interleave_wd(nc.vector.tensor_copy, 1, slice(1, 2))
+        interleave_wd(nc.scalar.copy, 1, slice(2, 4))
         quantize_wd(1, 0)
         quantize_wd(1, 1)
         for t in (2, 3):
             quantize_wd(0, t)
             quantize_wd(1, t)
-        quantize_x(1, reuse.tile([P, HALF], U32, name="x_codes1", align_bytes=64, offset=0))
 
-        a_pair = {
-            (c, k): ps.tile([P, 2, CHUNK], F32, name="a_pair%d%d" % (c, k), tag="bank%d" % (2 * c + k))
-            for c in range(2)
-            for k in range(2)
-        }
-        a_bank = {c: ps.tile([P, PACK, CHUNK], F32, name="a_bank%d" % c, tag="bank%d" % (c + 2)) for c in (2, 3)}
-        for c in (2, 3):
-            a_pair[c, 0], a_pair[c, 1] = a_bank[c][:, :2, :], a_bank[c][:, 2:, :]
-        q = sb.tile([P, PACK, HALF], F32, name="q", align_bytes=64)
-        q_late = sb.tile([P, PACK, HALF], F32, name="q_late", align_bytes=64)
-        u, r, inv = {}, {}, {}
-        g_bf = {}
-        g_late = sb.tile([P, HALF, PACK], BF16, name="g_late", align_bytes=64)
-        wv_bf, wv_codes, wv_scales = {}, {}, {}
-        for c in range(2):
-            inv[c] = sb.tile([P, PACK, CHUNK], F32, name="inv%d" % c, tag="inv%d" % c, align_bytes=64)
-            u[c] = sb.tile([P, PACK, CHUNK], F32, name="u%d" % c, tag="u%d" % c, align_bytes=64)
+        def scores(bank, t, h, cols):
+            m = slice((t % 2) * P, (t % 2 + 1) * P)
+            nc.tensor.matmul_mx(
+                out=bank,
+                lhsT=wd_codes[t // 2][:, m].bitcast(E4M3),
+                lhsT_scale=wd_scales[t // 2][:, m],
+                rhs=x_codes[h][:, cols].bitcast(E4M3),
+                rhs_scale=x_scales[h][:, cols],
+                start=True,
+                stop=True,
+            )
 
         def part(c, piece=WHOLE):
             return slice((c % 2) * CHUNK + piece.start, (c % 2) * CHUNK + piece.stop)
 
-        def first_product(c, k):
-            for t in (2 * k, 2 * k + 1):
-                m = slice((t % 2) * P, (t % 2 + 1) * P)
-                nc.tensor.matmul_mx(
-                    out=a_pair[c, k][:, t % 2, :],
-                    lhsT=wd_codes[t // 2][:, m].bitcast(E4M3),
-                    lhsT_scale=wd_scales[t // 2][:, m],
-                    rhs=x_codes[c // 2][:, part(c)].bitcast(E4M3),
-                    rhs_scale=x_scales[c // 2][:, part(c)],
-                    start=True,
-                    stop=True,
-                )
+        a_slot = [ps.tile([P, HALF], F32, name="a_slot%d" % t, tag="bank%d" % t) for t in range(2)]
+        a_pair = ps.tile([P, 2, HALF], F32, name="a_pair", tag="bank2")
+        a_late = {c: ps.tile([P, PACK, CHUNK], F32, name="a_late%d" % c, tag="bank%d" % (c - 2)) for c in (2, 3)}
+        for t in range(PACK):
+            scores(a_slot[t][:] if t < 2 else a_pair[:, t - 2, :], t, 0, slice(0, HALF))
+
+        q_early = sb.tile([P, PACK, HALF], F32, name="q_early", align_bytes=64)
+        u_early = sb.tile([P, PACK, HALF], F32, name="u_early", align_bytes=64)
+        q = [q_early[:, :, part(0)], q_early[:, :, part(1)]] + [t[:] for t in tiles("q_late", 2, [P, PACK, CHUNK], F32)]
+        num_early = tagged("num_early", "num_early", [P, HALF, PACK], F32)
+        num = [num_early[:, part(0), :], num_early[:, part(1), :]]
+        num += [tagged("num%d" % c, "num%d" % c, [P, CHUNK, PACK], F32)[:] for c in (2, 3)]
+        g_early = tagged("g_early", "g_early", [P, HALF, PACK], BF16)
+        wv_codes, wv_scales = {}, {}
+
+        def residual_slot(t):
+            nc.vector.tensor_tensor(q_early[:, t, :], a_slot[t][:], y_pair[0][:, t, :], ALU.subtract)
+            nc.scalar.activation(u_early[:, t, :], q_early[:, t, :], ACT.Square)
+
+        def residual_pair(c):
+            nc.vector.tensor_tensor(q[c][:, 2:, :], a_pair[:, :, part(c)], y_pair[1][:, :, part(c)], ALU.subtract)
+            nc.scalar.activation(u_early[:, 2:, part(c)], q[c][:, 2:, :], ACT.Square)
 
         def residual_late(c):
-            nc.vector.tensor_tensor(q_late[:, :, part(c)], a_bank[c][:], y_late[:, :, part(c)], ALU.subtract)
+            for t in range(PACK):
+                scores(a_late[c][:, t, :], t, 1, part(c))
+            nc.vector.tensor_tensor(q[c], a_late[c][:], y_late[:, :, part(c)], ALU.subtract)
 
-        def residual_pair(c, k):
-            targets = y_pair[k][:, :, part(c)]
-            slots = slice(2 * k, 2 * k + 2)
-            nc.vector.tensor_tensor(q[:, slots, part(c)], a_pair[c, k][:], targets, ALU.subtract)
-
-        def square_pair(c, k):
-            slots = slice(2 * k, 2 * k + 2)
-            nc.scalar.activation(u[c][:, slots, :], q[:, slots, part(c)], ACT.Square)
-
-        def root_pair(k):
-            r[0, k] = sb.tile([P, 2, CHUNK], F32, name="r0_%d" % k, tag="r0_%d" % k, align_bytes=64)
-            nc.scalar.activation(r[0, k][:], u[0][:, 2 * k : 2 * k + 2, :], ACT.Abs_reciprocal_sqrt, bias=1.0)
-
-        def inverse_pair(k):
-            nc.scalar.activation(inv[0][:, 2 * k : 2 * k + 2, :], r[0, k][:], ACT.Square)
-
-        def root(c, piece):
-            tag = "r%d_%d" % (c, piece.start)
-            if tag not in late_tiles:
-                late_tiles[tag] = sb.tile([P, PACK, CHUNK // 2], F32, name=tag, tag=tag, align_bytes=64)
-            r[c, piece.start] = late_tiles[tag]
-            nc.scalar.activation(r[c, piece.start][:], u[c][:, :, piece], ACT.Abs_reciprocal_sqrt, bias=1.0)
-
-        def inverse(c, piece):
-            nc.scalar.activation(inv[c][:, :, piece], r[c, piece.start][:], ACT.Square)
-
-        def square_late(c, piece):
-            nc.scalar.activation(
-                u[c][:, piece, :].rearrange("p (n e) t -> p n t e", e=2),
-                q_late[:, :, part(c, piece)].rearrange("p t (n e) -> p n t e", e=2),
-                ACT.Square,
-            )
-
-        def root_late(c, piece):
-            tag = "r%d_%d" % (c, piece.start)
-            r[c, piece.start] = late_tiles[tag]
-            nc.scalar.activation(r[c, piece.start][:], u[c][:, piece, :], ACT.Abs_reciprocal_sqrt, bias=1.0)
-
-        def inverse_late(c, piece):
-            tag = "inv%d_%d" % (c, piece.start)
-            inv[c, piece.start] = late_tiles[tag]
-            nc.scalar.activation(inv[c, piece.start][:], r[c, piece.start][:], ACT.Square)
-
-        def gradient(c, piece=WHOLE):
-            g_bf[c, piece.start] = sb.tile([P, piece.stop - piece.start, PACK], BF16, name="g%d_%d" % (c, piece.start), align_bytes=64)
+        def numerator(c):
             nc.vector.tensor_tensor(
-                g_bf[c, piece.start][:].rearrange("p (n e) t -> p n t e", e=2),
-                num[:, :, part(c, piece)].rearrange("p t (n e) -> p n t e", e=2),
-                inv[c][:, :, piece].rearrange("p t (n e) -> p n t e", e=2),
+                pairs_of_position_major(num[c]),
+                pairs_of_slot_major(q[c]),
+                pairs_of_slot_major(table[c][:]),
                 ALU.mult,
             )
 
-        def gradient_late(engine, c, piece):
-            engine.tensor_tensor(g_late[:, part(c, piece), :], num_late[:, part(c, piece), :], inv[c, piece.start][:], ALU.mult)
+        def root(target, source):
+            nc.scalar.activation(target, source, ACT.Abs_reciprocal_sqrt, bias=1.0)
 
-        def quantize_g(c, piece=WHOLE):
-            cols = slice(c * CHUNK + piece.start, c * CHUNK + piece.stop)
-            nc.vector.quantize_mx(
-                out=g_codes[:, cols].bitcast(E5M2),
-                scales=g_scales[:, cols],
-                in_=g_bf[c, piece.start][:].rearrange("p i t -> p (i t)"),
-            )
+        def square(target, source):
+            nc.scalar.activation(target, source, ACT.Square)
 
-        def quantize_g_late(c, piece):
-            cols = slice(c * CHUNK + piece.start, c * CHUNK + piece.stop)
-            nc.vector.quantize_mx(
-                out=g_codes[:, cols].bitcast(E5M2),
-                scales=g_scales[:, cols],
-                in_=g_late[:, part(c, piece), :].rearrange("p i t -> p (i t)"),
-            )
+        def root_of_early(cols):
+            root(pairs_of_position_major(root_early[:, cols, :]), pairs_of_slot_major(u_early[:, :, cols]))
 
-        def interleave_wv(b, source, tag=None):
-            if tag:
-                wv_bf[b] = sb.tile([P, P, PACK], BF16, name="wv_bf%d" % b, tag=tag, align_bytes=64)
-            else:
-                wv_bf[b] = reuse.tile([P, P, PACK], BF16, name="wv_bf%d" % b, align_bytes=64, offset=1024 * (b + 1))
-            nc.scalar.copy(
-                wv_bf[b][:].rearrange("p (n e) j -> p n j e", e=4),
-                source.rearrange("p j (n e) -> p n j e", e=4),
-            )
+        def inverse_of_early(cols):
+            square(inv_early[:, cols, :], root_early[:, cols, :])
 
-        def quantize_wv(b, tag):
-            wv_codes[b] = sb.tile([P, P], U32, name="wv_codes%d" % b, tag=tag, align_bytes=64)
+        def square_late(c):
+            square(pairs_of_position_major(u_late[:, part(c), :]), pairs_of_slot_major(q[c]))
+
+        def gradient(engine, target, numerators, inverses):
+            engine.tensor_tensor(target, numerators, inverses, ALU.mult)
+
+        def quantize_g(source, first):
+            place = slice(first, first + source.shape[1])
+            quantize(g_codes[:, place], g_scales[:, place], source, E5M2)
+
+        def quantize_wv(b, values, tag):
+            wv_codes[b] = tagged("wv_codes%d" % b, tag, [P, P], U32)
             wv_scales[b] = sb.tile([P, P], U8, name="wv_scales%d" % b, align_bytes=64)
-            nc.vector.quantize_mx(
-                out=wv_codes[b][:].bitcast(E4M3), scales=wv_scales[b][:], in_=wv_bf[b][:].rearrange("p d j -> p (d j)")
-            )
+            quantize(wv_codes[b][:], wv_scales[b][:], values[:], E4M3)
 
-        def second_product(b, cols, tag, copy, slot=None):
+        def second_pass(b, cols, bank_tag):
             count = cols.stop - cols.start
-            bank = ps.tile([P, count], F32, name="dx_" + tag, tag=tag)
+            name = "dx%d_%d" % (b, cols.start)
+            bank = ps.tile([P, count], F32, name=name, tag=bank_tag)
             nc.tensor.matmul_mx(
                 out=bank[:],
                 lhsT=wv_codes[b][:].bitcast(E4M3),
@@ -294,105 +251,91 @@ def tile_attend_gml_cau_kernel(tc, xT, wd, wv, y, cw, rw, offs, out):
                 start=True,
                 stop=True,
             )
-            dx = sb.tile([P, count], F32, name="dx_sb_" + tag, tag=slot or "dx_" + tag, align_bytes=64)
+            return bank
+
+        def second_product(b, cols, bank_tag, copy, buffer_tag):
+            bank = second_pass(b, cols, bank_tag)
+            dx = tagged("dx%d_%d_sb" % (b, cols.start), buffer_tag, [P, cols.stop - cols.start], F32)
             copy(dx[:], bank[:])
             return dx
 
-        def scatter_on_vector(b, first, values):
-            count = values.shape[1]
-            nc.vector.tensor_copy(window[b][:].indirect(offsets[:, first // 16 : (first + count) // 16]), values)
+        def listed(b, first, count):
+            return window[b][:].indirect(offsets[:, first // 16 : (first + count) // 16])
 
-        def scatter_chunk(b, first, values):
-            nc.vector.tensor_tensor(
-                window[b][:].indirect(offsets[:, first // 16 : (first + CHUNK) // 16]), values, zeros[:], ALU.add
-            )
+        def scatter_on_vector(b, first, values):
+            nc.vector.tensor_copy(listed(b, first, values.shape[1]), values)
 
         def scatter_on_scalar(b, first, values):
-            count = values.shape[1]
-            nc.scalar.activation(window[b][:].indirect(offsets[:, first // 16 : (first + count) // 16]), values, ACT.Copy)
+            nc.scalar.activation(listed(b, first, values.shape[1]), values, ACT.Copy)
 
         def store(b):
             for cols in (slice(0, T // 2), slice(T // 2, T)):
                 nc.sync.dma_start(out[b * P : (b + 1) * P, cols], window[b][:, cols])
 
-        num = sb.tile([P, PACK, HALF], F32, name="num", tag="num", align_bytes=64)
-        interleave_wv(0, wv_first[0][:])
-        for c, k in ((0, 0), (1, 0), (0, 1), (1, 1), (2, 0), (2, 1), (3, 0), (3, 1)):
-            first_product(c, k)
-        for k in range(2):
-            for c in range(2):
-                residual_pair(c, k)
-        square_pair(0, 0)
-        square_pair(1, 0)
-        root_pair(0)
-        square_pair(0, 1)
-        inverse_pair(0)
-        square_pair(1, 1)
-        root_pair(1)
-        root(1, LOW)
-        inverse_pair(1)
-        root(1, HIGH)
-        inverse(1, LOW)
-        inverse(1, HIGH)
-        interleave_wv(1, wv_first[1][:], "r1_0")
-        nc.vector.tensor_tensor(num[:], q[:], weight_rows[:, :, :HALF], ALU.mult)
+        def round_wv_on_gpsimd(target, source):
+            nc.gpsimd.tensor_scalar(target[:], source.rearrange("p j d -> p d j"), 1.0, 0.0, ALU.mult, ALU.add)
+
+        wv_bf0 = tagged("wv_bf0", "wd_bf1", [P, P, PACK], BF16)
+        round_wv_on_gpsimd(wv_bf0, wv_first[:])
+        wv_bf1 = tagged("wv_bf1", "wv_bf1", [P, P, PACK], BF16)
+        wv_bf2 = tagged("wv_bf2", "wv_bf2", [P, P, PACK], BF16)
+        round_wv_on_gpsimd(wv_bf1, wv_middle[:, :, :P])
+        round_wv_on_gpsimd(wv_bf2, wv_middle[:, :, P:])
+
+        for t in range(2):
+            residual_slot(t)
+        for c in range(2):
+            residual_pair(c)
+        numerator(0)
+        numerator(1)
         residual_late(2)
         residual_late(3)
-        gradient(0)
-        gradient(1, LOW)
-        gradient(1, HIGH)
-        quantize_wv(0, "r0_1")
-        quantize_g(0)
-        quantize_g(1, LOW)
-        quantize_g(1, HIGH)
-        u_late = sb.tile([P, HALF, PACK], F32, name="u_late", tag="r1_64", align_bytes=64)
-        u[2], u[3] = u_late[:, :CHUNK, :], u_late[:, CHUNK:, :]
-        square_late(2, LOW)
-        square_late(2, HIGH)
-        root_late(2, LOW)
-        root_late(2, HIGH)
-        inverse_late(2, LOW)
-        square_late(3, WHOLE)
-        inverse_late(2, HIGH)
-        root_late(3, LOW)
-        root_late(3, HIGH)
-        inverse_late(3, LOW)
-        inverse_late(3, HIGH)
-        num_late = sb.tile([P, HALF, PACK], F32, name="num_late", tag="num", align_bytes=64)
-        nc.vector.tensor_tensor(
-            num_late[:].rearrange("p (n e) t -> p n t e", e=2),
-            q_late[:].rearrange("p t (n e) -> p n t e", e=2),
-            weight_rows[:, :, HALF:].rearrange("p t (n e) -> p n t e", e=2),
-            ALU.mult,
-        )
-        early = second_product(0, slice(0, HALF), "bank0", nc.vector.tensor_copy)
-        quantize_wv(1, "wv_codes1")
-        scatter_on_vector(0, 0, early[:])
-        gradient_late(nc.gpsimd, 2, LOW)
-        gradient_late(nc.gpsimd, 2, HIGH)
-        gradient_late(nc.gpsimd, 3, LOW)
-        quantize_g_late(2, WHOLE)
-        gradient_late(nc.vector, 3, HIGH)
-        quantize_g_late(3, LOW)
-        quantize_g_late(3, HIGH)
-        first_half = second_product(1, slice(0, HALF), "bank5", nc.scalar.copy, "r3_64")
-        interleave_wv(2, wv_last[:, :, :P], "r3_0")
-        third = second_product(0, slice(2 * CHUNK, 3 * CHUNK), "bank3", nc.scalar.copy)
+        numerator(2)
+        numerator(3)
+        for c in range(2):
+            root_of_early(part(c))
+        for c in range(2):
+            inverse_of_early(part(c))
+        for c in (2, 3):
+            square_late(c)
+        root(root2[:], u_late[:, part(2), :])
+        root(root3[:], u_late[:, part(3), :])
+        square(inv_late[0][:], root2[:])
+        square(inv_late[1][:], root3[:])
+
+        gradient(nc.gpsimd, g_early[:, part(0), :], num[0], inv_early[:, part(0), :])
+        gradient(nc.vector, g_early[:, part(1), :], num[1], inv_early[:, part(1), :])
+        quantize_wv(0, wv_bf0, "root_early")
+        quantize_g(g_early[:], 0)
+        quantize_wv(1, wv_bf1, "inv_early")
+        quantize_wv(2, wv_bf2, "num_early")
+        early = second_product(0, slice(0, HALF), "bank3", nc.vector.tensor_copy, "dx_early")
+        scatter_on_scalar(0, 0, early[:])
+        g_late = tiles("g_late", 2, [P, CHUNK, PACK], BF16)
+        for c in (2, 3):
+            gradient(nc.vector, g_late[c - 2][:], num[c], inv_late[c - 2][:])
+        for c in (2, 3):
+            quantize_g(g_late[c - 2][:], c * CHUNK)
+        first_half = second_product(1, slice(0, HALF), "bank5", nc.vector.tensor_copy, "inv3")
         scatter_on_scalar(1, 0, first_half[:])
-        interleave_wv(3, wv_last[:, :, P:], "r3_64")
-        quantize_wv(2, "wv_codes2")
-        scatter_chunk(0, 2 * CHUNK, third[:])
-        last = second_product(0, slice(3 * CHUNK, N), "bank1", nc.vector.tensor_copy)
-        scatter_chunk(0, 3 * CHUNK, last[:])
+        late = sb.tile([P, HALF], F32, name="dx_late", align_bytes=64)
+        for c in (2, 3):
+            bank = second_pass(0, slice(c * CHUNK, (c + 1) * CHUNK), "bank%d" % (3 - c))
+            nc.vector.tensor_copy(late[:, part(c)], bank[:])
+        scatter_on_vector(0, HALF, late[:])
         store(0)
-        second_half = second_product(1, slice(HALF, N), "bank5", nc.scalar.copy, "r2_0")
+        second_half = second_product(1, slice(HALF, N), "bank5", nc.scalar.copy, "root3")
+        wv_bf3 = tagged("wv_bf3", "inv3", [P, P, PACK], BF16)
+        nc.scalar.copy(
+            wv_bf3[:].rearrange("p (n e) j -> p n j e", e=4), wv_last[:].rearrange("p j (n e) -> p n j e", e=4)
+        )
         scatter_on_scalar(1, HALF, second_half[:])
         store(1)
-        dx = second_product(2, slice(0, N), "bank1", nc.vector.tensor_copy, "dx_w2")
-        quantize_wv(3, "wv_codes3")
-        scatter_on_vector(2, 0, dx[:])
+        dx2 = second_product(2, slice(0, N), "bank0", nc.vector.tensor_copy, "dx_w2")
+        quantize_wv(3, wv_bf3, "wv_codes3")
+        scatter_on_vector(2, 0, dx2[:])
         store(2)
-        dx = second_product(3, slice(0, N), "bank5", nc.scalar.copy, "r1_64")
+        dx3 = second_product(3, slice(0, N), "bank0", nc.scalar.copy, "u_late")
         for first in (0, HALF):
-            scatter_on_scalar(3, first, dx[:, first : first + HALF])
+            scatter_on_scalar(3, first, dx3[:, first : first + HALF])
         store(3)

@@ -48,11 +48,11 @@ def tile_attend_gml_cau_kernel(tc, xT, wd, wv, y, cw, rw, offs, out):
         offsets = sb.tile([P, N // 16], U16, name="offsets")
         weights_row = sb.tile([P, N], F32, name="weights_row", align_bytes=DMA_ALIGN)
         nc.gpsimd.memset(weights_row[:], 0.0)
-        u_late = tagged("u_late", "u_late", [P, HALF, PACK], F32)
+        u_late = {c: tagged("u%d" % c, "u%d" % c, [P, CHUNK, PACK], F32) for c in (2, 3)}
         root2 = tagged("root2", "root2", [P, CHUNK, PACK], F32)
         root3 = tagged("root3", "root3", [P, CHUNK, PACK], F32)
         inv_late = [tagged("inv%d" % c, "inv%d" % c, [P, CHUNK, PACK], F32) for c in (2, 3)]
-        root_early = tagged("root_early", "root_early", [P, HALF, PACK], F32)
+        root_early = [tagged("root%d" % c, "root%d" % c, [P, CHUNK, PACK], F32) for c in range(2)]
         inv_early = tagged("inv_early", "inv_early", [P, HALF, PACK], F32)
         wd_raw = tiles("wd_raw", 2, [P, PACK, V // 2], F32, DMA_ALIGN)
         wv_first = sb.tile([P, PACK, P], F32, name="wv_first", align_bytes=DMA_ALIGN)
@@ -60,7 +60,8 @@ def tile_attend_gml_cau_kernel(tc, xT, wd, wv, y, cw, rw, offs, out):
         wv_last = sb.tile([P, PACK, P], F32, name="wv_last", align_bytes=DMA_ALIGN)
         x_plane = tiles("x_plane", PACK, [P, T], F32, DMA_ALIGN)
         y_pair = tiles("y_pair", 2, [P, 2, HALF], F32, DMA_ALIGN)
-        y_late = sb.tile([P, PACK, HALF], F32, name="y_late", align_bytes=DMA_ALIGN)
+        reuse = ctx.enter_context(tc.tile_pool(name="reuse", bufs=1))
+        y_late = reuse.tile([P, PACK, HALF], F32, name="y_late", align_bytes=DMA_ALIGN, offset=0)
 
         x_rows = xT.rearrange("(p j) c -> p j c", j=PACK)
         wd_rows = wd.rearrange("(p j) v -> p j v", j=PACK)
@@ -176,10 +177,13 @@ def tile_attend_gml_cau_kernel(tc, xT, wd, wv, y, cw, rw, offs, out):
             return slice((c % 2) * CHUNK + piece.start, (c % 2) * CHUNK + piece.stop)
 
         a_slot = [ps.tile([P, HALF], F32, name="a_slot%d" % t, tag="bank%d" % t) for t in range(2)]
-        a_pair = ps.tile([P, 2, HALF], F32, name="a_pair", tag="bank2")
+        a_pair = [ps.tile([P, 2, CHUNK], F32, name="a_pair%d" % c, tag="bank%d" % (2 + c)) for c in range(2)]
         a_late = {c: ps.tile([P, PACK, CHUNK], F32, name="a_late%d" % c, tag="bank%d" % (c - 2)) for c in (2, 3)}
-        for t in range(PACK):
-            scores(a_slot[t][:] if t < 2 else a_pair[:, t - 2, :], t, 0, slice(0, HALF))
+        for t in range(2):
+            scores(a_slot[t][:], t, 0, slice(0, HALF))
+        for c in range(2):
+            for t in (2, 3):
+                scores(a_pair[c][:, t - 2, :], t, 0, part(c))
 
         q_early = sb.tile([P, PACK, HALF], F32, name="q_early", align_bytes=64)
         u_early = sb.tile([P, PACK, HALF], F32, name="u_early", align_bytes=64)
@@ -187,7 +191,7 @@ def tile_attend_gml_cau_kernel(tc, xT, wd, wv, y, cw, rw, offs, out):
         num_early = tagged("num_early", "num_early", [P, HALF, PACK], F32)
         num = [num_early[:, part(0), :], num_early[:, part(1), :]]
         num += [tagged("num%d" % c, "num%d" % c, [P, CHUNK, PACK], F32)[:] for c in (2, 3)]
-        g_early = tagged("g_early", "g_early", [P, HALF, PACK], BF16)
+        g_early = reuse.tile([P, HALF, PACK], BF16, name="g_early", align_bytes=64, offset=0)
         wv_codes, wv_scales = {}, {}
 
         def residual_slot(t):
@@ -195,7 +199,7 @@ def tile_attend_gml_cau_kernel(tc, xT, wd, wv, y, cw, rw, offs, out):
             nc.scalar.activation(u_early[:, t, :], q_early[:, t, :], ACT.Square)
 
         def residual_pair(c):
-            nc.vector.tensor_tensor(q[c][:, 2:, :], a_pair[:, :, part(c)], y_pair[1][:, :, part(c)], ALU.subtract)
+            nc.vector.tensor_tensor(q[c][:, 2:, :], a_pair[c][:], y_pair[1][:, :, part(c)], ALU.subtract)
             nc.scalar.activation(u_early[:, 2:, part(c)], q[c][:, 2:, :], ACT.Square)
 
         def residual_late(c):
@@ -217,14 +221,14 @@ def tile_attend_gml_cau_kernel(tc, xT, wd, wv, y, cw, rw, offs, out):
         def square(target, source):
             nc.scalar.activation(target, source, ACT.Square)
 
-        def root_of_early(cols):
-            root(pairs_of_position_major(root_early[:, cols, :]), pairs_of_slot_major(u_early[:, :, cols]))
+        def root_of_early(c):
+            root(pairs_of_position_major(root_early[c][:]), pairs_of_slot_major(u_early[:, :, part(c)]))
 
-        def inverse_of_early(cols):
-            square(inv_early[:, cols, :], root_early[:, cols, :])
+        def inverse_of_early(c):
+            square(inv_early[:, part(c), :], root_early[c][:])
 
         def square_late(c):
-            square(pairs_of_position_major(u_late[:, part(c), :]), pairs_of_slot_major(q[c]))
+            square(pairs_of_position_major(u_late[c][:]), pairs_of_slot_major(q[c]))
 
         def gradient(engine, target, numerators, inverses):
             engine.tensor_tensor(target, numerators, inverses, ALU.mult)
@@ -233,8 +237,8 @@ def tile_attend_gml_cau_kernel(tc, xT, wd, wv, y, cw, rw, offs, out):
             place = slice(first, first + source.shape[1])
             quantize(g_codes[:, place], g_scales[:, place], source, E5M2)
 
-        def quantize_wv(b, values, tag):
-            wv_codes[b] = tagged("wv_codes%d" % b, tag, [P, P], U32)
+        def quantize_wv(b, values, codes):
+            wv_codes[b] = codes
             wv_scales[b] = sb.tile([P, P], U8, name="wv_scales%d" % b, align_bytes=64)
             quantize(wv_codes[b][:], wv_scales[b][:], values[:], E4M3)
 
@@ -293,31 +297,34 @@ def tile_attend_gml_cau_kernel(tc, xT, wd, wv, y, cw, rw, offs, out):
         numerator(2)
         numerator(3)
         for c in range(2):
-            root_of_early(part(c))
+            root_of_early(c)
         for c in range(2):
-            inverse_of_early(part(c))
+            inverse_of_early(c)
         for c in (2, 3):
             square_late(c)
-        root(root2[:], u_late[:, part(2), :])
-        root(root3[:], u_late[:, part(3), :])
-        square(inv_late[0][:], root2[:])
+        root(root2[:], u_late[2][:])
+        root(root3[:], u_late[3][:])
+        square(inv_late[0][:, HIGH, :], root2[:, HIGH, :])
         square(inv_late[1][:], root3[:])
 
         gradient(nc.gpsimd, g_early[:, part(0), :], num[0], inv_early[:, part(0), :])
         gradient(nc.vector, g_early[:, part(1), :], num[1], inv_early[:, part(1), :])
-        quantize_wv(0, wv_bf0, "root_early")
+        quantize_wv(0, wv_bf0, reuse.tile([P, P], U32, name="wv_codes0", align_bytes=64, offset=2048))
         quantize_g(g_early[:], 0)
-        quantize_wv(1, wv_bf1, "inv_early")
-        quantize_wv(2, wv_bf2, "num_early")
+        once = tagged("once", "inv_early", [P, CHUNK // 2, PACK], F32)
+        gradient(nc.vector, once[:], num[2][:, LOW, :], root2[:, LOW, :])
+        quantize_wv(1, wv_bf1, tagged("wv_codes1", "num_early", [P, P], U32))
+        g_late = tiles("g_late", 2, [P, CHUNK, PACK], BF16)
+        gradient(nc.vector, g_late[0][:, LOW, :], once[:], root2[:, LOW, :])
         early = second_product(0, slice(0, HALF), "bank3", nc.vector.tensor_copy, "dx_early")
         scatter_on_scalar(0, 0, early[:])
-        g_late = tiles("g_late", 2, [P, CHUNK, PACK], BF16)
-        for c in (2, 3):
-            gradient(nc.vector, g_late[c - 2][:], num[c], inv_late[c - 2][:])
+        gradient(nc.vector, g_late[0][:, HIGH, :], num[2][:, HIGH, :], inv_late[0][:, HIGH, :])
+        gradient(nc.vector, g_late[1][:], num[3], inv_late[1][:])
         for c in (2, 3):
             quantize_g(g_late[c - 2][:], c * CHUNK)
         first_half = second_product(1, slice(0, HALF), "bank5", nc.vector.tensor_copy, "inv3")
         scatter_on_scalar(1, 0, first_half[:])
+        quantize_wv(2, wv_bf2, tagged("wv_codes2", "num3", [P, P], U32))
         late = sb.tile([P, HALF], F32, name="dx_late", align_bytes=64)
         for c in (2, 3):
             bank = second_pass(0, slice(c * CHUNK, (c + 1) * CHUNK), "bank%d" % (3 - c))
@@ -332,10 +339,10 @@ def tile_attend_gml_cau_kernel(tc, xT, wd, wv, y, cw, rw, offs, out):
         scatter_on_scalar(1, HALF, second_half[:])
         store(1)
         dx2 = second_product(2, slice(0, N), "bank0", nc.vector.tensor_copy, "dx_w2")
-        quantize_wv(3, wv_bf3, "wv_codes3")
+        quantize_wv(3, wv_bf3, tagged("wv_codes3", "wv_codes3", [P, P], U32))
         scatter_on_vector(2, 0, dx2[:])
         store(2)
-        dx3 = second_product(3, slice(0, N), "bank0", nc.scalar.copy, "u_late")
+        dx3 = second_product(3, slice(0, N), "bank0", nc.scalar.copy, "u2")
         for first in (0, HALF):
             scatter_on_scalar(3, first, dx3[:, first : first + HALF])
         store(3)

@@ -106,7 +106,7 @@ def tile_attend_gml_cau_kernel(tc, xT, wd, wv, y, cw, rw, offs, out):
         cw_col = sb.tile([P, PACK, 1], F32, name="cw_col")
         rw_col = sb.tile([P, CHUNKS, 1], F32, name="rw_col")
         nc.scalar.copy(cw_col[:], cw_turned[:, :, 0:1])
-        nc.scalar.copy(rw_col[:], rw_turned[:, :, 1:2])
+        nc.scalar.activation(rw_col[:], rw_turned[:, :, 1:2], ACT.Copy, scale=-1.0)
         cw_spread = ps.tile([P, PACK, P], F32, name="cw_spread", tag="bank2")
         for t in range(PACK):
             nc.tensor.transpose(cw_spread[:, t, :], cw_col[:, t, :].to_broadcast([P, P]), identity[:])
@@ -195,17 +195,17 @@ def tile_attend_gml_cau_kernel(tc, xT, wd, wv, y, cw, rw, offs, out):
         wv_codes, wv_scales = {}, {}
 
         def residual_slot(t):
-            nc.vector.tensor_tensor(q_early[:, t, :], a_slot[t][:], y_pair[0][:, t, :], ALU.subtract)
+            nc.vector.tensor_tensor(q_early[:, t, :], y_pair[0][:, t, :], a_slot[t][:], ALU.subtract)
             nc.scalar.activation(u_early[:, t, :], q_early[:, t, :], ACT.Square)
 
         def residual_pair(c):
-            nc.vector.tensor_tensor(q[c][:, 2:, :], a_pair[c][:], y_pair[1][:, :, part(c)], ALU.subtract)
+            nc.vector.tensor_tensor(q[c][:, 2:, :], y_pair[1][:, :, part(c)], a_pair[c][:], ALU.subtract)
             nc.scalar.activation(u_early[:, 2:, part(c)], q[c][:, 2:, :], ACT.Square)
 
         def residual_late(c):
             for t in range(PACK):
                 scores(a_late[c][:, t, :], t, 1, part(c))
-            nc.vector.tensor_tensor(q[c], a_late[c][:], y_late[:, :, part(c)], ALU.subtract)
+            nc.vector.tensor_tensor(q[c], y_late[:, :, part(c)], a_late[c][:], ALU.subtract)
 
         def numerator(c):
             nc.vector.tensor_tensor(

@@ -48,12 +48,13 @@ def tile_attend_gml_cau_kernel(tc, xT, wd, wv, y, cw, rw, offs, out):
         offsets = sb.tile([P, N // 16], U16, name="offsets")
         weights_row = sb.tile([P, N], F32, name="weights_row", align_bytes=DMA_ALIGN)
         nc.gpsimd.memset(weights_row[:], 0.0)
-        u_late = {c: tagged("u%d" % c, "u%d" % c, [P, CHUNK, PACK], F32) for c in (2, 3)}
-        root2 = tagged("root2", "root2", [P, CHUNK, PACK], F32)
-        root3 = tagged("root3", "root3", [P, CHUNK, PACK], F32)
-        inv_late = [tagged("inv%d" % c, "inv%d" % c, [P, CHUNK, PACK], F32) for c in (2, 3)]
-        root_early = [tagged("root%d" % c, "root%d" % c, [P, CHUNK, PACK], F32) for c in range(2)]
-        inv_early = tagged("inv_early", "inv_early", [P, HALF, PACK], F32)
+        u_late = {c: tagged("u%d" % c, "u%d" % c, [P, PACK, CHUNK], F32) for c in (2, 3)}
+        root2 = tagged("root2", "root2", [P, PACK, CHUNK], F32)
+        root3 = tagged("root3", "root3", [P, PACK, CHUNK], F32)
+        inv_late = [tagged("inv%d" % c, "inv%d" % c, [P, PACK, CHUNK], F32) for c in (2, 3)]
+        early_shapes = ([P, CHUNK, PACK], [P, PACK, CHUNK])
+        root_early = [tagged("root%d" % c, "root%d" % c, early_shapes[c], F32) for c in range(2)]
+        inv_early = [tagged("inv%d" % c, "inv%d" % c, early_shapes[c], F32) for c in range(2)]
         wd_raw = tiles("wd_raw", 2, [P, PACK, V // 2], F32, DMA_ALIGN)
         wv_first = sb.tile([P, PACK, P], F32, name="wv_first", align_bytes=DMA_ALIGN)
         wv_middle = sb.tile([P, PACK, 2 * P], F32, name="wv_middle", align_bytes=DMA_ALIGN)
@@ -188,9 +189,7 @@ def tile_attend_gml_cau_kernel(tc, xT, wd, wv, y, cw, rw, offs, out):
         q_early = sb.tile([P, PACK, HALF], F32, name="q_early", align_bytes=64)
         u_early = sb.tile([P, PACK, HALF], F32, name="u_early", align_bytes=64)
         q = [q_early[:, :, part(0)], q_early[:, :, part(1)]] + [t[:] for t in tiles("q_late", 2, [P, PACK, CHUNK], F32)]
-        num_early = tagged("num_early", "num_early", [P, HALF, PACK], F32)
-        num = [num_early[:, part(0), :], num_early[:, part(1), :]]
-        num += [tagged("num%d" % c, "num%d" % c, [P, CHUNK, PACK], F32)[:] for c in (2, 3)]
+        num = [tagged("num%d" % c, "num%d" % c, early_shapes[min(c, 1)], F32)[:] for c in range(CHUNKS)]
         g_early = reuse.tile([P, HALF, PACK], BF16, name="g_early", align_bytes=64, offset=0)
         wv_codes, wv_scales = {}, {}
 
@@ -208,12 +207,15 @@ def tile_attend_gml_cau_kernel(tc, xT, wd, wv, y, cw, rw, offs, out):
             nc.vector.tensor_tensor(q[c], y_late[:, :, part(c)], a_late[c][:], ALU.subtract)
 
         def numerator(c):
-            nc.vector.tensor_tensor(
-                pairs_of_position_major(num[c]),
-                pairs_of_slot_major(q[c]),
-                pairs_of_slot_major(table[c][:]),
-                ALU.mult,
-            )
+            if c == 0:
+                nc.vector.tensor_tensor(
+                    pairs_of_position_major(num[c]),
+                    pairs_of_slot_major(q[c]),
+                    pairs_of_slot_major(table[c][:]),
+                    ALU.mult,
+                )
+            else:
+                nc.vector.tensor_tensor(num[c], q[c], table[c][:], ALU.mult)
 
         def root(target, source):
             nc.scalar.activation(target, source, ACT.Abs_reciprocal_sqrt, bias=1.0)
@@ -222,16 +224,21 @@ def tile_attend_gml_cau_kernel(tc, xT, wd, wv, y, cw, rw, offs, out):
             nc.scalar.activation(target, source, ACT.Square)
 
         def root_of_early(c):
-            root(pairs_of_position_major(root_early[c][:]), pairs_of_slot_major(u_early[:, :, part(c)]))
+            if c == 0:
+                root(pairs_of_position_major(root_early[c][:]), pairs_of_slot_major(u_early[:, :, part(c)]))
+            else:
+                root(root_early[c][:], u_early[:, :, part(c)])
 
         def inverse_of_early(c):
-            square(inv_early[:, part(c), :], root_early[c][:])
+            square(inv_early[c][:], root_early[c][:])
 
         def square_late(c):
-            square(pairs_of_position_major(u_late[c][:]), pairs_of_slot_major(q[c]))
+            square(u_late[c][:], q[c])
 
-        def gradient(engine, target, numerators, inverses):
-            engine.tensor_tensor(target, numerators, inverses, ALU.mult)
+        def gradient(target, first, second):
+            nc.vector.tensor_tensor(
+                pairs_of_position_major(target), pairs_of_slot_major(first), pairs_of_slot_major(second), ALU.mult
+            )
 
         def quantize_g(source, first):
             place = slice(first, first + source.shape[1])
@@ -304,22 +311,22 @@ def tile_attend_gml_cau_kernel(tc, xT, wd, wv, y, cw, rw, offs, out):
             square_late(c)
         root(root2[:], u_late[2][:])
         root(root3[:], u_late[3][:])
-        square(inv_late[0][:, HIGH, :], root2[:, HIGH, :])
+        square(inv_late[0][:, :, HIGH], root2[:, :, HIGH])
         square(inv_late[1][:], root3[:])
 
-        gradient(nc.gpsimd, g_early[:, part(0), :], num[0], inv_early[:, part(0), :])
-        gradient(nc.vector, g_early[:, part(1), :], num[1], inv_early[:, part(1), :])
+        nc.gpsimd.tensor_tensor(g_early[:, part(0), :], num[0], inv_early[0][:], ALU.mult)
+        gradient(g_early[:, part(1), :], num[1], inv_early[1][:])
         quantize_wv(0, wv_bf0, reuse.tile([P, P], U32, name="wv_codes0", align_bytes=64, offset=2048))
         quantize_g(g_early[:], 0)
-        once = tagged("once", "inv_early", [P, CHUNK // 2, PACK], F32)
-        gradient(nc.vector, once[:], num[2][:, LOW, :], root2[:, LOW, :])
-        quantize_wv(1, wv_bf1, tagged("wv_codes1", "num_early", [P, P], U32))
+        once = tagged("once", "inv1", [P, PACK, CHUNK // 2], F32)
+        nc.vector.tensor_tensor(once[:], num[2][:, :, LOW], root2[:, :, LOW], ALU.mult)
+        quantize_wv(1, wv_bf1, tagged("wv_codes1", "num1", [P, P], U32))
         g_late = tiles("g_late", 2, [P, CHUNK, PACK], BF16)
-        gradient(nc.vector, g_late[0][:, LOW, :], once[:], root2[:, LOW, :])
+        gradient(g_late[0][:, LOW, :], once[:], root2[:, :, LOW])
         early = second_product(0, slice(0, HALF), "bank3", nc.vector.tensor_copy, "dx_early")
         scatter_on_scalar(0, 0, early[:])
-        gradient(nc.vector, g_late[0][:, HIGH, :], num[2][:, HIGH, :], inv_late[0][:, HIGH, :])
-        gradient(nc.vector, g_late[1][:], num[3], inv_late[1][:])
+        gradient(g_late[0][:, HIGH, :], num[2][:, :, HIGH], inv_late[0][:, :, HIGH])
+        gradient(g_late[1][:], num[3], inv_late[1][:])
         for c in (2, 3):
             quantize_g(g_late[c - 2][:], c * CHUNK)
         first_half = second_product(1, slice(0, HALF), "bank5", nc.vector.tensor_copy, "inv3")

@@ -332,24 +332,29 @@ def tile_attend_gml_cau_kernel(tc, xT, wd, wv, y, cw, rw, offs, out):
         first_half = second_product(1, slice(0, HALF), "bank5", nc.vector.tensor_copy, "inv3")
         scatter_on_scalar(1, 0, first_half[:])
         quantize_wv(2, wv_bf2, tagged("wv_codes2", "num3", [P, P], U32))
+        wv_bf3 = tagged("wv_bf3", "wv_bf2", [P, P, PACK], BF16)
+        round_wv_on_gpsimd(wv_bf3, wv_last[:])
         late = sb.tile([P, HALF], F32, name="dx_late", align_bytes=64)
         for c in (2, 3):
             bank = second_pass(0, slice(c * CHUNK, (c + 1) * CHUNK), "bank%d" % (3 - c))
             nc.vector.tensor_copy(late[:, part(c)], bank[:])
+        dx2 = sb.tile([P, N], F32, name="dx2", align_bytes=64)
+        bank = second_pass(2, slice(0, HALF), "bank1")
+        nc.vector.tensor_copy(dx2[:, :HALF], bank[:])
         scatter_on_vector(0, HALF, late[:])
         store(0)
         second_half = second_product(1, slice(HALF, N), "bank5", nc.scalar.copy, "root3")
-        wv_bf3 = tagged("wv_bf3", "inv3", [P, P, PACK], BF16)
-        nc.scalar.copy(
-            wv_bf3[:].rearrange("p (n e) j -> p n j e", e=4), wv_last[:].rearrange("p j (n e) -> p n j e", e=4)
-        )
         scatter_on_scalar(1, HALF, second_half[:])
         store(1)
-        dx2 = second_product(2, slice(0, N), "bank0", nc.vector.tensor_copy, "dx_w2")
+        bank = second_pass(2, slice(HALF, N), "bank0")
+        nc.vector.tensor_copy(dx2[:, HALF:], bank[:])
         quantize_wv(3, wv_bf3, tagged("wv_codes3", "wv_codes3", [P, P], U32))
         scatter_on_vector(2, 0, dx2[:])
         store(2)
-        dx3 = second_product(3, slice(0, N), "bank0", nc.scalar.copy, "u2")
-        for first in (0, HALF):
-            scatter_on_scalar(3, first, dx3[:, first : first + HALF])
+        halves = [
+            second_product(3, slice(h * HALF, (h + 1) * HALF), "bank%d" % (6 + h), nc.scalar.copy, "u%d" % (2 + h))
+            for h in range(2)
+        ]
+        for h in range(2):
+            scatter_on_scalar(3, h * HALF, halves[h][:])
         store(3)

@@ -55,13 +55,16 @@ def tile_attend_gml_cau_kernel(tc, xT, wd, wv, y, cw, rw, offs, out):
         early_shapes = ([P, CHUNK, PACK], [P, PACK, CHUNK])
         root_early = [tagged("root%d" % c, "root%d" % c, early_shapes[c], F32) for c in range(2)]
         inv_early = [tagged("inv%d" % c, "inv%d" % c, early_shapes[c], F32) for c in range(2)]
-        wd_raw = tiles("wd_raw", 2, [P, PACK, V // 2], F32, DMA_ALIGN)
+        reuse = ctx.enter_context(tc.tile_pool(name="reuse", bufs=1))
+        wd_raw = [
+            sb.tile([P, PACK, V // 2], F32, name="wd_raw0", align_bytes=DMA_ALIGN),
+            reuse.tile([P, PACK, V // 2], F32, name="wd_raw1", align_bytes=DMA_ALIGN, offset=4096),
+        ]
         wv_first = sb.tile([P, PACK, P], F32, name="wv_first", align_bytes=DMA_ALIGN)
         wv_middle = sb.tile([P, PACK, 2 * P], F32, name="wv_middle", align_bytes=DMA_ALIGN)
         wv_last = sb.tile([P, PACK, P], F32, name="wv_last", align_bytes=DMA_ALIGN)
         x_plane = tiles("x_plane", PACK, [P, T], F32, DMA_ALIGN)
         y_pair = tiles("y_pair", 2, [P, 2, HALF], F32, DMA_ALIGN)
-        reuse = ctx.enter_context(tc.tile_pool(name="reuse", bufs=1))
         y_late = reuse.tile([P, PACK, HALF], F32, name="y_late", align_bytes=DMA_ALIGN, offset=0)
 
         x_rows = xT.rearrange("(p j) c -> p j c", j=PACK)
@@ -119,7 +122,7 @@ def tile_attend_gml_cau_kernel(tc, xT, wd, wv, y, cw, rw, offs, out):
                 nc.tensor.transpose(table[c][:, t, :], table_turned[c][:, t, :], identity[:])
 
         x_bf = [tagged("x_bf%d" % h, "x_bf%d" % h, [P, HALF, PACK], BF16) for h in range(2)]
-        x_codes = tiles("x_codes", 2, [P, HALF], U32)
+        x_codes = [sb.tile([P, HALF], U32, name="x_codes0", align_bytes=64)]
         x_scales = tiles("x_scales", 2, [P, HALF], U8)
         for j in range(PACK):
             for h in range(2):
@@ -129,8 +132,7 @@ def tile_attend_gml_cau_kernel(tc, xT, wd, wv, y, cw, rw, offs, out):
         def quantize(codes, scales, values, fmt):
             nc.vector.quantize_mx(out=codes.bitcast(fmt), scales=scales, in_=values.rearrange("p i j -> p (i j)"))
 
-        for h in range(2):
-            quantize(x_codes[h][:], x_scales[h][:], x_bf[h][:], E4M3)
+        quantize(x_codes[0][:], x_scales[0][:], x_bf[0][:], E4M3)
 
         wd_bf = [tagged("wd_bf%d" % k, "wd_bf%d" % k, [P, 2, P, PACK], BF16) for k in range(2)]
         wd_codes = tiles("wd_codes", 2, [P, 2 * P], U32)
@@ -153,14 +155,16 @@ def tile_attend_gml_cau_kernel(tc, xT, wd, wv, y, cw, rw, offs, out):
         interleave_wd(nc.scalar.copy, 0, slice(2, 4))
         quantize_wd(0, 0)
         quantize_wd(0, 1)
-        interleave_wd(nc.vector.tensor_copy, 1, slice(0, 1))
-        interleave_wd(nc.vector.tensor_copy, 1, slice(1, 2))
+        interleave_wd(nc.vector.tensor_copy, 1, slice(0, 2))
         interleave_wd(nc.scalar.copy, 1, slice(2, 4))
         quantize_wd(1, 0)
         quantize_wd(1, 1)
-        for t in (2, 3):
-            quantize_wd(0, t)
-            quantize_wd(1, t)
+        for t in range(2):
+            cols = slice(t * P, (t + 1) * P)
+            quantize(wd_codes[1][:, cols], wd_scales[1][:, cols], wd_bf[1][:, t, :, :], E4M3)
+
+        x_codes.append(reuse.tile([P, HALF], U32, name="x_codes1", align_bytes=64, offset=4096))
+        quantize(x_codes[1][:], x_scales[1][:], x_bf[1][:], E4M3)
 
         def scores(bank, t, h, cols):
             m = slice((t % 2) * P, (t % 2 + 1) * P)
@@ -286,7 +290,7 @@ def tile_attend_gml_cau_kernel(tc, xT, wd, wv, y, cw, rw, offs, out):
         def round_wv_on_gpsimd(target, source):
             nc.gpsimd.tensor_scalar(target[:], source.rearrange("p j d -> p d j"), 1.0, 0.0, ALU.mult, ALU.add)
 
-        wv_bf0 = tagged("wv_bf0", "wd_bf1", [P, P, PACK], BF16)
+        wv_bf0 = tagged("wv_bf0", "x_bf1", [P, P, PACK], BF16)
         round_wv_on_gpsimd(wv_bf0, wv_first[:])
         wv_bf1 = tagged("wv_bf1", "wv_bf1", [P, P, PACK], BF16)
         wv_bf2 = tagged("wv_bf2", "wv_bf2", [P, P, PACK], BF16)
@@ -324,13 +328,13 @@ def tile_attend_gml_cau_kernel(tc, xT, wd, wv, y, cw, rw, offs, out):
         g_late = tiles("g_late", 2, [P, CHUNK, PACK], BF16)
         gradient(g_late[0][:, LOW, :], once[:], root2[:, :, LOW])
         early = second_product(0, slice(0, HALF), "bank3", nc.vector.tensor_copy, "dx_early")
+        first_half = second_product(1, slice(0, HALF), "bank5", nc.scalar.copy, "u3")
         scatter_on_scalar(0, 0, early[:])
+        scatter_on_scalar(1, 0, first_half[:])
         gradient(g_late[0][:, HIGH, :], num[2][:, :, HIGH], inv_late[0][:, :, HIGH])
         gradient(g_late[1][:], num[3], inv_late[1][:])
         for c in (2, 3):
             quantize_g(g_late[c - 2][:], c * CHUNK)
-        first_half = second_product(1, slice(0, HALF), "bank5", nc.vector.tensor_copy, "inv3")
-        scatter_on_scalar(1, 0, first_half[:])
         quantize_wv(2, wv_bf2, tagged("wv_codes2", "num3", [P, P], U32))
         wv_bf3 = tagged("wv_bf3", "wv_bf2", [P, P, PACK], BF16)
         round_wv_on_gpsimd(wv_bf3, wv_last[:])
@@ -352,7 +356,7 @@ def tile_attend_gml_cau_kernel(tc, xT, wd, wv, y, cw, rw, offs, out):
         scatter_on_vector(2, 0, dx2[:])
         store(2)
         halves = [
-            second_product(3, slice(h * HALF, (h + 1) * HALF), "bank%d" % (6 + h), nc.scalar.copy, "u%d" % (2 + h))
+            second_product(3, slice(h * HALF, (h + 1) * HALF), "bank%d" % (6 + h), nc.scalar.copy, "inv%d" % (2 + h))
             for h in range(2)
         ]
         for h in range(2):

@@ -316,7 +316,8 @@ def tile_attend_gml_cau_kernel(tc, xT, wd, wv, y, cw, rw, offs, out):
         root(root2[:], u_late[2][:])
         root(root3[:], u_late[3][:])
         square(inv_late[0][:, :, HIGH], root2[:, :, HIGH])
-        square(inv_late[1][:], root3[:])
+        for piece in (LOW, HIGH):
+            square(inv_late[1][:, :, piece], root3[:, :, piece])
 
         nc.gpsimd.tensor_tensor(g_early[:, part(0), :], num[0], inv_early[0][:], ALU.mult)
         gradient(g_early[:, part(1), :], num[1], inv_early[1][:])
@@ -332,13 +333,14 @@ def tile_attend_gml_cau_kernel(tc, xT, wd, wv, y, cw, rw, offs, out):
         scatter_on_scalar(0, 0, early[:])
         scatter_on_scalar(1, 0, first_half[:])
         gradient(g_late[0][:, HIGH, :], num[2][:, :, HIGH], inv_late[0][:, :, HIGH])
-        gradient(g_late[1][:], num[3], inv_late[1][:])
-        for c in (2, 3):
-            quantize_g(g_late[c - 2][:], c * CHUNK)
-        quantize_wv(2, wv_bf2, tagged("wv_codes2", "num3", [P, P], U32))
+        gradient(g_late[1][:, LOW, :], num[3][:, :, LOW], inv_late[1][:, :, LOW])
+        gradient(g_late[1][:, HIGH, :], num[3][:, :, HIGH], inv_late[1][:, :, HIGH])
+        quantize_g(g_late[0][:], 2 * CHUNK)
+        quantize_g(g_late[1][:], 3 * CHUNK)
+        quantize_wv(2, wv_bf2, tagged("wv_codes2", "inv3", [P, P], U32))
         wv_bf3 = tagged("wv_bf3", "wv_bf2", [P, P, PACK], BF16)
         round_wv_on_gpsimd(wv_bf3, wv_last[:])
-        late = sb.tile([P, HALF], F32, name="dx_late", align_bytes=64)
+        late = tagged("dx_late", "num3", [P, HALF], F32)
         for c in (2, 3):
             bank = second_pass(0, slice(c * CHUNK, (c + 1) * CHUNK), "bank%d" % (3 - c))
             nc.vector.tensor_copy(late[:, part(c)], bank[:])
@@ -356,7 +358,7 @@ def tile_attend_gml_cau_kernel(tc, xT, wd, wv, y, cw, rw, offs, out):
         scatter_on_vector(2, 0, dx2[:])
         store(2)
         halves = [
-            second_product(3, slice(h * HALF, (h + 1) * HALF), "bank%d" % (6 + h), nc.scalar.copy, "inv%d" % (2 + h))
+            second_product(3, slice(h * HALF, (h + 1) * HALF), "bank%d" % (6 + h), nc.scalar.copy, ("inv2", "num2")[h])
             for h in range(2)
         ]
         for h in range(2):

@@ -60,9 +60,7 @@ def tile_attend_gml_cau_kernel(tc, xT, wd, wv, y, cw, rw, offs, out):
             sb.tile([P, PACK, V // 2], F32, name="wd_raw0", align_bytes=DMA_ALIGN),
             reuse.tile([P, PACK, V // 2], F32, name="wd_raw1", align_bytes=DMA_ALIGN, offset=4096),
         ]
-        wv_first = sb.tile([P, PACK, P], F32, name="wv_first", align_bytes=DMA_ALIGN)
-        wv_middle = sb.tile([P, PACK, 2 * P], F32, name="wv_middle", align_bytes=DMA_ALIGN)
-        wv_last = sb.tile([P, PACK, P], F32, name="wv_last", align_bytes=DMA_ALIGN)
+        wv_raw = tiles("wv_raw", 2, [P, PACK, 2 * P], F32, DMA_ALIGN)
         x_plane = tiles("x_plane", PACK, [P, T], F32, DMA_ALIGN)
         y_pair = tiles("y_pair", 2, [P, 2, HALF], F32, DMA_ALIGN)
         y_late = reuse.tile([P, PACK, HALF], F32, name="y_late", align_bytes=DMA_ALIGN, offset=0)
@@ -81,10 +79,9 @@ def tile_attend_gml_cau_kernel(tc, xT, wd, wv, y, cw, rw, offs, out):
             nc.sync.dma_start(wd_raw[h][:], wd_rows[:, :, h * (V // 2) : (h + 1) * (V // 2)])
         nc.sync.dma_start(y_pair[0][:], y_rows[:, :2, :HALF])
         nc.sync.dma_start(y_pair[1][:], y_rows[:, 2:, :HALF])
-        nc.sync.dma_start(wv_first[:], wv_rows[:, :, :P])
-        nc.sync.dma_start(wv_middle[:], wv_rows[:, :, P : 3 * P])
+        nc.sync.dma_start(wv_raw[0][:], wv_rows[:, :, : 2 * P])
         nc.sync.dma_start(y_late[:], y_rows[:, :, HALF:])
-        nc.sync.dma_start(wv_last[:], wv_rows[:, :, 3 * P :])
+        nc.sync.dma_start(wv_raw[1][:], wv_rows[:, :, 2 * P :])
 
         warm = sb.tile([P, 1], F32, name="warm")
         warm_out = sb.tile([P, 1], F32, name="warm_out")
@@ -110,7 +107,7 @@ def tile_attend_gml_cau_kernel(tc, xT, wd, wv, y, cw, rw, offs, out):
         cw_col = sb.tile([P, PACK, 1], F32, name="cw_col")
         rw_col = sb.tile([P, CHUNKS, 1], F32, name="rw_col")
         nc.scalar.copy(cw_col[:], cw_turned[:, :, 0:1])
-        nc.scalar.activation(rw_col[:], rw_turned[:, :, 1:2], ACT.Copy, scale=-1.0)
+        nc.scalar.copy(rw_col[:], rw_turned[:, :, 1:2])
         cw_spread = ps.tile([P, PACK, P], F32, name="cw_spread", tag="bank2")
         for t in range(PACK):
             nc.tensor.transpose(cw_spread[:, t, :], cw_col[:, t, :].to_broadcast([P, P]), identity[:])
@@ -198,17 +195,17 @@ def tile_attend_gml_cau_kernel(tc, xT, wd, wv, y, cw, rw, offs, out):
         wv_codes, wv_scales = {}, {}
 
         def residual_slot(t):
-            nc.vector.tensor_tensor(q_early[:, t, :], y_pair[0][:, t, :], a_slot[t][:], ALU.subtract)
+            nc.vector.tensor_tensor(q_early[:, t, :], a_slot[t][:], y_pair[0][:, t, :], ALU.subtract)
             nc.scalar.activation(u_early[:, t, :], q_early[:, t, :], ACT.Square)
 
         def residual_pair(c):
-            nc.vector.tensor_tensor(q[c][:, 2:, :], y_pair[1][:, :, part(c)], a_pair[c][:], ALU.subtract)
+            nc.vector.tensor_tensor(q[c][:, 2:, :], a_pair[c][:], y_pair[1][:, :, part(c)], ALU.subtract)
             nc.scalar.activation(u_early[:, 2:, part(c)], q[c][:, 2:, :], ACT.Square)
 
         def residual_late(c):
             for t in range(PACK):
                 scores(a_late[c][:, t, :], t, 1, part(c))
-            nc.vector.tensor_tensor(q[c], y_late[:, :, part(c)], a_late[c][:], ALU.subtract)
+            nc.vector.tensor_tensor(q[c], a_late[c][:], y_late[:, :, part(c)], ALU.subtract)
 
         def numerator(c):
             if c == 0:
@@ -291,11 +288,9 @@ def tile_attend_gml_cau_kernel(tc, xT, wd, wv, y, cw, rw, offs, out):
             nc.gpsimd.tensor_scalar(target[:], source.rearrange("p j d -> p d j"), 1.0, 0.0, ALU.mult, ALU.add)
 
         wv_bf0 = tagged("wv_bf0", "x_bf1", [P, P, PACK], BF16)
-        round_wv_on_gpsimd(wv_bf0, wv_first[:])
+        round_wv_on_gpsimd(wv_bf0, wv_raw[0][:, :, :P])
         wv_bf1 = tagged("wv_bf1", "wv_bf1", [P, P, PACK], BF16)
-        wv_bf2 = tagged("wv_bf2", "wv_bf2", [P, P, PACK], BF16)
-        round_wv_on_gpsimd(wv_bf1, wv_middle[:, :, :P])
-        round_wv_on_gpsimd(wv_bf2, wv_middle[:, :, P:])
+        round_wv_on_gpsimd(wv_bf1, wv_raw[0][:, :, P:])
 
         for t in range(2):
             residual_slot(t)
@@ -326,7 +321,7 @@ def tile_attend_gml_cau_kernel(tc, xT, wd, wv, y, cw, rw, offs, out):
         once = tagged("once", "inv1", [P, PACK, CHUNK // 2], F32)
         nc.vector.tensor_tensor(once[:], num[2][:, :, LOW], root2[:, :, LOW], ALU.mult)
         quantize_wv(1, wv_bf1, tagged("wv_codes1", "num1", [P, P], U32))
-        g_late = tiles("g_late", 2, [P, CHUNK, PACK], BF16)
+        g_late = [tagged("g_late%d" % i, "g_late%d" % i, [P, CHUNK, PACK], BF16) for i in range(2)]
         gradient(g_late[0][:, LOW, :], once[:], root2[:, :, LOW])
         early = second_product(0, slice(0, HALF), "bank3", nc.vector.tensor_copy, "dx_early")
         first_half = second_product(1, slice(0, HALF), "bank5", nc.scalar.copy, "u3")
@@ -337,23 +332,21 @@ def tile_attend_gml_cau_kernel(tc, xT, wd, wv, y, cw, rw, offs, out):
         gradient(g_late[1][:, HIGH, :], num[3][:, :, HIGH], inv_late[1][:, :, HIGH])
         quantize_g(g_late[0][:], 2 * CHUNK)
         quantize_g(g_late[1][:], 3 * CHUNK)
-        quantize_wv(2, wv_bf2, tagged("wv_codes2", "inv3", [P, P], U32))
-        wv_bf3 = tagged("wv_bf3", "wv_bf2", [P, P, PACK], BF16)
-        round_wv_on_gpsimd(wv_bf3, wv_last[:])
+        wv_bf2 = tagged("wv_bf2", "g_late0", [P, P, PACK], BF16)
+        round_wv_on_gpsimd(wv_bf2, wv_raw[1][:, :, :P])
         late = tagged("dx_late", "num3", [P, HALF], F32)
         for c in (2, 3):
             bank = second_pass(0, slice(c * CHUNK, (c + 1) * CHUNK), "bank%d" % (3 - c))
             nc.vector.tensor_copy(late[:, part(c)], bank[:])
-        dx2 = sb.tile([P, N], F32, name="dx2", align_bytes=64)
-        bank = second_pass(2, slice(0, HALF), "bank1")
-        nc.vector.tensor_copy(dx2[:, :HALF], bank[:])
+        quantize_wv(2, wv_bf2, tagged("wv_codes2", "wv_codes2", [P, P], U32))
+        wv_bf3 = tagged("wv_bf3", "g_late0", [P, P, PACK], BF16)
+        round_wv_on_gpsimd(wv_bf3, wv_raw[1][:, :, P:])
         scatter_on_vector(0, HALF, late[:])
         store(0)
         second_half = second_product(1, slice(HALF, N), "bank5", nc.scalar.copy, "root3")
         scatter_on_scalar(1, HALF, second_half[:])
         store(1)
-        bank = second_pass(2, slice(HALF, N), "bank0")
-        nc.vector.tensor_copy(dx2[:, HALF:], bank[:])
+        dx2 = second_product(2, slice(0, N), "bank0", nc.vector.tensor_copy, "dx2")
         quantize_wv(3, wv_bf3, tagged("wv_codes3", "wv_codes3", [P, P], U32))
         scatter_on_vector(2, 0, dx2[:])
         store(2)

@@ -23,6 +23,7 @@ CHUNK = 128
 CHUNKS = N // CHUNK
 BLOCKS = D // P
 DMA_ALIGN = 256
+TWICE = 32
 WHOLE, LOW, HIGH = slice(0, CHUNK), slice(0, CHUNK // 2), slice(CHUNK // 2, CHUNK)
 
 
@@ -310,7 +311,7 @@ def tile_attend_gml_cau_kernel(tc, xT, wd, wv, y, cw, rw, offs, out):
             square_late(c)
         root(root2[:], u_late[2][:])
         root(root3[:], u_late[3][:])
-        square(inv_late[0][:, :, HIGH], root2[:, :, HIGH])
+        square(inv_late[0][:, :, TWICE:], root2[:, :, TWICE:])
         for piece in (LOW, HIGH):
             square(inv_late[1][:, :, piece], root3[:, :, piece])
 
@@ -318,20 +319,20 @@ def tile_attend_gml_cau_kernel(tc, xT, wd, wv, y, cw, rw, offs, out):
         gradient(g_early[:, part(1), :], num[1], inv_early[1][:])
         quantize_wv(0, wv_bf0, reuse.tile([P, P], U32, name="wv_codes0", align_bytes=64, offset=2048))
         quantize_g(g_early[:], 0)
-        once = tagged("once", "inv1", [P, PACK, CHUNK // 2], F32)
-        nc.vector.tensor_tensor(once[:], num[2][:, :, LOW], root2[:, :, LOW], ALU.mult)
+        once = tagged("once", "inv1", [P, PACK, TWICE], F32)
+        nc.vector.tensor_tensor(once[:], num[2][:, :, :TWICE], root2[:, :, :TWICE], ALU.mult)
         quantize_wv(1, wv_bf1, tagged("wv_codes1", "num1", [P, P], U32))
         g_late = [tagged("g_late%d" % i, "g_late%d" % i, [P, CHUNK, PACK], BF16) for i in range(2)]
-        gradient(g_late[0][:, LOW, :], once[:], root2[:, :, LOW])
+        gradient(g_late[0][:, :TWICE, :], once[:], root2[:, :, :TWICE])
         early = second_product(0, slice(0, HALF), "bank3", nc.vector.tensor_copy, "dx_early")
-        first_half = second_product(1, slice(0, HALF), "bank5", nc.scalar.copy, "u3")
         scatter_on_scalar(0, 0, early[:])
-        scatter_on_scalar(1, 0, first_half[:])
-        gradient(g_late[0][:, HIGH, :], num[2][:, :, HIGH], inv_late[0][:, :, HIGH])
+        gradient(g_late[0][:, TWICE:, :], num[2][:, :, TWICE:], inv_late[0][:, :, TWICE:])
         gradient(g_late[1][:, LOW, :], num[3][:, :, LOW], inv_late[1][:, :, LOW])
         gradient(g_late[1][:, HIGH, :], num[3][:, :, HIGH], inv_late[1][:, :, HIGH])
         quantize_g(g_late[0][:], 2 * CHUNK)
         quantize_g(g_late[1][:], 3 * CHUNK)
+        first_half = second_product(1, slice(0, HALF), "bank5", nc.vector.tensor_copy, "inv3")
+        scatter_on_scalar(1, 0, first_half[:])
         wv_bf2 = tagged("wv_bf2", "g_late0", [P, P, PACK], BF16)
         round_wv_on_gpsimd(wv_bf2, wv_raw[1][:, :, :P])
         late = tagged("dx_late", "num3", [P, HALF], F32)

from contextlib import ExitStack

import concourse.mybir as mybir
from concourse.masks import make_identity

N, T, D, V = 512, 2048, 512, 512
FLOPS = 2 * 2 * N * D * V

F32 = mybir.dt.float32
BF16 = mybir.dt.bfloat16
U32 = mybir.dt.uint32
U16 = mybir.dt.uint16
U8 = mybir.dt.uint8
E4M3 = mybir.dt.float8_e4m3fn_x4
E5M2 = mybir.dt.float8_e5m2_x4
ALU = mybir.AluOpType
ACT = mybir.ActivationFunctionType

P = 128
PACK = 4
HALF = N // 2
CHUNK = 128
CHUNKS = N // CHUNK
BLOCKS = D // P
DMA_ALIGN = 256
TWICE = 32
WHOLE, LOW, HIGH = slice(0, CHUNK), slice(0, CHUNK // 2), slice(CHUNK // 2, CHUNK)


def tile_attend_gml_cau_kernel(tc, xT, wd, wv, y, cw, rw, offs, out):
    nc = tc.nc
    with ExitStack() as ctx:
        sb = ctx.enter_context(tc.tile_pool(name="sb", bufs=1))
        ps = ctx.enter_context(tc.psum_pool(name="ps", bufs=1))

        def tiles(name, count, shape, dtype, align=64):
            return [sb.tile(shape, dtype, name="%s%d" % (name, i), align_bytes=align) for i in range(count)]

        def tagged(name, tag, shape, dtype):
            return sb.tile(shape, dtype, name=name, tag=tag, align_bytes=64)

        def pairs_of_slot_major(ap):
            return ap.rearrange("p t (n e) -> p n t e", e=2)

        def pairs_of_position_major(ap):
            return ap.rearrange("p (n e) t -> p n t e", e=2)

        vector_windows = tiles("vector_window", 2, [P, T], F32, DMA_ALIGN)
        offsets = sb.tile([P, N // 16], U16, name="offsets")
        weights_row = sb.tile([P, N], F32, name="weights_row", align_bytes=DMA_ALIGN)
        nc.gpsimd.memset(weights_row[:], 0.0)
        u_late = {c: tagged("u%d" % c, "u%d" % c, [P, PACK, CHUNK], F32) for c in (2, 3)}
        root2 = tagged("root2", "root2", [P, PACK, CHUNK], F32)
        root3 = tagged("root3", "root3", [P, PACK, CHUNK], F32)
        inv_late = [tagged("inv%d" % c, "inv%d" % c, [P, PACK, CHUNK], F32) for c in (2, 3)]
        early_shapes = ([P, CHUNK, PACK], [P, PACK, CHUNK])
        root_early = [tagged("root%d" % c, "root%d" % c, early_shapes[c], F32) for c in range(2)]
        inv_early = [tagged("inv%d" % c, "inv%d" % c, early_shapes[c], F32) for c in range(2)]
        reuse = ctx.enter_context(tc.tile_pool(name="reuse", bufs=1))
        wd_raw = [
            sb.tile([P, PACK, V // 2], F32, name="wd_raw0", align_bytes=DMA_ALIGN),
            reuse.tile([P, PACK, V // 2], F32, name="wd_raw1", align_bytes=DMA_ALIGN, offset=4096),
        ]
        wv_raw = tiles("wv_raw", 2, [P, PACK, 2 * P], F32, DMA_ALIGN)
        x_plane = tiles("x_plane", PACK, [P, T], F32, DMA_ALIGN)
        y_pair = tiles("y_pair", 2, [P, 2, HALF], F32, DMA_ALIGN)
        y_late = reuse.tile([P, PACK, HALF], F32, name="y_late", align_bytes=DMA_ALIGN, offset=0)

        x_rows = xT.rearrange("(p j) c -> p j c", j=PACK)
        wd_rows = wd.rearrange("(p j) v -> p j v", j=PACK)
        wv_rows = wv.rearrange("(p j) d -> p j d", j=PACK)
        y_rows = y.rearrange("(p t) i -> p t i", t=PACK)
        nc.sync.dma_start(x_plane[0][:], x_rows[:, 0, :])
        nc.sync.dma_start(offsets[:], offs)
        nc.sync.dma_start(weights_row[0:1, :], cw.rearrange("v o -> o v"))
        nc.sync.dma_start(weights_row[1:2, :], rw[0:1, :])
        for j in range(1, PACK):
            nc.sync.dma_start(x_plane[j][:], x_rows[:, j, :])
        for h in range(2):
            nc.sync.dma_start(wd_raw[h][:], wd_rows[:, :, h * (V // 2) : (h + 1) * (V // 2)])
        nc.sync.dma_start(y_pair[0][:], y_rows[:, :2, :HALF])
        nc.sync.dma_start(y_pair[1][:], y_rows[:, 2:, :HALF])
        nc.sync.dma_start(wv_raw[0][:], wv_rows[:, :, : 2 * P])
        nc.sync.dma_start(y_late[:], y_rows[:, :, HALF:])
        nc.sync.dma_start(wv_raw[1][:], wv_rows[:, :, 2 * P :])

        warm = sb.tile([P, 1], F32, name="warm")
        warm_out = sb.tile([P, 1], F32, name="warm_out")
        nc.vector.memset(warm[:], 0.0)
        nc.scalar.activation(warm_out[:], warm[:], ACT.Abs_reciprocal_sqrt, bias=1.0)

        far = ctx.enter_context(tc.tile_pool(name="far", bufs=1))
        scalar_windows = [far.tile([P, T], F32, name="scalar_window%d" % i, align_bytes=DMA_ALIGN) for i in range(2)]
        window = [vector_windows[0], scalar_windows[0], vector_windows[1], scalar_windows[1]]
        identity = sb.tile([P, P], F32, name="identity")
        make_identity(nc, identity[:])
        for b in range(BLOCKS):
            (nc.vector if b < 2 else nc.gpsimd).memset(window[b][:], 0.0)
        g_codes = sb.tile([P, N], U32, name="g_codes", align_bytes=64)
        g_scales = sb.tile([P, N], U8, name="g_scales", align_bytes=64)

        cw_turned = ps.tile([P, PACK, P], F32, name="cw_turned", tag="bank0")
        rw_turned = ps.tile([P, CHUNKS, P], F32, name="rw_turned", tag="bank1")
        for t in range(PACK):
            nc.tensor.transpose(cw_turned[:, t, :], weights_row[:, t::PACK], identity[:])
        for c in range(CHUNKS):
            nc.tensor.transpose(rw_turned[:, c, :], weights_row[:, c * CHUNK : (c + 1) * CHUNK], identity[:])
        cw_col = sb.tile([P, PACK, 1], F32, name="cw_col")
        rw_col = sb.tile([P, CHUNKS, 1], F32, name="rw_col")
        nc.scalar.copy(cw_col[:], cw_turned[:, :, 0:1])
        nc.scalar.copy(rw_col[:], rw_turned[:, :, 1:2])
        cw_spread = ps.tile([P, PACK, P], F32, name="cw_spread", tag="bank2")
        for t in range(PACK):
            nc.tensor.transpose(cw_spread[:, t, :], cw_col[:, t, :].to_broadcast([P, P]), identity[:])
        table_turned = tiles("table_turned", CHUNKS, [P, PACK, P], F32)
        table = [ps.tile([P, PACK, CHUNK], F32, name="table%d" % c, tag="bank%d" % (4 + c)) for c in range(CHUNKS)]
        for c in range(CHUNKS):
            nc.scalar.activation(table_turned[c][:], cw_spread[:], ACT.Copy, scale=rw_col[:, c, :])
            for t in range(PACK):
                nc.tensor.transpose(table[c][:, t, :], table_turned[c][:, t, :], identity[:])

        x_bf = [tagged("x_bf%d" % h, "x_bf%d" % h, [P, HALF, PACK], BF16) for h in range(2)]
        x_codes = [sb.tile([P, HALF], U32, name="x_codes0", align_bytes=64)]
        x_scales = tiles("x_scales", 2, [P, HALF], U8)
        for j in range(PACK):
            for h in range(2):
                cols = HALF // 16
                nc.vector.tensor_copy(x_bf[h][:, :, j], x_plane[j][:].indirect(offsets[:, h * cols : (h + 1) * cols]))

        def quantize(codes, scales, values, fmt):
            nc.vector.quantize_mx(out=codes.bitcast(fmt), scales=scales, in_=values.rearrange("p i j -> p (i j)"))

        quantize(x_codes[0][:], x_scales[0][:], x_bf[0][:], E4M3)

        wd_bf = [tagged("wd_bf%d" % k, "wd_bf%d" % k, [P, 2, P, PACK], BF16) for k in range(2)]
        wd_codes = tiles("wd_codes", 2, [P, 2 * P], U32)
        wd_scales = tiles("wd_scales", 2, [P, 2 * P], U8)

        def interleave_wd(copy, h, slots):
            k = slots.start // 2
            own = slice(slots.start - 2 * k, slots.stop - 2 * k)
            copy(
                wd_bf[k][:, own, h * (P // 2) : (h + 1) * (P // 2), :].rearrange("p t m j -> p m j t"),
                wd_raw[h][:].rearrange("p j (m t) -> p m j t", t=PACK)[:, :, :, slots],
            )

        def quantize_wd(h, t):
            cols = slice((t % 2) * P + h * (P // 2), (t % 2) * P + (h + 1) * (P // 2))
            values = wd_bf[t // 2][:, t % 2, h * (P // 2) : (h + 1) * (P // 2), :]
            quantize(wd_codes[t // 2][:, cols], wd_scales[t // 2][:, cols], values, E4M3)

        interleave_wd(nc.scalar.copy, 0, slice(0, 2))
        interleave_wd(nc.scalar.copy, 0, slice(2, 4))
        quantize_wd(0, 0)
        quantize_wd(0, 1)
        interleave_wd(nc.vector.tensor_copy, 1, slice(0, 2))
        interleave_wd(nc.scalar.copy, 1, slice(2, 4))
        quantize_wd(1, 0)
        quantize_wd(1, 1)
        for t in range(2):
            cols = slice(t * P, (t + 1) * P)
            quantize(wd_codes[1][:, cols], wd_scales[1][:, cols], wd_bf[1][:, t, :, :], E4M3)

        x_codes.append(reuse.tile([P, HALF], U32, name="x_codes1", align_bytes=64, offset=4096))
        quantize(x_codes[1][:], x_scales[1][:], x_bf[1][:], E4M3)

        def scores(bank, t, h, cols):
            m = slice((t % 2) * P, (t % 2 + 1) * P)
            nc.tensor.matmul_mx(
                out=bank,
                lhsT=wd_codes[t // 2][:, m].bitcast(E4M3),
                lhsT_scale=wd_scales[t // 2][:, m],
                rhs=x_codes[h][:, cols].bitcast(E4M3),
                rhs_scale=x_scales[h][:, cols],
                start=True,
                stop=True,
            )

        def part(c, piece=WHOLE):
            return slice((c % 2) * CHUNK + piece.start, (c % 2) * CHUNK + piece.stop)

        a_slot = [ps.tile([P, HALF], F32, name="a_slot%d" % t, tag="bank%d" % t) for t in range(2)]
        a_pair = [ps.tile([P, 2, CHUNK], F32, name="a_pair%d" % c, tag="bank%d" % (2 + c)) for c in range(2)]
        a_late = {c: ps.tile([P, PACK, CHUNK], F32, name="a_late%d" % c, tag="bank%d" % (c - 2)) for c in (2, 3)}
        for t in range(2):
            scores(a_slot[t][:], t, 0, slice(0, HALF))
        for c in range(2):
            for t in (2, 3):
                scores(a_pair[c][:, t - 2, :], t, 0, part(c))

        q_early = sb.tile([P, PACK, HALF], F32, name="q_early", align_bytes=64)
        u_early = sb.tile([P, PACK, HALF], F32, name="u_early", align_bytes=64)
        q = [q_early[:, :, part(0)], q_early[:, :, part(1)]] + [t[:] for t in tiles("q_late", 2, [P, PACK, CHUNK], F32)]
        num = [tagged("num%d" % c, "num%d" % c, early_shapes[min(c, 1)], F32)[:] for c in range(CHUNKS)]
        g_early = reuse.tile([P, HALF, PACK], BF16, name="g_early", align_bytes=64, offset=0)
        wv_codes, wv_scales = {}, {}

        def residual_slot(t):
            nc.vector.tensor_tensor(q_early[:, t, :], a_slot[t][:], y_pair[0][:, t, :], ALU.subtract)
            nc.scalar.activation(u_early[:, t, :], q_early[:, t, :], ACT.Square)

        def residual_pair(c):
            nc.vector.tensor_tensor(q[c][:, 2:, :], a_pair[c][:], y_pair[1][:, :, part(c)], ALU.subtract)
            nc.scalar.activation(u_early[:, 2:, part(c)], q[c][:, 2:, :], ACT.Square)

        def residual_late(c):
            for t in range(PACK):
                scores(a_late[c][:, t, :], t, 1, part(c))
            nc.vector.tensor_tensor(q[c], a_late[c][:], y_late[:, :, part(c)], ALU.subtract)

        def numerator(c):
            if c == 0:
                nc.vector.tensor_tensor(
                    pairs_of_position_major(num[c]),
                    pairs_of_slot_major(q[c]),
                    pairs_of_slot_major(table[c][:]),
                    ALU.mult,
                )
            else:
                nc.vector.tensor_tensor(num[c], q[c], table[c][:], ALU.mult)

        def root(target, source):
            nc.scalar.activation(target, source, ACT.Abs_reciprocal_sqrt, bias=1.0)

        def square(target, source):
            nc.scalar.activation(target, source, ACT.Square)

        def root_of_early(c):
            if c == 0:
                root(pairs_of_position_major(root_early[c][:]), pairs_of_slot_major(u_early[:, :, part(c)]))
            else:
                root(root_early[c][:], u_early[:, :, part(c)])

        def inverse_of_early(c):
            square(inv_early[c][:], root_early[c][:])

        def square_late(c):
            square(u_late[c][:], q[c])

        def gradient(target, first, second):
            nc.vector.tensor_tensor(
                pairs_of_position_major(target), pairs_of_slot_major(first), pairs_of_slot_major(second), ALU.mult
            )

        def quantize_g(source, first):
            place = slice(first, first + source.shape[1])
            quantize(g_codes[:, place], g_scales[:, place], source, E5M2)

        def quantize_wv(b, values, codes):
            wv_codes[b] = codes
            wv_scales[b] = sb.tile([P, P], U8, name="wv_scales%d" % b, align_bytes=64)
            quantize(wv_codes[b][:], wv_scales[b][:], values[:], E4M3)

        def second_pass(b, cols, bank_tag):
            count = cols.stop - cols.start
            name = "dx%d_%d" % (b, cols.start)
            bank = ps.tile([P, count], F32, name=name, tag=bank_tag)
            nc.tensor.matmul_mx(
                out=bank[:],
                lhsT=wv_codes[b][:].bitcast(E4M3),
                lhsT_scale=wv_scales[b][:],
                rhs=g_codes[:, cols].bitcast(E5M2),
                rhs_scale=g_scales[:, cols],
                start=True,
                stop=True,
            )
            return bank

        def second_product(b, cols, bank_tag, copy, buffer_tag):
            bank = second_pass(b, cols, bank_tag)
            dx = tagged("dx%d_%d_sb" % (b, cols.start), buffer_tag, [P, cols.stop - cols.start], F32)
            copy(dx[:], bank[:])
            return dx

        def listed(b, first, count):
            return window[b][:].indirect(offsets[:, first // 16 : (first + count) // 16])

        def scatter_on_vector(b, first, values):
            nc.vector.tensor_copy(listed(b, first, values.shape[1]), values)

        def scatter_on_scalar(b, first, values):
            nc.scalar.activation(listed(b, first, values.shape[1]), values, ACT.Copy)

        def store(b):
            for cols in (slice(0, T // 2), slice(T // 2, T)):
                nc.sync.dma_start(out[b * P : (b + 1) * P, cols], window[b][:, cols])

        def round_wv_on_gpsimd(target, source):
            nc.gpsimd.tensor_scalar(target[:], source.rearrange("p j d -> p d j"), 1.0, 0.0, ALU.mult, ALU.add)

        wv_bf0 = tagged("wv_bf0", "x_bf1", [P, P, PACK], BF16)
        round_wv_on_gpsimd(wv_bf0, wv_raw[0][:, :, :P])
        wv_bf1 = tagged("wv_bf1", "wv_bf1", [P, P, PACK], BF16)
        round_wv_on_gpsimd(wv_bf1, wv_raw[0][:, :, P:])

        for t in range(2):
            residual_slot(t)
        for c in range(2):
            residual_pair(c)
        numerator(0)
        numerator(1)
        residual_late(2)
        residual_late(3)
        numerator(2)
        numerator(3)
        for c in range(2):
            root_of_early(c)
        for c in range(2):
            inverse_of_early(c)
        for c in (2, 3):
            square_late(c)
        root(root2[:], u_late[2][:])
        root(root3[:], u_late[3][:])
        square(inv_late[0][:, :, TWICE:], root2[:, :, TWICE:])
        for piece in (LOW, HIGH):
            square(inv_late[1][:, :, piece], root3[:, :, piece])

        nc.gpsimd.tensor_tensor(g_early[:, part(0), :], num[0], inv_early[0][:], ALU.mult)
        gradient(g_early[:, part(1), :], num[1], inv_early[1][:])
        quantize_wv(0, wv_bf0, reuse.tile([P, P], U32, name="wv_codes0", align_bytes=64, offset=2048))
        quantize_g(g_early[:], 0)
        once = tagged("once", "inv1", [P, PACK, TWICE], F32)
        nc.vector.tensor_tensor(once[:], num[2][:, :, :TWICE], root2[:, :, :TWICE], ALU.mult)
        quantize_wv(1, wv_bf1, tagged("wv_codes1", "num1", [P, P], U32))
        g_late = [tagged("g_late%d" % i, "g_late%d" % i, [P, CHUNK, PACK], BF16) for i in range(2)]
        gradient(g_late[0][:, :TWICE, :], once[:], root2[:, :, :TWICE])
        early = second_product(0, slice(0, HALF), "bank3", nc.vector.tensor_copy, "dx_early")
        scatter_on_scalar(0, 0, early[:])
        gradient(g_late[0][:, TWICE:, :], num[2][:, :, TWICE:], inv_late[0][:, :, TWICE:])
        gradient(g_late[1][:, LOW, :], num[3][:, :, LOW], inv_late[1][:, :, LOW])
        gradient(g_late[1][:, HIGH, :], num[3][:, :, HIGH], inv_late[1][:, :, HIGH])
        quantize_g(g_late[0][:], 2 * CHUNK)
        quantize_g(g_late[1][:], 3 * CHUNK)
        first_half = second_product(1, slice(0, HALF), "bank5", nc.vector.tensor_copy, "inv3")
        scatter_on_scalar(1, 0, first_half[:])
        wv_bf2 = tagged("wv_bf2", "g_late0", [P, P, PACK], BF16)
        round_wv_on_gpsimd(wv_bf2, wv_raw[1][:, :, :P])
        late = tagged("dx_late", "num3", [P, HALF], F32)
        for c in (2, 3):
            bank = second_pass(0, slice(c * CHUNK, (c + 1) * CHUNK), "bank%d" % (3 - c))
            nc.vector.tensor_copy(late[:, part(c)], bank[:])
        quantize_wv(2, wv_bf2, tagged("wv_codes2", "wv_codes2", [P, P], U32))
        wv_bf3 = tagged("wv_bf3", "g_late0", [P, P, PACK], BF16)
        round_wv_on_gpsimd(wv_bf3, wv_raw[1][:, :, P:])
        scatter_on_vector(0, HALF, late[:])
        store(0)
        second_half = second_product(1, slice(HALF, N), "bank5", nc.scalar.copy, "root3")
        scatter_on_scalar(1, HALF, second_half[:])
        store(1)
        dx2 = second_product(2, slice(0, N), "bank0", nc.vector.tensor_copy, "dx2")
        quantize_wv(3, wv_bf3, tagged("wv_codes3", "wv_codes3", [P, P], U32))
        scatter_on_vector(2, 0, dx2[:])
        store(2)
        halves = [
            second_product(3, slice(h * HALF, (h + 1) * HALF), "bank%d" % (6 + h), nc.scalar.copy, ("inv2", "num2")[h])
            for h in range(2)
        ]
        for h in range(2):
            scatter_on_scalar(3, h * HALF, halves[h][:])
        store(3)
